import numpy as np
import ml_dtypes


def mxq(x, axis, fmt="e4m3"):
    dtype, down = {"e4m3": (ml_dtypes.float8_e4m3fn, 7), "e5m2": (ml_dtypes.float8_e5m2, 14)}[fmt]
    v = np.moveaxis(np.asarray(x, np.float32).astype(ml_dtypes.bfloat16).astype(np.float64), axis, -1)
    blocks = v.reshape(v.shape[:-1] + (-1, 32))
    amax = np.abs(blocks).max(-1, keepdims=True)
    byte = np.maximum(np.where(amax > 0, np.frexp(amax)[1] - 1 + 127, 0) - down, 1)
    scale = np.exp2(byte - 127.0)
    codes = (blocks / scale).astype(np.float32).astype(dtype).astype(np.float64)
    return np.moveaxis((codes * scale).reshape(v.shape), -1, axis)


WIDE = False


def mx_kscale(k):
    if not WIDE:
        return np.ones(k)
    levels = np.array([10, -10, 5, -5, 0])
    if k % 512:
        return np.exp2(np.random.permutation(np.resize(levels, k // 32))).repeat(32)
    a = np.empty((k // 512, 16))
    for p in range(k // 512):
        a[p, :8] = np.random.permutation(np.resize(levels, 8))
        for g in range(8):
            far = levels[np.abs(levels - a[p, g]) >= 10]
            a[p, g + 8] = far[np.random.randint(len(far))]
    return np.exp2(a.ravel()).repeat(32)


BF16 = ml_dtypes.bfloat16


def bf(x):
    return np.asarray(x, np.float32).astype(BF16)


def f64(x):
    return np.asarray(x).astype(np.float64)


E2M1 = np.array([0.0, 0.5, 1.0, 1.5, 2.0, 3.0, 4.0, 6.0, -0.0, -0.5, -1.0, -1.5, -2.0, -3.0, -4.0, -6.0])


def pack_weight(w, fmt):
    k, n = w.shape
    w = f64(bf(w)).reshape(k // 32, 32, n)
    amax = np.abs(w).max(1)
    if fmt == "e4m3":
        byte = np.frexp(amax)[1] - 1 + 127 - 7
    else:
        mant, ex = np.frexp(amax / 6.0)
        byte = np.where(mant > 0.5, ex, ex - 1) + 127
    byte = np.clip(np.where(amax > 0, byte, 1), 1, 254)
    scaled = (w * np.exp2(127.0 - byte)[:, None, :]).reshape(k, n).astype(np.float32)
    by_word = np.ascontiguousarray(scaled.reshape(k // 512, 128, 4, n).transpose(0, 1, 3, 2))
    if fmt == "e4m3":
        words = by_word.astype(ml_dtypes.float8_e4m3fn).view(np.uint8)
    else:
        c = by_word.astype(ml_dtypes.float4_e2m1fn).view(np.uint8) & 0xF
        words = c[..., 0::2] | (c[..., 1::2] << 4)
    return np.ascontiguousarray(words), np.ascontiguousarray(byte.astype(np.uint8).reshape(k // 512, 16, n))


def unpack_weight(words, scales, fmt):
    g, p, n, _ = words.shape
    if fmt == "e4m3":
        vals = np.ascontiguousarray(words).view(ml_dtypes.float8_e4m3fn).astype(np.float64)
    else:
        nib = np.empty((g, p, n, 4), np.uint8)
        nib[..., 0::2] = words & 0xF
        nib[..., 1::2] = words >> 4
        vals = E2M1[nib]
    vals = vals * np.repeat(np.exp2(scales.astype(np.float64) - 127.0), 8, axis=1)[..., None]
    return vals.transpose(0, 1, 3, 2).reshape(g * 512, n)
def pack4(w):
    words, scales = pack_weight(w, "e2m1")
    return words.reshape(words.shape[0], 128, -1), scales


def unpack4(words, scales):
    return unpack_weight(words.reshape(words.shape[0], 128, -1, 2), scales, "e2m1")


T, E, H, C, P = 512, 2048, 8, 128, 2048


def draw0():
    s, f = mx_kscale(E), mx_kscale(T)
    a = np.exp(2.0 * np.random.standard_normal((H, T, P)))
    a = a / a.sum(1, keepdims=True)
    r = np.exp(0.7 * np.random.standard_normal(T))
    z = 1.0 / (a * r[:, None]).sum(1)
    attn_words, attn_scales = pack4((a * f[:, None]).reshape(H * T, P))
    return {"text": bf(np.random.standard_normal((T, E)) * s),
            "wv": bf(np.random.standard_normal((E, H * C)) / np.sqrt(E) / s[:, None]),
            "reweight": bf(r / f),
            "attn_words": attn_words,
            "attn_scales": attn_scales,
            "renorm": bf(z)}


def core(text, wv, reweight, attn_words, attn_scales, renorm):
    v = mxq(f64(text), 1, "e4m3") @ mxq(f64(wv), 0, "e4m3")
    u = mxq(v * f64(reweight)[:, None], 0, "e4m3")
    u = u.reshape(T, H, C).transpose(1, 0, 2)
    a = unpack4(attn_words, attn_scales).reshape(H, T, P).transpose(0, 2, 1)
    y = a @ u
    return y * f64(renorm)[:, :, None]


def e4m3fn_bytes(y):
    return np.clip(np.asarray(y, np.float64), -448.0, 448.0).astype(np.float32).astype(ml_dtypes.float8_e4m3fn).view(np.uint8)


def e4m3fn_values(b):
    return np.asarray(b, np.uint8).view(ml_dtypes.float8_e4m3fn).astype(np.float64)


def setup_inputs():
    d = draw0()
    x0 = np.asarray(d['wv']).astype(np.float64)
    s = (np.max(np.abs(x0), axis=(1,), keepdims=True) / 448.0).astype(np.float32)
    out = {}
    for k, v in d.items():
        if k == 'wv':
            out['wv_bytes'] = e4m3fn_bytes(x0 / s.astype(np.float64))
            out['wv_scale'] = s
        else:
            out[k] = v
    return out


def reference(text, wv_bytes, wv_scale, reweight, attn_words, attn_scales, renorm):
    return core(text, e4m3fn_values(wv_bytes) * wv_scale.astype(np.float64), reweight, attn_words, attn_scales, renorm)

@@ -1,0 +1,384 @@
+from contextlib import ExitStack
+
+import concourse.mybir as mybir
+from concourse.masks import make_identity
+
+FLOPS = 2 * 512 * 2048 * 1024 + 2 * 8 * 2048 * 512 * 128
+
+F32 = mybir.dt.float32
+BF16 = mybir.dt.bfloat16
+I32 = mybir.dt.int32
+U32 = mybir.dt.uint32
+U8 = mybir.dt.uint8
+FP8 = mybir.dt.float8_e4m3fn
+E4X4 = mybir.dt.float8_e4m3fn_x4
+F4X4 = mybir.dt.float4_e2m1fn_x4
+COPY = mybir.ActivationFunctionType.Copy
+MULT = mybir.AluOpType.mult
+
+P = 128
+T, E, H, C, PIX = 512, 2048, 8, 128, 2048
+D = H * C
+G = E // 512
+GW = 512
+S_TILES = PIX // P
+
+
+def tile_prompt_map_edit_s13_kernel(tc, text, wv_bytes, wv_scale, reweight, attn_words, attn_scales, renorm, out):
+    nc = tc.nc
+    with ExitStack() as ctx:
+        keep = ctx.enter_context(tc.tile_pool(name="keep", bufs=1))
+        work = ctx.enter_context(tc.tile_pool(name="work", bufs=3))
+        ypool = ctx.enter_context(tc.tile_pool(name="ypool", bufs=6))
+        psum_v = ctx.enter_context(tc.psum_pool(name="psum_v", bufs=2))
+        psum_y = ctx.enter_context(tc.psum_pool(name="psum_y", bufs=6))
+        ctx.enter_context(tc.manual_schedule())
+
+        wscale = keep.tile([P, 4 * G], F32, name="wscale")
+        rw = keep.tile([P, 4], BF16, name="rw")
+        rn_rows = keep.tile([P, P], BF16, name="rn_rows")
+        rn_rows32 = keep.tile([P, P], F32, name="rn_rows32")
+        rn = keep.tile([P, P], F32, name="rn")
+        ident = keep.tile([P, P], F32, name="ident")
+        dummy = keep.tile([P, 2], F32, name="dummy")
+        wv_raw = [keep.tile([P, 4 * D], U8, name="wv_raw%d" % g) for g in range(G)]
+        text_sb = [keep.tile([P, E], BF16, name="text_sb%d" % t) for t in range(4)]
+        text_gr = [keep.tile([P, E], BF16, name="text_gr%d" % t, align_bytes=64) for t in range(4)]
+        text_codes = [keep.tile([P, E // 4], U32, name="text_codes%d" % t, align_bytes=64) for t in range(4)]
+        text_scales = [keep.tile([P, E // 4], U8, name="text_scales%d" % t, align_bytes=64) for t in range(4)]
+        wv_codes = [keep.tile([P, D], U32, name="wv_codes%d" % g, align_bytes=64) for g in range(G)]
+        wv_scales = [keep.tile([P, D], U8, name="wv_scales%d" % g, align_bytes=64) for g in range(G)]
+        a_words = [keep.tile([P, 2 * PIX], U8, name="a_words%d" % h, align_bytes=64) for h in range(H)]
+        a_scales = keep.tile([P, H * PIX], U8, name="a_scales", align_bytes=64)
+        u_codes = [keep.tile([P, C], U32, name="u_codes%d" % h, align_bytes=64) for h in range(H)]
+        u_scales = [keep.tile([P, C], U8, name="u_scales%d" % h, align_bytes=64) for h in range(H)]
+        y_sb = {}
+        rnt16 = keep.tile([P, 64], BF16, name="rnt16")
+        rnt = keep.tile([P, 64], F32, name="rnt")
+
+        nc.vector.memset(dummy[:], 0.0)
+        nc.scalar.activation(out=dummy[:, 0:1], in_=dummy[:, 1:2], func=COPY)
+        nc.vector.memset(a_scales[:].bitcast(I32), 0)
+        make_identity(nc, ident[:])
+
+        nc.sync.dma_start(
+            out=wscale[:].rearrange("p (g t) -> p g t", t=4),
+            in_=wv_scale.rearrange("(g p t) o -> p g (t o)", p=P, t=4),
+        )
+        text_rows = text.rearrange("(m t) e -> m t e", t=4)
+        for g in range(G):
+            nc.sync.dma_start(
+                out=wv_raw[g][:],
+                in_=wv_bytes[512 * g : 512 * (g + 1), :].rearrange("(p t) n -> p (t n)", t=4),
+            )
+        for t in range(4):
+            nc.sync.dma_start(out=text_sb[t][:], in_=text_rows[:, t, :])
+        nc.sync.dma_start(out=rw[:], in_=reweight.rearrange("(p t) -> p t", t=4))
+        nc.sync.dma_start(out=rn_rows[:], in_=renorm.rearrange("h (s p) -> (h s) p", p=P))
+        nc.sync.dma_start(
+            out=rnt16[:].rearrange("p (h k s) -> p h k s", h=4, k=2),
+            in_=renorm[4:8].rearrange("h (k p s) -> p h k s", k=2, s=8),
+        )
+        scale_rows = attn_scales.bitcast(I32).rearrange("h (q r) n -> r q h n", r=4)
+        a_scales_i = a_scales[:].bitcast(I32).rearrange("p (h n) -> p h n", h=H)
+        for r in range(4):
+            nc.sync.dma_start(out=a_scales_i[r:128:32], in_=scale_rows[r])
+        for h in range(H):
+            nc.sync.dma_start(out=a_words[h][:], in_=attn_words[h])
+
+        wide = {}
+        grouped = {}
+        v_ps = {}
+        u_gr = {}
+        y_ps = {}
+
+        def text_turn(t, engs):
+            words = text_sb[t][:].bitcast(F32)
+            for gp in range(2):
+                bank = psum_y.tile([P, 4, P], F32, name="bank")
+                for gg in range(2):
+                    g = 2 * gp + gg
+                    for u in range(2):
+                        nc.tensor.transpose(bank[:, 2 * gg + u, :], words[:, 256 * g + u : 256 * (g + 1) : 2], ident[:])
+                dst = text_gr[t][:, 1024 * gp : 1024 * (gp + 1)].bitcast(F32).rearrange("p (g m u) -> p g m u", g=2, u=2)
+                src = bank[:].rearrange("p (g u) m -> p g m u", u=2)
+                if engs[gp] == "s":
+                    nc.scalar.copy(out=dst, in_=src)
+                else:
+                    nc.vector.tensor_copy(out=dst, in_=src)
+
+        def text_quant(t):
+            nc.vector.quantize_mx(out=text_codes[t][:].bitcast(E4X4), scales=text_scales[t][:], in_=text_gr[t][:])
+
+        def widen(eng, b, g, t):
+            if (b, g) not in wide:
+                w = work.tile([P, 4, GW], BF16, name="wide", bufs=4)
+                wide[(b, g)] = w
+            src = wv_raw[g][:, D * t + GW * b : D * t + GW * (b + 1)].bitcast(FP8)
+            dst = wide[(b, g)][:, t, :]
+            sc = wscale[:, 4 * g + t : 4 * g + t + 1]
+            if eng == "s":
+                nc.scalar.activation(out=dst, in_=src, func=COPY, scale=sc)
+            else:
+                nc.vector.tensor_scalar(out=dst, in0=src, scalar1=sc, scalar2=None, op0=MULT)
+
+        def interleave(b, g):
+            gr = work.tile([P, 4 * GW], BF16, name="grouped", align_bytes=64, bufs=4)
+            grouped[(b, g)] = gr
+            nc.vector.tensor_copy(
+                out=gr[:].rearrange("p (c i t) -> p c t i", i=4, t=4),
+                in_=wide[(b, g)][:].rearrange("p t (c i) -> p c t i", i=4),
+            )
+
+        def wv_quant(b, g):
+            cols = slice(GW * b, GW * (b + 1))
+            nc.vector.quantize_mx(out=wv_codes[g][:, cols].bitcast(E4X4), scales=wv_scales[g][:, cols], in_=grouped[(b, g)][:])
+
+        def stage1(h):
+            ps = psum_v.tile([P, 4, C], F32, name="v_ps")
+            v_ps[h] = ps
+            for t in range(4):
+                for g in range(G):
+                    nc.tensor.matmul_mx(
+                        out=ps[:, t, :],
+                        lhsT=text_codes[t][:, P * g : P * (g + 1)].bitcast(E4X4),
+                        lhsT_scale=text_scales[t][:, P * g : P * (g + 1)],
+                        rhs=wv_codes[g][:, C * h : C * (h + 1)].bitcast(E4X4),
+                        rhs_scale=wv_scales[g][:, C * h : C * (h + 1)],
+                        start=(g == 0),
+                        stop=(g == G - 1),
+                    )
+
+        def u_evict(h):
+            ug = work.tile([P, 4 * C], BF16, name="u_gr", align_bytes=64)
+            u_gr[h] = ug
+            nc.vector.tensor_tensor(
+                out=ug[:].rearrange("p (n t) -> p n t", t=4),
+                in0=v_ps[h][:].rearrange("p t n -> p n t"),
+                in1=rw[:].unsqueeze(1).to_broadcast([P, C, 4]),
+                op=MULT,
+            )
+
+        def u_quant(h):
+            nc.vector.quantize_mx(out=u_codes[h][:].bitcast(E4X4), scales=u_scales[h][:], in_=u_gr[h][:])
+
+        def stage2(h, b):
+            ps = psum_y.tile([P, 4, C], F32, name="bank")
+            y_ps[(h, b)] = ps
+            for j in range(4):
+                s = 4 * b + j
+                nc.tensor.matmul_mx(
+                    out=ps[:, j, :],
+                    lhsT=a_words[h][:, 2 * P * s : 2 * P * (s + 1)].bitcast(F4X4),
+                    lhsT_scale=a_scales[:, PIX * h + P * s : PIX * h + P * (s + 1)],
+                    rhs=u_codes[h][:].bitcast(E4X4),
+                    rhs_scale=u_scales[h][:],
+                    start=True,
+                    stop=True,
+                )
+
+        def y_evict(eng, h, b):
+            new_y(h)
+            ps = y_ps[(h, b)]
+            col = S_TILES * h + 4 * b
+            if eng == "s":
+                for j in range(4):
+                    nc.scalar.activation(
+                        out=y_sb[h][:, 4 * b + j, :], in_=ps[:, j, :], func=COPY, scale=rn[:, col + j : col + j + 1]
+                    )
+            else:
+                nc.vector.tensor_tensor(
+                    out=y_sb[h][:, 4 * b : 4 * b + 4, :],
+                    in0=ps[:],
+                    in1=rn[:, col : col + 4].unsqueeze(2).to_broadcast([P, 4, C]),
+                    op=MULT,
+                )
+
+        yt = {}
+        z_ps = {}
+
+        def new_y(h):
+            if h not in y_sb:
+                y = ypool.tile([P, S_TILES, C], F32, name="y_sb")
+                y_sb[h] = y
+
+        def stage2t(h, k, i):
+            ps = psum_y.tile([P, 512], F32, name="bank")
+            y_ps[(h, k, i)] = ps
+            n0 = 512 * (2 * k + i)
+            nc.tensor.matmul_mx(
+                out=ps[:],
+                lhsT=u_codes[h][:].bitcast(E4X4),
+                lhsT_scale=u_scales[h][:],
+                rhs=a_words[h][:, 2 * n0 : 2 * (n0 + 512)].bitcast(F4X4),
+                rhs_scale=a_scales[:, PIX * h + n0 : PIX * h + n0 + 512],
+                start=True,
+                stop=True,
+            )
+
+        def regroup(eng, h, k, i):
+            if i == 0:
+                y = work.tile([P, 8, P], F32, name="yt")
+                yt[(h, k)] = y
+            dst = yt[(h, k)][:, :, 64 * i : 64 * (i + 1)]
+            src = y_ps[(h, k, i)][:].rearrange("c (p s) -> c s p", s=8)
+            if eng == "s":
+                nc.scalar.copy(out=dst, in_=src)
+            else:
+                nc.vector.tensor_copy(out=dst, in_=src)
+
+        def turn(h, k, q):
+            ps = psum_y.tile([P, 4, C], F32, name="bank")
+            z_ps[(h, k, q)] = ps
+            for j in range(4):
+                nc.tensor.transpose(ps[:, j, :], yt[(h, k)][:, 4 * q + j, :], ident[:])
+
+        def z_evict(eng, h, k, q):
+            ps = z_ps[(h, k, q)]
+            col = 16 * (h - 4) + 8 * k + 4 * q
+            new_y(h)
+            s0 = 8 * k + 4 * q
+            if eng == "s":
+                for j in range(4):
+                    nc.scalar.activation(
+                        out=y_sb[h][:, s0 + j, :], in_=ps[:, j, :], func=COPY, scale=rnt[:, col + j : col + j + 1]
+                    )
+            else:
+                nc.vector.tensor_tensor(
+                    out=y_sb[h][:, s0 : s0 + 4, :],
+                    in0=ps[:],
+                    in1=rnt[:, col : col + 4].unsqueeze(2).to_broadcast([P, 4, C]),
+                    op=MULT,
+                )
+
+        def storet(h, k):
+            nc.sync.dma_start(
+                out=out[h].rearrange("(k p s) c -> p k s c", k=2, s=8)[:, k],
+                in_=y_sb[h][:, 8 * k : 8 * k + 8, :],
+            )
+
+        def store(h, b0, b1):
+            nc.sync.dma_start(
+                out=out[h].rearrange("(s p) c -> p s c", p=P)[:, 4 * b0 : 4 * b1, :],
+                in_=y_sb[h][:, 4 * b0 : 4 * b1, :],
+            )
+
+        def widen4(b, g, engs):
+            for t in range(4):
+                widen(engs[t], b, g, t)
+
+        widen4(0, 0, "vsvv")
+        widen("v", 1, 0, 1)
+        widen("s", 1, 0, 0)
+        widen("s", 1, 0, 2)
+        interleave(0, 0)
+        widen4(0, 1, "vsss")
+        wv_quant(0, 0)
+        interleave(0, 1)
+        widen4(0, 2, "vsss")
+        wv_quant(0, 1)
+        widen4(0, 3, "vsss")
+        interleave(0, 2)
+        wv_quant(0, 2)
+        interleave(0, 3)
+        text_turn(0, "ss")
+        text_quant(0)
+        wv_quant(0, 3)
+        text_turn(1, "ss")
+        text_quant(1)
+        text_turn(2, "ss")
+        nc.vector.tensor_copy(out=rn_rows32[:], in_=rn_rows[:])
+        nc.vector.tensor_copy(out=rnt[:], in_=rnt16[:])
+        text_quant(2)
+        text_turn(3, "ss")
+        widen("v", 1, 0, 3)
+        text_quant(3)
+        rn_ps = psum_v.tile([P, P], F32, name="v_ps")
+        nc.tensor.transpose(rn_ps[:], rn_rows32[:], ident[:])
+        nc.scalar.copy(out=rn[:], in_=rn_ps[:])
+
+        def bank_y(eng, h, b, n=2):
+            stage2(h, b)
+            y_evict(eng, h, b)
+            if n == 1:
+                store(h, b, b + 1)
+            elif b % 2:
+                store(h, b - 1, b + 1)
+
+        stage1(0)
+        stage1(1)
+        widen4(1, 1, "ssss")
+        interleave(1, 0)
+        widen4(1, 2, "vsss")
+        u_evict(0)
+        wv_quant(1, 0)
+        u_quant(0)
+        u_evict(1)
+        stage1(2)
+        interleave(1, 1)
+        u_quant(1)
+        wv_quant(1, 1)
+        widen("s", 1, 3, 0)
+        widen("s", 1, 3, 1)
+        for b in range(4):
+            bank_y("s", 0, b)
+        interleave(1, 2)
+        u_evict(2)
+        wv_quant(1, 2)
+        u_quant(2)
+        for b in range(4):
+            bank_y("s", 1, b)
+        stage1(3)
+        widen("v", 1, 3, 2)
+        widen("v", 1, 3, 3)
+        u_evict(3)
+        interleave(1, 3)
+        u_quant(3)
+        wv_quant(1, 3)
+        for b in range(4):
+            bank_y("ssvv"[b], 2, b)
+        bank_y("s", 3, 0)
+        bank_y("v", 3, 1)
+        bank_y("s", 3, 2)
+        stage1(4)
+        bank_y("s", 3, 3)
+        stage1(5)
+        u_evict(4)
+        u_quant(4)
+        u_evict(5)
+
+        units = [(h, k) for h in range(4, 8) for k in range(2)]
+
+        def front(n):
+            h, k = units[n]
+            for i in range(2):
+                stage2t(h, k, i)
+                regroup("sv"[i], h, k, i)
+
+        def back(n):
+            h, k = units[n]
+            for q in range(2):
+                turn(h, k, q)
+                z_evict("sv"[q], h, k, q)
+            storet(h, k)
+
+        front(0)
+        u_quant(5)
+        front(1)
+        back(0)
+        stage1(6)
+        front(2)
+        back(1)
+        u_evict(6)
+        stage1(7)
+        front(3)
+        back(2)
+        u_quant(6)
+        u_evict(7)
+        front(4)
+        u_quant(7)
+        back(3)
+        for n in range(5, 8):
+            front(n)
+            back(n - 1)
+        back(7)

@@ -20,8 +20,12 @@ P = 128
 T, E, H, C, PIX = 512, 2048, 8, 128, 2048
 D = H * C
 G = E // 512
-GW = 512
-S_TILES = PIX // P
+HALF = PIX // 2
+RUN = HALF // P
+STEPS = 2 * H
+PAIR = 2 * C
+EARLY_HEADS = 2
+DIRECT = 3
 
 
 def tile_prompt_map_edit_s13_kernel(tc, text, wv_bytes, wv_scale, reweight, attn_words, attn_scales, renorm, out):
@@ -29,101 +33,117 @@ def tile_prompt_map_edit_s13_kernel(tc, text, wv_bytes, wv_scale, reweight, attn
     with ExitStack() as ctx:
         keep = ctx.enter_context(tc.tile_pool(name="keep", bufs=1))
         work = ctx.enter_context(tc.tile_pool(name="work", bufs=3))
-        ypool = ctx.enter_context(tc.tile_pool(name="ypool", bufs=6))
         psum_v = ctx.enter_context(tc.psum_pool(name="psum_v", bufs=2))
-        psum_y = ctx.enter_context(tc.psum_pool(name="psum_y", bufs=6))
+        psum_z = ctx.enter_context(tc.psum_pool(name="psum_z", bufs=3))
+        psum_y = ctx.enter_context(tc.psum_pool(name="psum_y", bufs=3))
         ctx.enter_context(tc.manual_schedule())
 
-        wscale = keep.tile([P, 4 * G], F32, name="wscale")
+        wscale = keep.tile([P, G, 8], F32, name="wscale")
         rw = keep.tile([P, 4], BF16, name="rw")
-        rn_rows = keep.tile([P, P], BF16, name="rn_rows")
-        rn_rows32 = keep.tile([P, P], F32, name="rn_rows32")
-        rn = keep.tile([P, P], F32, name="rn")
+        rn_rows = keep.tile([P, HALF], BF16, name="rn_rows")
+        rn = keep.tile([P, RUN, STEPS], F32, name="rn")
+        rn_d = keep.tile([P, RUN, 2 * DIRECT], F32, name="rn_d")
         ident = keep.tile([P, P], F32, name="ident")
-        dummy = keep.tile([P, 2], F32, name="dummy")
+        pick = keep.tile([P, STEPS], BF16, name="pick")
         wv_raw = [keep.tile([P, 4 * D], U8, name="wv_raw%d" % g) for g in range(G)]
         text_sb = [keep.tile([P, E], BF16, name="text_sb%d" % t) for t in range(4)]
-        text_gr = [keep.tile([P, E], BF16, name="text_gr%d" % t, align_bytes=64) for t in range(4)]
         text_codes = [keep.tile([P, E // 4], U32, name="text_codes%d" % t, align_bytes=64) for t in range(4)]
         text_scales = [keep.tile([P, E // 4], U8, name="text_scales%d" % t, align_bytes=64) for t in range(4)]
-        wv_codes = [keep.tile([P, D], U32, name="wv_codes%d" % g, align_bytes=64) for g in range(G)]
-        wv_scales = [keep.tile([P, D], U8, name="wv_scales%d" % g, align_bytes=64) for g in range(G)]
+        wv_codes = {}
+        wv_scales = {}
+        for b in range(H // 2):
+            for g in range(G):
+                wv_codes[(b, g)] = keep.tile([P, PAIR], U32, name="wv_codes%d%d" % (b, g), align_bytes=64)
+                wv_scales[(b, g)] = keep.tile([P, PAIR], U8, name="wv_scales%d%d" % (b, g), align_bytes=64)
         a_words = [keep.tile([P, 2 * PIX], U8, name="a_words%d" % h, align_bytes=64) for h in range(H)]
-        a_scales = keep.tile([P, H * PIX], U8, name="a_scales", align_bytes=64)
+        scale_runs = [range(0, EARLY_HEADS), range(EARLY_HEADS, H)]
+        a_scales = [keep.tile([P, len(r) * PIX], U8, name="a_scales%d" % r.start, align_bytes=64) for r in scale_runs]
         u_codes = [keep.tile([P, C], U32, name="u_codes%d" % h, align_bytes=64) for h in range(H)]
         u_scales = [keep.tile([P, C], U8, name="u_scales%d" % h, align_bytes=64) for h in range(H)]
-        y_sb = {}
-        rnt16 = keep.tile([P, 64], BF16, name="rnt16")
-        rnt = keep.tile([P, 64], F32, name="rnt")
 
-        nc.vector.memset(dummy[:], 0.0)
-        nc.scalar.activation(out=dummy[:, 0:1], in_=dummy[:, 1:2], func=COPY)
-        nc.vector.memset(a_scales[:].bitcast(I32), 0)
+        nc.vector.memset(rn_rows[:].bitcast(I32), 0)
+        nc.vector.memset(a_scales[0][:].bitcast(I32), 0)
+        nc.vector.memset(a_scales[1][:].bitcast(I32), 0)
         make_identity(nc, ident[:])
 
-        nc.sync.dma_start(
-            out=wscale[:].rearrange("p (g t) -> p g t", t=4),
-            in_=wv_scale.rearrange("(g p t) o -> p g (t o)", p=P, t=4),
-        )
         text_rows = text.rearrange("(m t) e -> m t e", t=4)
-        for g in range(G):
-            nc.sync.dma_start(
-                out=wv_raw[g][:],
-                in_=wv_bytes[512 * g : 512 * (g + 1), :].rearrange("(p t) n -> p (t n)", t=4),
-            )
-        for t in range(4):
+
+        def load_wv(g):
+            nc.sync.dma_start(out=wv_raw[g][:], in_=wv_bytes[512 * g : 512 * (g + 1), :].rearrange("(p t) n -> p (t n)", t=4))
+
+        def load_text(t):
             nc.sync.dma_start(out=text_sb[t][:], in_=text_rows[:, t, :])
-        nc.sync.dma_start(out=rw[:], in_=reweight.rearrange("(p t) -> p t", t=4))
-        nc.sync.dma_start(out=rn_rows[:], in_=renorm.rearrange("h (s p) -> (h s) p", p=P))
-        nc.sync.dma_start(
-            out=rnt16[:].rearrange("p (h k s) -> p h k s", h=4, k=2),
-            in_=renorm[4:8].rearrange("h (k p s) -> p h k s", k=2, s=8),
-        )
-        scale_rows = attn_scales.bitcast(I32).rearrange("h (q r) n -> r q h n", r=4)
-        a_scales_i = a_scales[:].bitcast(I32).rearrange("p (h n) -> p h n", h=H)
-        for r in range(4):
-            nc.sync.dma_start(out=a_scales_i[r:128:32], in_=scale_rows[r])
-        for h in range(H):
+
+        def load_scales(i):
+            heads = scale_runs[i]
+            rows = attn_scales[heads.start : heads.stop].bitcast(I32).rearrange("h (q r) n -> r q h n", r=4)
+            dst = a_scales[i][:].bitcast(I32).rearrange("p (h n) -> p h n", h=len(heads))
+            for r in range(4):
+                nc.sync.dma_start(out=dst[r:128:32], in_=rows[r])
+
+        def load_words(h):
             nc.sync.dma_start(out=a_words[h][:], in_=attn_words[h])
 
+        nc.scalar.dma_start(out=wscale[:, :, 0:4], in_=wv_scale.rearrange("(g p t) o -> p g (t o)", p=P, t=4))
+        load_wv(0)
+        load_text(0)
+        load_wv(1)
+        nc.sync.dma_start(out=rn_rows[0:STEPS, :], in_=renorm.rearrange("h (k n) -> (h k) n", k=2))
+        for t in range(1, 4):
+            load_text(t)
+        load_wv(2)
+        load_wv(3)
+        nc.sync.dma_start(out=rw[:], in_=reweight.rearrange("(p t) -> p t", t=4))
+        load_words(0)
+        load_scales(0)
+        load_words(1)
+        load_scales(1)
+        for h in range(2, H):
+            load_words(h)
+
+        text_gr = {}
         wide = {}
         grouped = {}
         v_ps = {}
         u_gr = {}
+        z_ps = {}
+        z_sb = {}
         y_ps = {}
+        y_sb = {}
 
-        def text_turn(t, engs):
+        def text_turn(t):
             words = text_sb[t][:].bitcast(F32)
+            gr = work.tile([P, E], BF16, name="text_gr", align_bytes=64, bufs=2)
+            text_gr[t] = gr
             for gp in range(2):
-                bank = psum_y.tile([P, 4, P], F32, name="bank")
+                if gp == 0:
+                    bank = psum_z.tile([P, 4, P], F32, name="z_bank")
+                else:
+                    bank = psum_y.tile([P, 4, P], F32, name="y_bank")
                 for gg in range(2):
                     g = 2 * gp + gg
                     for u in range(2):
                         nc.tensor.transpose(bank[:, 2 * gg + u, :], words[:, 256 * g + u : 256 * (g + 1) : 2], ident[:])
-                dst = text_gr[t][:, 1024 * gp : 1024 * (gp + 1)].bitcast(F32).rearrange("p (g m u) -> p g m u", g=2, u=2)
-                src = bank[:].rearrange("p (g u) m -> p g m u", u=2)
-                if engs[gp] == "s":
-                    nc.scalar.copy(out=dst, in_=src)
-                else:
-                    nc.vector.tensor_copy(out=dst, in_=src)
+                nc.scalar.copy(
+                    out=gr[:, 1024 * gp : 1024 * (gp + 1)].bitcast(F32).rearrange("p (g m u) -> p g m u", g=2, u=2),
+                    in_=bank[:].rearrange("p (g u) m -> p g m u", u=2),
+                )
 
         def text_quant(t):
             nc.vector.quantize_mx(out=text_codes[t][:].bitcast(E4X4), scales=text_scales[t][:], in_=text_gr[t][:])
 
-        def widen(eng, b, g, t):
-            if (b, g) not in wide:
-                w = work.tile([P, 4, GW], BF16, name="wide", bufs=4)
-                wide[(b, g)] = w
-            src = wv_raw[g][:, D * t + GW * b : D * t + GW * (b + 1)].bitcast(FP8)
-            dst = wide[(b, g)][:, t, :]
-            sc = wscale[:, 4 * g + t : 4 * g + t + 1]
-            if eng == "s":
-                nc.scalar.activation(out=dst, in_=src, func=COPY, scale=sc)
-            else:
-                nc.vector.tensor_scalar(out=dst, in0=src, scalar1=sc, scalar2=None, op0=MULT)
+        def widen(b, g, engines):
+            wide[(b, g)] = work.tile([P, 4, PAIR], BF16, name="wide", bufs=7)
+            for t in range(4):
+                src = wv_raw[g][:, D * t + PAIR * b : D * t + PAIR * (b + 1)].bitcast(FP8)
+                dst = wide[(b, g)][:, t, :]
+                if engines[t] == "s":
+                    nc.scalar.activation(out=dst, in_=src, func=COPY, scale=wscale[:, g, t : t + 1])
+                else:
+                    nc.vector.tensor_scalar(out=dst, in0=src, scalar1=wscale[:, g, t : t + 1], scalar2=None, op0=MULT)
 
         def interleave(b, g):
-            gr = work.tile([P, 4 * GW], BF16, name="grouped", align_bytes=64, bufs=4)
+            gr = work.tile([P, 4 * PAIR], BF16, name="grouped", align_bytes=64)
             grouped[(b, g)] = gr
             nc.vector.tensor_copy(
                 out=gr[:].rearrange("p (c i t) -> p c t i", i=4, t=4),
@@ -131,254 +151,215 @@ def tile_prompt_map_edit_s13_kernel(tc, text, wv_bytes, wv_scale, reweight, attn
             )
 
         def wv_quant(b, g):
-            cols = slice(GW * b, GW * (b + 1))
-            nc.vector.quantize_mx(out=wv_codes[g][:, cols].bitcast(E4X4), scales=wv_scales[g][:, cols], in_=grouped[(b, g)][:])
+            nc.vector.quantize_mx(out=wv_codes[(b, g)][:].bitcast(E4X4), scales=wv_scales[(b, g)][:], in_=grouped[(b, g)][:])
 
-        def stage1(h):
-            ps = psum_v.tile([P, 4, C], F32, name="v_ps")
-            v_ps[h] = ps
-            for t in range(4):
-                for g in range(G):
+        done = {}
+
+        def values(h, gs, ts):
+            if h not in v_ps:
+                if h // 2 == 1:
+                    v_ps[h] = psum_y.tile([P, 4, C], F32, name="y_bank")
+                else:
+                    v_ps[h] = psum_v.tile([P, 4, C], F32, name="v_bank")
+                done[h] = 0
+            b, c0 = h // 2, C * (h % 2)
+            for g in gs:
+                for t in ts:
+                    done[h] = done[h] + 1
                     nc.tensor.matmul_mx(
-                        out=ps[:, t, :],
+                        out=v_ps[h][:, t, :],
                         lhsT=text_codes[t][:, P * g : P * (g + 1)].bitcast(E4X4),
                         lhsT_scale=text_scales[t][:, P * g : P * (g + 1)],
-                        rhs=wv_codes[g][:, C * h : C * (h + 1)].bitcast(E4X4),
-                        rhs_scale=wv_scales[g][:, C * h : C * (h + 1)],
-                        start=(g == 0),
-                        stop=(g == G - 1),
+                        rhs=wv_codes[(b, g)][:, c0 : c0 + C].bitcast(E4X4),
+                        rhs_scale=wv_scales[(b, g)][:, c0 : c0 + C],
+                        start=(done[h] == 1),
+                        stop=(done[h] == 4 * G),
                     )
 
         def u_evict(h):
-            ug = work.tile([P, 4 * C], BF16, name="u_gr", align_bytes=64)
+            ug = work.tile([P, 4 * C], BF16, name="u_gr", align_bytes=64, bufs=2)
             u_gr[h] = ug
             nc.vector.tensor_tensor(
-                out=ug[:].rearrange("p (n t) -> p n t", t=4),
-                in0=v_ps[h][:].rearrange("p t n -> p n t"),
-                in1=rw[:].unsqueeze(1).to_broadcast([P, C, 4]),
+                out=ug[:].rearrange("p (c i t) -> p c t i", i=2, t=4),
+                in0=v_ps[h][:].rearrange("p t (c i) -> p c t i", i=2),
+                in1=rw[:].unsqueeze(1).unsqueeze(3).to_broadcast([P, C // 2, 4, 2]),
                 op=MULT,
             )
 
         def u_quant(h):
             nc.vector.quantize_mx(out=u_codes[h][:].bitcast(E4X4), scales=u_scales[h][:], in_=u_gr[h][:])
 
-        def stage2(h, b):
-            ps = psum_y.tile([P, 4, C], F32, name="bank")
-            y_ps[(h, b)] = ps
+        def mix(n, i):
+            h, k = divmod(n, 2)
+            ps = psum_z.tile([P, 512], F32, name="z_bank")
+            z_ps[(n, i)] = ps
+            n0 = HALF * k + 512 * i
+            run = 0 if h < EARLY_HEADS else 1
+            s0 = PIX * (h - scale_runs[run].start) + n0
+            nc.tensor.matmul_mx(
+                out=ps[:],
+                lhsT=u_codes[h][:].bitcast(E4X4),
+                lhsT_scale=u_scales[h][:],
+                rhs=a_words[h][:, 2 * n0 : 2 * (n0 + 512)].bitcast(F4X4),
+                rhs_scale=a_scales[run][:, s0 : s0 + 512],
+                start=True,
+                stop=True,
+            )
+
+        def mix_direct(n, q):
+            h, k = divmod(n, 2)
+            ps = psum_z.tile([P, 4, C], F32, name="z_bank")
+            y_ps[(n, q)] = ps
+            run = 0 if h < EARLY_HEADS else 1
             for j in range(4):
-                s = 4 * b + j
+                n0 = HALF * k + P * (4 * q + j)
+                s0 = PIX * (h - scale_runs[run].start) + n0
                 nc.tensor.matmul_mx(
                     out=ps[:, j, :],
-                    lhsT=a_words[h][:, 2 * P * s : 2 * P * (s + 1)].bitcast(F4X4),
-                    lhsT_scale=a_scales[:, PIX * h + P * s : PIX * h + P * (s + 1)],
+                    lhsT=a_words[h][:, 2 * n0 : 2 * (n0 + P)].bitcast(F4X4),
+                    lhsT_scale=a_scales[run][:, s0 : s0 + P],
                     rhs=u_codes[h][:].bitcast(E4X4),
                     rhs_scale=u_scales[h][:],
                     start=True,
                     stop=True,
                 )
 
-        def y_evict(eng, h, b):
-            new_y(h)
-            ps = y_ps[(h, b)]
-            col = S_TILES * h + 4 * b
-            if eng == "s":
-                for j in range(4):
-                    nc.scalar.activation(
-                        out=y_sb[h][:, 4 * b + j, :], in_=ps[:, j, :], func=COPY, scale=rn[:, col + j : col + j + 1]
-                    )
-            else:
-                nc.vector.tensor_tensor(
-                    out=y_sb[h][:, 4 * b : 4 * b + 4, :],
-                    in0=ps[:],
-                    in1=rn[:, col : col + 4].unsqueeze(2).to_broadcast([P, 4, C]),
-                    op=MULT,
-                )
-
-        yt = {}
-        z_ps = {}
-
-        def new_y(h):
-            if h not in y_sb:
-                y = ypool.tile([P, S_TILES, C], F32, name="y_sb")
-                y_sb[h] = y
-
-        def stage2t(h, k, i):
-            ps = psum_y.tile([P, 512], F32, name="bank")
-            y_ps[(h, k, i)] = ps
-            n0 = 512 * (2 * k + i)
-            nc.tensor.matmul_mx(
-                out=ps[:],
-                lhsT=u_codes[h][:].bitcast(E4X4),
-                lhsT_scale=u_scales[h][:],
-                rhs=a_words[h][:, 2 * n0 : 2 * (n0 + 512)].bitcast(F4X4),
-                rhs_scale=a_scales[:, PIX * h + n0 : PIX * h + n0 + 512],
-                start=True,
-                stop=True,
-            )
-
-        def regroup(eng, h, k, i):
+        def regroup(n, i):
             if i == 0:
-                y = work.tile([P, 8, P], F32, name="yt")
-                yt[(h, k)] = y
-            dst = yt[(h, k)][:, :, 64 * i : 64 * (i + 1)]
-            src = y_ps[(h, k, i)][:].rearrange("c (p s) -> c s p", s=8)
-            if eng == "s":
-                nc.scalar.copy(out=dst, in_=src)
-            else:
-                nc.vector.tensor_copy(out=dst, in_=src)
+                z_sb[n] = work.tile([P, RUN, P], F32, name="z_sb")
+            nc.scalar.copy(
+                out=z_sb[n][:, :, 64 * i : 64 * (i + 1)],
+                in_=z_ps[(n, i)][:].rearrange("c (p s) -> c s p", s=RUN),
+            )
 
-        def turn(h, k, q):
-            ps = psum_y.tile([P, 4, C], F32, name="bank")
-            z_ps[(h, k, q)] = ps
-            for j in range(4):
-                nc.tensor.transpose(ps[:, j, :], yt[(h, k)][:, 4 * q + j, :], ident[:])
-
-        def z_evict(eng, h, k, q):
-            ps = z_ps[(h, k, q)]
-            col = 16 * (h - 4) + 8 * k + 4 * q
-            new_y(h)
-            s0 = 8 * k + 4 * q
-            if eng == "s":
+        def turn(n):
+            for q in range(2):
+                ps = psum_y.tile([P, 4, C], F32, name="y_bank")
+                y_ps[(n, q)] = ps
                 for j in range(4):
-                    nc.scalar.activation(
-                        out=y_sb[h][:, s0 + j, :], in_=ps[:, j, :], func=COPY, scale=rnt[:, col + j : col + j + 1]
-                    )
+                    nc.tensor.transpose(ps[:, j, :], z_sb[n][:, 4 * q + j, :], ident[:])
+
+        def y_evict(n, q, on_scalar):
+            if n not in y_sb:
+                y_sb[n] = work.tile([P, RUN, C], F32, name="y_sb", bufs=10)
+            ps = y_ps[(n, q)]
+            fac = rn_d if n < 2 * DIRECT else rn
+            if on_scalar:
+                for j in range(4):
+                    s = 4 * q + j
+                    nc.scalar.activation(out=y_sb[n][:, s, :], in_=ps[:, j, :], func=COPY, scale=fac[:, s, n : n + 1])
             else:
                 nc.vector.tensor_tensor(
-                    out=y_sb[h][:, s0 : s0 + 4, :],
+                    out=y_sb[n][:, 4 * q : 4 * q + 4, :],
                     in0=ps[:],
-                    in1=rnt[:, col : col + 4].unsqueeze(2).to_broadcast([P, 4, C]),
+                    in1=fac[:, 4 * q : 4 * q + 4, n : n + 1].to_broadcast([P, 4, C]),
                     op=MULT,
                 )
 
-        def storet(h, k):
-            nc.sync.dma_start(
-                out=out[h].rearrange("(k p s) c -> p k s c", k=2, s=8)[:, k],
-                in_=y_sb[h][:, 8 * k : 8 * k + 8, :],
-            )
+        def store(n):
+            h, k = divmod(n, 2)
+            if h < DIRECT:
+                dst = out[h].rearrange("(k s p) c -> p k s c", k=2, s=RUN)[:, k]
+            else:
+                dst = out[h].rearrange("(k p s) c -> p k s c", k=2, s=RUN)[:, k]
+            nc.sync.dma_start(out=dst, in_=y_sb[n][:])
 
-        def store(h, b0, b1):
-            nc.sync.dma_start(
-                out=out[h].rearrange("(s p) c -> p s c", p=P)[:, 4 * b0 : 4 * b1, :],
-                in_=y_sb[h][:, 4 * b0 : 4 * b1, :],
-            )
-
-        def widen4(b, g, engs):
-            for t in range(4):
-                widen(engs[t], b, g, t)
-
-        widen4(0, 0, "vsvv")
-        widen("v", 1, 0, 1)
-        widen("s", 1, 0, 0)
-        widen("s", 1, 0, 2)
+        later = [(1, 2), (1, 3), (2, 1), (2, 2), (2, 3), (3, 0), (3, 1), (3, 2), (3, 3)]
+        ON_SCALAR = 5
+        nc.vector.tensor_copy(out=pick[:], in_=ident[:, 0:STEPS])
+        widen(0, 0, "vvvv")
+        widen(1, 0, "ssss")
+        widen(2, 0, "vvvv")
         interleave(0, 0)
-        widen4(0, 1, "vsss")
+        text_turn(0)
+        interleave(1, 0)
         wv_quant(0, 0)
+        widen(0, 1, "vvvv")
+        wv_quant(1, 0)
+        rn_ps = psum_y.tile([P, RUN, STEPS], F32, name="y_bank")
+        for s in range(RUN):
+            nc.tensor.matmul(rn_ps[:, s, :], lhsT=rn_rows[:, s:HALF:RUN], rhs=pick[:], start=True, stop=True)
+        rnd_ps = psum_z.tile([P, RUN, 2 * DIRECT], F32, name="z_bank")
+        for s in range(RUN):
+            nc.tensor.matmul(rnd_ps[:, s, :], lhsT=rn_rows[:, P * s : P * (s + 1)], rhs=pick[:, 0 : 2 * DIRECT], start=True, stop=True)
+        widen(1, 1, "ssss")
         interleave(0, 1)
-        widen4(0, 2, "vsss")
+        text_quant(0)
         wv_quant(0, 1)
-        widen4(0, 3, "vsss")
+        text_turn(1)
+        interleave(1, 1)
+        text_turn(2)
+        text_quant(1)
+        wv_quant(1, 1)
+        text_turn(3)
+        nc.scalar.copy(out=rn[:], in_=rn_ps[:])
+        nc.scalar.copy(out=rn_d[:], in_=rnd_ps[:])
+        widen(0, 2, "vvvv")
+        text_quant(2)
+        for h in range(2):
+            values(h, range(2), range(3))
         interleave(0, 2)
+        widen(0, 3, "vvss")
         wv_quant(0, 2)
         interleave(0, 3)
-        text_turn(0, "ss")
-        text_quant(0)
-        wv_quant(0, 3)
-        text_turn(1, "ss")
-        text_quant(1)
-        text_turn(2, "ss")
-        nc.vector.tensor_copy(out=rn_rows32[:], in_=rn_rows[:])
-        nc.vector.tensor_copy(out=rnt[:], in_=rnt16[:])
-        text_quant(2)
-        text_turn(3, "ss")
-        widen("v", 1, 0, 3)
         text_quant(3)
-        rn_ps = psum_v.tile([P, P], F32, name="v_ps")
-        nc.tensor.transpose(rn_ps[:], rn_rows32[:], ident[:])
-        nc.scalar.copy(out=rn[:], in_=rn_ps[:])
-
-        def bank_y(eng, h, b, n=2):
-            stage2(h, b)
-            y_evict(eng, h, b)
-            if n == 1:
-                store(h, b, b + 1)
-            elif b % 2:
-                store(h, b - 1, b + 1)
-
-        stage1(0)
-        stage1(1)
-        widen4(1, 1, "ssss")
-        interleave(1, 0)
-        widen4(1, 2, "vsss")
+        for b, g in later[:ON_SCALAR]:
+            widen(b, g, "ssss")
+        for h in range(2):
+            values(h, range(2, 3), range(3))
+        wv_quant(0, 3)
+        for h in range(2):
+            values(h, range(3), range(3, 4))
+            values(h, range(3, 4), range(4))
+        for h in range(2, 4):
+            values(h, range(2), range(4))
+        interleave(2, 0)
         u_evict(0)
-        wv_quant(1, 0)
+        wv_quant(2, 0)
         u_quant(0)
-        u_evict(1)
-        stage1(2)
-        interleave(1, 1)
-        u_quant(1)
-        wv_quant(1, 1)
-        widen("s", 1, 3, 0)
-        widen("s", 1, 3, 1)
-        for b in range(4):
-            bank_y("s", 0, b)
-        interleave(1, 2)
-        u_evict(2)
-        wv_quant(1, 2)
-        u_quant(2)
-        for b in range(4):
-            bank_y("s", 1, b)
-        stage1(3)
-        widen("v", 1, 3, 2)
-        widen("v", 1, 3, 3)
-        u_evict(3)
-        interleave(1, 3)
-        u_quant(3)
-        wv_quant(1, 3)
-        for b in range(4):
-            bank_y("ssvv"[b], 2, b)
-        bank_y("s", 3, 0)
-        bank_y("v", 3, 1)
-        bank_y("s", 3, 2)
-        stage1(4)
-        bank_y("s", 3, 3)
-        stage1(5)
-        u_evict(4)
-        u_quant(4)
-        u_evict(5)
 
-        units = [(h, k) for h in range(4, 8) for k in range(2)]
-
-        def front(n):
-            h, k = units[n]
-            for i in range(2):
-                stage2t(h, k, i)
-                regroup("sv"[i], h, k, i)
-
-        def back(n):
-            h, k = units[n]
+        unit_step = [max(0, j - 1) if j < ON_SCALAR else j for j in range(len(later))]
+        half_step = [1, 1] + [2, 3, 5, 6] + [8, 8, 9, 10]
+        halves = [(2 * b + j % 2, j // 2) for b in range(1, 4) for j in range(4)][2:]
+        for n in range(STEPS + 1):
+            units = [j for j in range(len(later)) if unit_step[j] == n]
+            ready = [h for (h, half), m in zip(halves, half_step) if half == 1 and m == n - 1] + ([1] if n == 0 else [])
+            direct = n < 2 * DIRECT
             for q in range(2):
-                turn(h, k, q)
-                z_evict("sv"[q], h, k, q)
-            storet(h, k)
-
-        front(0)
-        u_quant(5)
-        front(1)
-        back(0)
-        stage1(6)
-        front(2)
-        back(1)
-        u_evict(6)
-        stage1(7)
-        front(3)
-        back(2)
-        u_quant(6)
-        u_evict(7)
-        front(4)
-        u_quant(7)
-        back(3)
-        for n in range(5, 8):
-            front(n)
-            back(n - 1)
-        back(7)
+                if direct:
+                    mix_direct(n, q)
+                    y_evict(n, q, True)
+                elif n < STEPS:
+                    mix(n, q)
+            if direct:
+                store(n)
+            elif n < STEPS:
+                regroup(n, 0)
+            for (h, half), m in zip(halves, half_step):
+                if m == n:
+                    values(h, range(2 * half, 2 * half + 2), range(4))
+            if n > 2 * DIRECT:
+                turn(n - 1)
+            for j in units:
+                interleave(*later[j])
+                if j == units[0]:
+                    for h in ready:
+                        u_evict(h)
+                if ON_SCALAR <= j + 1 < len(later):
+                    widen(later[j + 1][0], later[j + 1][1], "vvvv")
+                if j == units[0]:
+                    for h in ready:
+                        u_quant(h)
+                wv_quant(*later[j])
+            if not units:
+                for h in ready:
+                    u_evict(h)
+            if not direct and n < STEPS:
+                regroup(n, 1)
+            if n > 2 * DIRECT:
+                y_evict(n - 1, 0, n <= 10)
+                y_evict(n - 1, 1, n <= 8)
+                store(n - 1)
+            if not units:
+                for h in ready:
+                    u_quant(h)

@@ -25,7 +25,7 @@ RUN = HALF // P
 STEPS = 2 * H
 PAIR = 2 * C
 EARLY_HEADS = 2
-DIRECT = 3
+DIRECT = range(6)
 
 
 def tile_prompt_map_edit_s13_kernel(tc, text, wv_bytes, wv_scale, reweight, attn_words, attn_scales, renorm, out):
@@ -41,8 +41,7 @@ def tile_prompt_map_edit_s13_kernel(tc, text, wv_bytes, wv_scale, reweight, attn
         wscale = keep.tile([P, G, 8], F32, name="wscale")
         rw = keep.tile([P, 4], BF16, name="rw")
         rn_rows = keep.tile([P, HALF], BF16, name="rn_rows")
-        rn = keep.tile([P, RUN, STEPS], F32, name="rn")
-        rn_d = keep.tile([P, RUN, 2 * DIRECT], F32, name="rn_d")
+        rn = keep.tile([P, 2, RUN, STEPS], F32, name="rn")
         ident = keep.tile([P, P], F32, name="ident")
         pick = keep.tile([P, STEPS], BF16, name="pick")
         wv_raw = [keep.tile([P, 4 * D], U8, name="wv_raw%d" % g) for g in range(G)]
@@ -113,7 +112,7 @@ def tile_prompt_map_edit_s13_kernel(tc, text, wv_bytes, wv_scale, reweight, attn
 
         def text_turn(t):
             words = text_sb[t][:].bitcast(F32)
-            gr = work.tile([P, E], BF16, name="text_gr", align_bytes=64, bufs=2)
+            gr = work.tile([P, E], BF16, name="text_gr", align_bytes=64, bufs=4)
             text_gr[t] = gr
             for gp in range(2):
                 if gp == 0:
@@ -132,11 +131,13 @@ def tile_prompt_map_edit_s13_kernel(tc, text, wv_bytes, wv_scale, reweight, attn
         def text_quant(t):
             nc.vector.quantize_mx(out=text_codes[t][:].bitcast(E4X4), scales=text_scales[t][:], in_=text_gr[t][:])
 
-        def widen(b, g, engines):
-            wide[(b, g)] = work.tile([P, 4, PAIR], BF16, name="wide", bufs=7)
+        def widen(bs, g, engines):
+            w = work.tile([P, 4, PAIR * len(bs)], BF16, name="wide%d" % len(bs), bufs=7 if len(bs) == 1 else 2)
+            for b in bs:
+                wide[(b, g)] = w[:, :, PAIR * (b - bs.start) : PAIR * (b - bs.start + 1)]
             for t in range(4):
-                src = wv_raw[g][:, D * t + PAIR * b : D * t + PAIR * (b + 1)].bitcast(FP8)
-                dst = wide[(b, g)][:, t, :]
+                src = wv_raw[g][:, D * t + PAIR * bs.start : D * t + PAIR * bs.stop].bitcast(FP8)
+                dst = w[:, t, :]
                 if engines[t] == "s":
                     nc.scalar.activation(out=dst, in_=src, func=COPY, scale=wscale[:, g, t : t + 1])
                 else:
@@ -147,7 +148,7 @@ def tile_prompt_map_edit_s13_kernel(tc, text, wv_bytes, wv_scale, reweight, attn
             grouped[(b, g)] = gr
             nc.vector.tensor_copy(
                 out=gr[:].rearrange("p (c i t) -> p c t i", i=4, t=4),
-                in_=wide[(b, g)][:].rearrange("p t (c i) -> p c t i", i=4),
+                in_=wide[(b, g)].rearrange("p t (c i) -> p c t i", i=4),
             )
 
         def wv_quant(b, g):
@@ -224,13 +225,15 @@ def tile_prompt_map_edit_s13_kernel(tc, text, wv_bytes, wv_scale, reweight, attn
                     stop=True,
                 )
 
-        def regroup(n, i):
+        def regroup(n, i, on_scalar):
             if i == 0:
                 z_sb[n] = work.tile([P, RUN, P], F32, name="z_sb")
-            nc.scalar.copy(
-                out=z_sb[n][:, :, 64 * i : 64 * (i + 1)],
-                in_=z_ps[(n, i)][:].rearrange("c (p s) -> c s p", s=RUN),
-            )
+            dst = z_sb[n][:, :, 64 * i : 64 * (i + 1)]
+            src = z_ps[(n, i)][:].rearrange("c (p s) -> c s p", s=RUN)
+            if on_scalar:
+                nc.scalar.copy(out=dst, in_=src)
+            else:
+                nc.vector.tensor_copy(out=dst, in_=src)
 
         def turn(n):
             for q in range(2):
@@ -243,7 +246,7 @@ def tile_prompt_map_edit_s13_kernel(tc, text, wv_bytes, wv_scale, reweight, attn
             if n not in y_sb:
                 y_sb[n] = work.tile([P, RUN, C], F32, name="y_sb", bufs=10)
             ps = y_ps[(n, q)]
-            fac = rn_d if n < 2 * DIRECT else rn
+            fac = rn[:, 0 if n in DIRECT else 1]
             if on_scalar:
                 for j in range(4):
                     s = 4 * q + j
@@ -256,110 +259,122 @@ def tile_prompt_map_edit_s13_kernel(tc, text, wv_bytes, wv_scale, reweight, attn
                     op=MULT,
                 )
 
-        def store(n):
+        def store(n, s0, s1):
             h, k = divmod(n, 2)
-            if h < DIRECT:
+            if n in DIRECT:
                 dst = out[h].rearrange("(k s p) c -> p k s c", k=2, s=RUN)[:, k]
             else:
                 dst = out[h].rearrange("(k p s) c -> p k s c", k=2, s=RUN)[:, k]
-            nc.sync.dma_start(out=dst, in_=y_sb[n][:])
+            nc.sync.dma_start(out=dst[:, s0:s1, :], in_=y_sb[n][:, s0:s1, :])
 
-        later = [(1, 2), (1, 3), (2, 1), (2, 2), (2, 3), (3, 0), (3, 1), (3, 2), (3, 3)]
-        ON_SCALAR = 5
+        def one(b):
+            return range(b, b + 1)
+
+        later = [(1, 1), (1, 2), (1, 3), (2, 0), (2, 1), (2, 2), (2, 3), (3, 0), (3, 1), (3, 2), (3, 3)]
+        ON_SCALAR = 6
         nc.vector.tensor_copy(out=pick[:], in_=ident[:, 0:STEPS])
-        widen(0, 0, "vvvv")
-        widen(1, 0, "ssss")
-        widen(2, 0, "vvvv")
+        widen(range(0, 2), 0, "vsvs")
+        widen(one(2), 0, "vvvs")
         interleave(0, 0)
         text_turn(0)
         interleave(1, 0)
         wv_quant(0, 0)
-        widen(0, 1, "vvvv")
+        widen(range(0, 2), 1, "vvvs")
         wv_quant(1, 0)
-        rn_ps = psum_y.tile([P, RUN, STEPS], F32, name="y_bank")
+        rn_ps = psum_v.tile([P, 2, RUN, STEPS], F32, name="v_bank")
         for s in range(RUN):
-            nc.tensor.matmul(rn_ps[:, s, :], lhsT=rn_rows[:, s:HALF:RUN], rhs=pick[:], start=True, stop=True)
-        rnd_ps = psum_z.tile([P, RUN, 2 * DIRECT], F32, name="z_bank")
-        for s in range(RUN):
-            nc.tensor.matmul(rnd_ps[:, s, :], lhsT=rn_rows[:, P * s : P * (s + 1)], rhs=pick[:, 0 : 2 * DIRECT], start=True, stop=True)
-        widen(1, 1, "ssss")
-        interleave(0, 1)
+            nc.tensor.matmul(rn_ps[:, 0, s, :], lhsT=rn_rows[:, P * s : P * (s + 1)], rhs=pick[:], start=True, stop=True)
+            nc.tensor.matmul(rn_ps[:, 1, s, :], lhsT=rn_rows[:, s:HALF:RUN], rhs=pick[:], start=True, stop=True)
+        nc.scalar.copy(out=rn[:], in_=rn_ps[:])
         text_quant(0)
-        wv_quant(0, 1)
         text_turn(1)
-        interleave(1, 1)
+        interleave(0, 1)
         text_turn(2)
         text_quant(1)
-        wv_quant(1, 1)
+        wv_quant(0, 1)
         text_turn(3)
-        nc.scalar.copy(out=rn[:], in_=rn_ps[:])
-        nc.scalar.copy(out=rn_d[:], in_=rnd_ps[:])
-        widen(0, 2, "vvvv")
+        widen(one(0), 2, "vvvv")
         text_quant(2)
         for h in range(2):
             values(h, range(2), range(3))
         interleave(0, 2)
-        widen(0, 3, "vvss")
+        widen(one(0), 3, "vvss")
         wv_quant(0, 2)
         interleave(0, 3)
         text_quant(3)
         for b, g in later[:ON_SCALAR]:
-            widen(b, g, "ssss")
+            if (b, g) not in wide:
+                widen(one(b), g, "ssss")
         for h in range(2):
             values(h, range(2, 3), range(3))
         wv_quant(0, 3)
         for h in range(2):
             values(h, range(3), range(3, 4))
             values(h, range(3, 4), range(4))
-        for h in range(2, 4):
-            values(h, range(2), range(4))
-        interleave(2, 0)
+        interleave(*later[0])
         u_evict(0)
-        wv_quant(2, 0)
+        wv_quant(*later[0])
         u_quant(0)
 
-        unit_step = [max(0, j - 1) if j < ON_SCALAR else j for j in range(len(later))]
-        half_step = [1, 1] + [2, 3, 5, 6] + [8, 8, 9, 10]
-        halves = [(2 * b + j % 2, j // 2) for b in range(1, 4) for j in range(4)][2:]
+        unit_step = [max(j // 2, j - 2) for j in range(len(later))]
+        evict_step = [1] + [m for m in (3, 6, 10) for h in range(2)]
+        passes = [(b, g) for b in range(1, 4) for g in range(G)]
+        mult_step = [min(unit_step[later.index(u)] + (2 if u[0] == 3 else 1), evict_step[2 * u[0] - 1] - 1) if u in later else 0 for u in passes]
+        pending = []
         for n in range(STEPS + 1):
-            units = [j for j in range(len(later)) if unit_step[j] == n]
-            ready = [h for (h, half), m in zip(halves, half_step) if half == 1 and m == n - 1] + ([1] if n == 0 else [])
-            direct = n < 2 * DIRECT
+            units = [j for j in range(1, len(later)) if unit_step[j] == n]
+            ready = [h for h in range(1, H) if evict_step[h - 1] == n]
+            direct = n in DIRECT
+            back = n >= 1 and n - 1 not in DIRECT
+            shared = n >= 15
             for q in range(2):
                 if direct:
                     mix_direct(n, q)
-                    y_evict(n, q, True)
                 elif n < STEPS:
                     mix(n, q)
-            if direct:
-                store(n)
-            elif n < STEPS:
-                regroup(n, 0)
-            for (h, half), m in zip(halves, half_step):
-                if m == n:
-                    values(h, range(2 * half, 2 * half + 2), range(4))
-            if n > 2 * DIRECT:
+            if not direct and n < STEPS:
+                regroup(n, 0, True)
+            if back:
                 turn(n - 1)
+            if not direct and n < STEPS:
+                regroup(n, 1, not shared)
+            for h in ready:
+                u_evict(h)
             for j in units:
                 interleave(*later[j])
-                if j == units[0]:
-                    for h in ready:
-                        u_evict(h)
-                if ON_SCALAR <= j + 1 < len(later):
-                    widen(later[j + 1][0], later[j + 1][1], "vvvv")
-                if j == units[0]:
-                    for h in ready:
-                        u_quant(h)
-                wv_quant(*later[j])
-            if not units:
-                for h in ready:
-                    u_evict(h)
-            if not direct and n < STEPS:
-                regroup(n, 1)
-            if n > 2 * DIRECT:
-                y_evict(n - 1, 0, n <= 10)
-                y_evict(n - 1, 1, n <= 8)
-                store(n - 1)
-            if not units:
+                spaced = bool(pending) or bool(ready)
+                for i in pending:
+                    wv_quant(*later[i])
+                pending.clear()
                 for h in ready:
                     u_quant(h)
+                ready = []
+                if j + 1 < len(later) and later[j + 1] not in wide:
+                    widen(one(later[j + 1][0]), later[j + 1][1], "vvvv")
+                    spaced = True
+                if spaced:
+                    wv_quant(*later[j])
+                else:
+                    pending.append(j)
+            if not units:
+                for i in pending:
+                    wv_quant(*later[i])
+                pending.clear()
+            if back:
+                y_evict(n - 1, 0, n <= 8 or shared)
+                if n == STEPS:
+                    store(n - 1, 0, 4)
+                y_evict(n - 1, 1, n <= 8)
+                store(n - 1, 4 if n == STEPS else 0, RUN)
+            if direct:
+                y_evict(n, 0, True)
+                if n == STEPS - 1:
+                    store(n, 0, 4)
+                y_evict(n, 1, n <= 8)
+                store(n, 4 if n == STEPS - 1 else 0, RUN)
+            for h in ready:
+                u_quant(h)
+            for (b, g), m in zip(passes, mult_step):
+                if m == n:
+                    values(2 * b, range(g, g + 1), range(4))
+                    values(2 * b + 1, range(g, g + 1), range(4))

@@ -24,7 +24,7 @@ HALF = PIX // 2
 RUN = HALF // P
 STEPS = 2 * H
 PAIR = 2 * C
-EARLY_HEADS = 2
+WORDS_AHEAD = 3
 DIRECT = range(6)
 
 
@@ -55,14 +55,12 @@ def tile_prompt_map_edit_s13_kernel(tc, text, wv_bytes, wv_scale, reweight, attn
                 wv_codes[(b, g)] = keep.tile([P, PAIR], U32, name="wv_codes%d%d" % (b, g), align_bytes=64)
                 wv_scales[(b, g)] = keep.tile([P, PAIR], U8, name="wv_scales%d%d" % (b, g), align_bytes=64)
         a_words = [keep.tile([P, 2 * PIX], U8, name="a_words%d" % h, align_bytes=64) for h in range(H)]
-        scale_runs = [range(0, EARLY_HEADS), range(EARLY_HEADS, H)]
-        a_scales = [keep.tile([P, len(r) * PIX], U8, name="a_scales%d" % r.start, align_bytes=64) for r in scale_runs]
+        a_scales = keep.tile([P, H * PIX], U8, name="a_scales", align_bytes=64)
         u_codes = [keep.tile([P, C], U32, name="u_codes%d" % h, align_bytes=64) for h in range(H)]
         u_scales = [keep.tile([P, C], U8, name="u_scales%d" % h, align_bytes=64) for h in range(H)]
 
         nc.vector.memset(rn_rows[:].bitcast(I32), 0)
-        nc.vector.memset(a_scales[0][:].bitcast(I32), 0)
-        nc.vector.memset(a_scales[1][:].bitcast(I32), 0)
+        nc.vector.memset(a_scales[:].bitcast(I32), 0)
         make_identity(nc, ident[:])
 
         text_rows = text.rearrange("(m t) e -> m t e", t=4)
@@ -73,10 +71,9 @@ def tile_prompt_map_edit_s13_kernel(tc, text, wv_bytes, wv_scale, reweight, attn
         def load_text(t):
             nc.sync.dma_start(out=text_sb[t][:], in_=text_rows[:, t, :])
 
-        def load_scales(i):
-            heads = scale_runs[i]
-            rows = attn_scales[heads.start : heads.stop].bitcast(I32).rearrange("h (q r) n -> r q h n", r=4)
-            dst = a_scales[i][:].bitcast(I32).rearrange("p (h n) -> p h n", h=len(heads))
+        def load_scales(b):
+            rows = attn_scales[2 * b : 2 * b + 2].bitcast(I32).rearrange("h (q r) n -> r q h n", r=4)
+            dst = a_scales[:, 2 * PIX * b : 2 * PIX * (b + 1)].bitcast(I32).rearrange("p (h n) -> p h n", h=2)
             for r in range(4):
                 nc.sync.dma_start(out=dst[r:128:32], in_=rows[r])
 
@@ -93,12 +90,10 @@ def tile_prompt_map_edit_s13_kernel(tc, text, wv_bytes, wv_scale, reweight, attn
         load_wv(2)
         load_wv(3)
         nc.sync.dma_start(out=rw[:], in_=reweight.rearrange("(p t) -> p t", t=4))
-        load_words(0)
-        load_scales(0)
-        load_words(1)
-        load_scales(1)
-        for h in range(2, H):
+        for h in range(WORDS_AHEAD):
             load_words(h)
+        for b in range(H // 2):
+            load_scales(b)
 
         text_gr = {}
         wide = {}
@@ -195,14 +190,13 @@ def tile_prompt_map_edit_s13_kernel(tc, text, wv_bytes, wv_scale, reweight, attn
             ps = psum_z.tile([P, 512], F32, name="z_bank")
             z_ps[(n, i)] = ps
             n0 = HALF * k + 512 * i
-            run = 0 if h < EARLY_HEADS else 1
-            s0 = PIX * (h - scale_runs[run].start) + n0
+            s0 = PIX * h + n0
             nc.tensor.matmul_mx(
                 out=ps[:],
                 lhsT=u_codes[h][:].bitcast(E4X4),
                 lhsT_scale=u_scales[h][:],
                 rhs=a_words[h][:, 2 * n0 : 2 * (n0 + 512)].bitcast(F4X4),
-                rhs_scale=a_scales[run][:, s0 : s0 + 512],
+                rhs_scale=a_scales[:, s0 : s0 + 512],
                 start=True,
                 stop=True,
             )
@@ -211,14 +205,13 @@ def tile_prompt_map_edit_s13_kernel(tc, text, wv_bytes, wv_scale, reweight, attn
             h, k = divmod(n, 2)
             ps = psum_z.tile([P, 4, C], F32, name="z_bank")
             y_ps[(n, q)] = ps
-            run = 0 if h < EARLY_HEADS else 1
             for j in range(4):
                 n0 = HALF * k + P * (4 * q + j)
-                s0 = PIX * (h - scale_runs[run].start) + n0
+                s0 = PIX * h + n0
                 nc.tensor.matmul_mx(
                     out=ps[:, j, :],
                     lhsT=a_words[h][:, 2 * n0 : 2 * (n0 + P)].bitcast(F4X4),
-                    lhsT_scale=a_scales[run][:, s0 : s0 + P],
+                    lhsT_scale=a_scales[:, s0 : s0 + P],
                     rhs=u_codes[h][:].bitcast(E4X4),
                     rhs_scale=u_scales[h][:],
                     start=True,
@@ -266,6 +259,8 @@ def tile_prompt_map_edit_s13_kernel(tc, text, wv_bytes, wv_scale, reweight, attn
             else:
                 dst = out[h].rearrange("(k p s) c -> p k s c", k=2, s=RUN)[:, k]
             nc.sync.dma_start(out=dst[:, s0:s1, :], in_=y_sb[n][:, s0:s1, :])
+            if 1 <= n <= H - WORDS_AHEAD:
+                load_words(WORDS_AHEAD + n - 1)
 
         def one(b):
             return range(b, b + 1)

@@ -24,7 +24,8 @@ HALF = PIX // 2
 RUN = HALF // P
 STEPS = 2 * H
 PAIR = 2 * C
-WORDS_AHEAD = 3
+WORDS_AHEAD = 7
+SCALES_AHEAD = 3
 DIRECT = range(6)
 
 
@@ -41,7 +42,7 @@ def tile_prompt_map_edit_s13_kernel(tc, text, wv_bytes, wv_scale, reweight, attn
         wscale = keep.tile([P, G, 8], F32, name="wscale")
         rw = keep.tile([P, 4], BF16, name="rw")
         rn_rows = keep.tile([P, HALF], BF16, name="rn_rows")
-        rn = keep.tile([P, 2, RUN, STEPS], F32, name="rn")
+        rn = keep.tile([P, 2, STEPS, RUN], F32, name="rn")
         ident = keep.tile([P, P], F32, name="ident")
         pick = keep.tile([P, STEPS], BF16, name="pick")
         wv_raw = [keep.tile([P, 4 * D], U8, name="wv_raw%d" % g) for g in range(G)]
@@ -71,10 +72,10 @@ def tile_prompt_map_edit_s13_kernel(tc, text, wv_bytes, wv_scale, reweight, attn
         def load_text(t):
             nc.sync.dma_start(out=text_sb[t][:], in_=text_rows[:, t, :])
 
-        def load_scales(b):
-            rows = attn_scales[2 * b : 2 * b + 2].bitcast(I32).rearrange("h (q r) n -> r q h n", r=4)
-            dst = a_scales[:, 2 * PIX * b : 2 * PIX * (b + 1)].bitcast(I32).rearrange("p (h n) -> p h n", h=2)
-            for r in range(4):
+        def load_scales(heads, rs):
+            rows = attn_scales[heads.start : heads.stop].bitcast(I32).rearrange("h (q r) n -> r q h n", r=4)
+            dst = a_scales[:, PIX * heads.start : PIX * heads.stop].bitcast(I32).rearrange("p (h n) -> p h n", h=len(heads))
+            for r in rs:
                 nc.sync.dma_start(out=dst[r:128:32], in_=rows[r])
 
         def load_words(h):
@@ -90,10 +91,10 @@ def tile_prompt_map_edit_s13_kernel(tc, text, wv_bytes, wv_scale, reweight, attn
         load_wv(2)
         load_wv(3)
         nc.sync.dma_start(out=rw[:], in_=reweight.rearrange("(p t) -> p t", t=4))
-        for h in range(WORDS_AHEAD):
+        load_words(0)
+        load_scales(range(SCALES_AHEAD), range(4))
+        for h in range(1, WORDS_AHEAD):
             load_words(h)
-        for b in range(H // 2):
-            load_scales(b)
 
         text_gr = {}
         wide = {}
@@ -239,16 +240,16 @@ def tile_prompt_map_edit_s13_kernel(tc, text, wv_bytes, wv_scale, reweight, attn
             if n not in y_sb:
                 y_sb[n] = work.tile([P, RUN, C], F32, name="y_sb", bufs=10)
             ps = y_ps[(n, q)]
-            fac = rn[:, 0 if n in DIRECT else 1]
+            fac = rn[:, 0 if n in DIRECT else 1, n, :]
             if on_scalar:
                 for j in range(4):
                     s = 4 * q + j
-                    nc.scalar.activation(out=y_sb[n][:, s, :], in_=ps[:, j, :], func=COPY, scale=fac[:, s, n : n + 1])
+                    nc.scalar.activation(out=y_sb[n][:, s, :], in_=ps[:, j, :], func=COPY, scale=fac[:, s : s + 1])
             else:
                 nc.vector.tensor_tensor(
                     out=y_sb[n][:, 4 * q : 4 * q + 4, :],
                     in0=ps[:],
-                    in1=fac[:, 4 * q : 4 * q + 4, n : n + 1].to_broadcast([P, 4, C]),
+                    in1=fac[:, 4 * q : 4 * q + 4].unsqueeze(2).to_broadcast([P, 4, C]),
                     op=MULT,
                 )
 
@@ -259,8 +260,11 @@ def tile_prompt_map_edit_s13_kernel(tc, text, wv_bytes, wv_scale, reweight, attn
             else:
                 dst = out[h].rearrange("(k p s) c -> p k s c", k=2, s=RUN)[:, k]
             nc.sync.dma_start(out=dst[:, s0:s1, :], in_=y_sb[n][:, s0:s1, :])
-            if 1 <= n <= H - WORDS_AHEAD:
-                load_words(WORDS_AHEAD + n - 1)
+            late = SCALES_AHEAD + n
+            if late < H:
+                load_scales(range(late, late + 1), range(4))
+            if n % 2 == 1 and WORDS_AHEAD + n // 2 < H:
+                load_words(WORDS_AHEAD + n // 2)
 
         def one(b):
             return range(b, b + 1)
@@ -280,7 +284,7 @@ def tile_prompt_map_edit_s13_kernel(tc, text, wv_bytes, wv_scale, reweight, attn
         for s in range(RUN):
             nc.tensor.matmul(rn_ps[:, 0, s, :], lhsT=rn_rows[:, P * s : P * (s + 1)], rhs=pick[:], start=True, stop=True)
             nc.tensor.matmul(rn_ps[:, 1, s, :], lhsT=rn_rows[:, s:HALF:RUN], rhs=pick[:], start=True, stop=True)
-        nc.scalar.copy(out=rn[:], in_=rn_ps[:])
+        nc.scalar.copy(out=rn[:], in_=rn_ps[:].rearrange("p d s n -> p d n s"))
         text_quant(0)
         text_turn(1)
         interleave(0, 1)
@@ -321,7 +325,7 @@ def tile_prompt_map_edit_s13_kernel(tc, text, wv_bytes, wv_scale, reweight, attn
             ready = [h for h in range(1, H) if evict_step[h - 1] == n]
             direct = n in DIRECT
             back = n >= 1 and n - 1 not in DIRECT
-            shared = n >= 15
+            shared = n >= 11
             for q in range(2):
                 if direct:
                     mix_direct(n, q)

@@ -56,12 +56,15 @@ def tile_prompt_map_edit_s13_kernel(tc, text, wv_bytes, wv_scale, reweight, attn
                 wv_codes[(b, g)] = keep.tile([P, PAIR], U32, name="wv_codes%d%d" % (b, g), align_bytes=64)
                 wv_scales[(b, g)] = keep.tile([P, PAIR], U8, name="wv_scales%d%d" % (b, g), align_bytes=64)
         a_words = [keep.tile([P, 2 * PIX], U8, name="a_words%d" % h, align_bytes=64) for h in range(H)]
-        a_scales = keep.tile([P, H * PIX], U8, name="a_scales", align_bytes=64)
+        scale_groups = [range(SCALES_AHEAD)] + [range(h, h + 1) for h in range(SCALES_AHEAD, H)]
+        scale_tiles = [keep.tile([P, len(r) * PIX], U8, name="a_scales%d" % r.start, align_bytes=64) for r in scale_groups]
+        a_scales = [scale_tiles[i][:, PIX * j : PIX * (j + 1)] for i, r in enumerate(scale_groups) for j in range(len(r))]
         u_codes = [keep.tile([P, C], U32, name="u_codes%d" % h, align_bytes=64) for h in range(H)]
         u_scales = [keep.tile([P, C], U8, name="u_scales%d" % h, align_bytes=64) for h in range(H)]
 
         nc.vector.memset(rn_rows[:].bitcast(I32), 0)
-        nc.vector.memset(a_scales[:].bitcast(I32), 0)
+        for tile in scale_tiles:
+            nc.vector.memset(tile[:].bitcast(I32), 0)
         make_identity(nc, ident[:])
 
         text_rows = text.rearrange("(m t) e -> m t e", t=4)
@@ -72,10 +75,11 @@ def tile_prompt_map_edit_s13_kernel(tc, text, wv_bytes, wv_scale, reweight, attn
         def load_text(t):
             nc.sync.dma_start(out=text_sb[t][:], in_=text_rows[:, t, :])
 
-        def load_scales(heads, rs):
+        def load_scales(i):
+            heads = scale_groups[i]
             rows = attn_scales[heads.start : heads.stop].bitcast(I32).rearrange("h (q r) n -> r q h n", r=4)
-            dst = a_scales[:, PIX * heads.start : PIX * heads.stop].bitcast(I32).rearrange("p (h n) -> p h n", h=len(heads))
-            for r in rs:
+            dst = scale_tiles[i][:].bitcast(I32).rearrange("p (h n) -> p h n", h=len(heads))
+            for r in range(4):
                 nc.sync.dma_start(out=dst[r:128:32], in_=rows[r])
 
         def load_words(h):
@@ -92,7 +96,7 @@ def tile_prompt_map_edit_s13_kernel(tc, text, wv_bytes, wv_scale, reweight, attn
         load_wv(3)
         nc.sync.dma_start(out=rw[:], in_=reweight.rearrange("(p t) -> p t", t=4))
         load_words(0)
-        load_scales(range(SCALES_AHEAD), range(4))
+        load_scales(0)
         for h in range(1, WORDS_AHEAD):
             load_words(h)
 
@@ -191,13 +195,12 @@ def tile_prompt_map_edit_s13_kernel(tc, text, wv_bytes, wv_scale, reweight, attn
             ps = psum_z.tile([P, 512], F32, name="z_bank")
             z_ps[(n, i)] = ps
             n0 = HALF * k + 512 * i
-            s0 = PIX * h + n0
             nc.tensor.matmul_mx(
                 out=ps[:],
                 lhsT=u_codes[h][:].bitcast(E4X4),
                 lhsT_scale=u_scales[h][:],
                 rhs=a_words[h][:, 2 * n0 : 2 * (n0 + 512)].bitcast(F4X4),
-                rhs_scale=a_scales[:, s0 : s0 + 512],
+                rhs_scale=a_scales[h][:, n0 : n0 + 512],
                 start=True,
                 stop=True,
             )
@@ -208,11 +211,10 @@ def tile_prompt_map_edit_s13_kernel(tc, text, wv_bytes, wv_scale, reweight, attn
             y_ps[(n, q)] = ps
             for j in range(4):
                 n0 = HALF * k + P * (4 * q + j)
-                s0 = PIX * h + n0
                 nc.tensor.matmul_mx(
                     out=ps[:, j, :],
                     lhsT=a_words[h][:, 2 * n0 : 2 * (n0 + P)].bitcast(F4X4),
-                    lhsT_scale=a_scales[:, s0 : s0 + P],
+                    lhsT_scale=a_scales[h][:, n0 : n0 + P],
                     rhs=u_codes[h][:].bitcast(E4X4),
                     rhs_scale=u_scales[h][:],
                     start=True,
@@ -260,9 +262,8 @@ def tile_prompt_map_edit_s13_kernel(tc, text, wv_bytes, wv_scale, reweight, attn
             else:
                 dst = out[h].rearrange("(k p s) c -> p k s c", k=2, s=RUN)[:, k]
             nc.sync.dma_start(out=dst[:, s0:s1, :], in_=y_sb[n][:, s0:s1, :])
-            late = SCALES_AHEAD + n
-            if late < H:
-                load_scales(range(late, late + 1), range(4))
+            if n + 1 < len(scale_groups):
+                load_scales(n + 1)
             if n % 2 == 1 and WORDS_AHEAD + n // 2 < H:
                 load_words(WORDS_AHEAD + n // 2)
 

@@ -132,7 +132,7 @@ def tile_prompt_map_edit_s13_kernel(tc, text, wv_bytes, wv_scale, reweight, attn
             nc.vector.quantize_mx(out=text_codes[t][:].bitcast(E4X4), scales=text_scales[t][:], in_=text_gr[t][:])
 
         def widen(bs, g, engines):
-            w = work.tile([P, 4, PAIR * len(bs)], BF16, name="wide%d" % len(bs), bufs=7 if len(bs) == 1 else 2)
+            w = work.tile([P, 4, PAIR * len(bs)], BF16, name="wide%d" % len(bs), bufs=8 if len(bs) == 1 else 2)
             for b in bs:
                 wide[(b, g)] = w[:, :, PAIR * (b - bs.start) : PAIR * (b - bs.start + 1)]
             for t in range(4):
@@ -271,7 +271,7 @@ def tile_prompt_map_edit_s13_kernel(tc, text, wv_bytes, wv_scale, reweight, attn
             return range(b, b + 1)
 
         later = [(1, 1), (1, 2), (1, 3), (2, 0), (2, 1), (2, 2), (2, 3), (3, 0), (3, 1), (3, 2), (3, 3)]
-        ON_SCALAR = 6
+        ON_SCALAR = 7
         nc.vector.tensor_copy(out=pick[:], in_=ident[:, 0:STEPS])
         widen(range(0, 2), 0, "vsvs")
         widen(one(2), 0, "vvvs")
@@ -316,10 +316,10 @@ def tile_prompt_map_edit_s13_kernel(tc, text, wv_bytes, wv_scale, reweight, attn
         wv_quant(*later[0])
         u_quant(0)
 
-        unit_step = [max(j // 2, j - 2) for j in range(len(later))]
-        evict_step = [1] + [m for m in (3, 6, 10) for h in range(2)]
+        unit_step = [max(0, j - 2) for j in range(len(later))]
+        evict_step = [1, 3, 4, 6, 6, 10, 10]
         passes = [(b, g) for b in range(1, 4) for g in range(G)]
-        mult_step = [min(unit_step[later.index(u)] + (2 if u[0] == 3 else 1), evict_step[2 * u[0] - 1] - 1) if u in later else 0 for u in passes]
+        mult_step = [min(unit_step[later.index(u)] + (2 if u[0] == 3 else 1), evict_step[2 * u[0] - 1] - 1) if u in later[1:] else 0 for u in passes]
         pending = []
         for n in range(STEPS + 1):
             units = [j for j in range(1, len(later)) if unit_step[j] == n]
@@ -361,17 +361,15 @@ def tile_prompt_map_edit_s13_kernel(tc, text, wv_bytes, wv_scale, reweight, attn
                     wv_quant(*later[i])
                 pending.clear()
             if back:
-                y_evict(n - 1, 0, n <= 8 or shared)
+                y_evict(n - 1, 0, True)
                 if n == STEPS:
                     store(n - 1, 0, 4)
                 y_evict(n - 1, 1, n <= 8)
                 store(n - 1, 4 if n == STEPS else 0, RUN)
             if direct:
                 y_evict(n, 0, True)
-                if n == STEPS - 1:
-                    store(n, 0, 4)
-                y_evict(n, 1, n <= 8)
-                store(n, 4 if n == STEPS - 1 else 0, RUN)
+                y_evict(n, 1, True)
+                store(n, 0, RUN)
             for h in ready:
                 u_quant(h)
             for (b, g), m in zip(passes, mult_step):

@@ -24,7 +24,8 @@ HALF = PIX // 2
 RUN = HALF // P
 STEPS = 2 * H
 PAIR = 2 * C
-WORDS_AHEAD = 7
+VALUES_DONE = 10
+WORDS_AHEAD = 8
 SCALES_AHEAD = 3
 DIRECT = range(6)
 
@@ -41,6 +42,7 @@ def tile_prompt_map_edit_s13_kernel(tc, text, wv_bytes, wv_scale, reweight, attn
 
         wscale = keep.tile([P, G, 8], F32, name="wscale")
         rw = keep.tile([P, 4], BF16, name="rw")
+        rw_walk = keep.tile([P, C // 2, 4, 2], F32, name="rw_walk")
         rn_rows = keep.tile([P, HALF], BF16, name="rn_rows")
         rn = keep.tile([P, 2, STEPS, RUN], F32, name="rn")
         ident = keep.tile([P, P], F32, name="ident")
@@ -56,14 +58,15 @@ def tile_prompt_map_edit_s13_kernel(tc, text, wv_bytes, wv_scale, reweight, attn
                 wv_codes[(b, g)] = keep.tile([P, PAIR], U32, name="wv_codes%d%d" % (b, g), align_bytes=64)
                 wv_scales[(b, g)] = keep.tile([P, PAIR], U8, name="wv_scales%d%d" % (b, g), align_bytes=64)
         a_words = [keep.tile([P, 2 * PIX], U8, name="a_words%d" % h, align_bytes=64) for h in range(H)]
-        scale_groups = [range(SCALES_AHEAD)] + [range(h, h + 1) for h in range(SCALES_AHEAD, H)]
-        scale_tiles = [keep.tile([P, len(r) * PIX], U8, name="a_scales%d" % r.start, align_bytes=64) for r in scale_groups]
+        scale_groups = [range(SCALES_AHEAD)] + [range(h, h + 1) for h in range(SCALES_AHEAD, H - 2)] + [range(H - 2, H)]
+        scale_tiles = [keep.tile([P, len(r) * PIX], U8, name="a_scales%d" % r.start, align_bytes=64) for r in scale_groups[:-1]]
+        scale_tiles.append(a_words[2])
         a_scales = [scale_tiles[i][:, PIX * j : PIX * (j + 1)] for i, r in enumerate(scale_groups) for j in range(len(r))]
         u_codes = [keep.tile([P, C], U32, name="u_codes%d" % h, align_bytes=64) for h in range(H)]
         u_scales = [keep.tile([P, C], U8, name="u_scales%d" % h, align_bytes=64) for h in range(H)]
 
         nc.vector.memset(rn_rows[:].bitcast(I32), 0)
-        for tile in scale_tiles:
+        for tile in scale_tiles[:-1]:
             nc.vector.memset(tile[:].bitcast(I32), 0)
         make_identity(nc, ident[:])
 
@@ -75,17 +78,19 @@ def tile_prompt_map_edit_s13_kernel(tc, text, wv_bytes, wv_scale, reweight, attn
         def load_text(t):
             nc.sync.dma_start(out=text_sb[t][:], in_=text_rows[:, t, :])
 
-        def load_scales(i):
+        def load_scales(i, queue):
             heads = scale_groups[i]
             rows = attn_scales[heads.start : heads.stop].bitcast(I32).rearrange("h (q r) n -> r q h n", r=4)
             dst = scale_tiles[i][:].bitcast(I32).rearrange("p (h n) -> p h n", h=len(heads))
             for r in range(4):
-                nc.sync.dma_start(out=dst[r:128:32], in_=rows[r])
+                queue.dma_start(out=dst[r:128:32], in_=rows[r])
 
         def load_words(h):
             nc.sync.dma_start(out=a_words[h][:], in_=attn_words[h])
 
         nc.scalar.dma_start(out=wscale[:, :, 0:4], in_=wv_scale.rearrange("(g p t) o -> p g (t o)", p=P, t=4))
+        nc.scalar.dma_start(out=rw[:], in_=reweight.rearrange("(p t) -> p t", t=4))
+        nc.scalar.copy(out=rw_walk[:], in_=rw[:].unsqueeze(1).unsqueeze(3).to_broadcast([P, C // 2, 4, 2]))
         load_wv(0)
         load_text(0)
         load_wv(1)
@@ -94,9 +99,8 @@ def tile_prompt_map_edit_s13_kernel(tc, text, wv_bytes, wv_scale, reweight, attn
             load_text(t)
         load_wv(2)
         load_wv(3)
-        nc.sync.dma_start(out=rw[:], in_=reweight.rearrange("(p t) -> p t", t=4))
         load_words(0)
-        load_scales(0)
+        load_scales(0, nc.sync)
         for h in range(1, WORDS_AHEAD):
             load_words(h)
 
@@ -183,7 +187,7 @@ def tile_prompt_map_edit_s13_kernel(tc, text, wv_bytes, wv_scale, reweight, attn
             nc.vector.tensor_tensor(
                 out=ug[:].rearrange("p (c i t) -> p c t i", i=2, t=4),
                 in0=v_ps[h][:].rearrange("p t (c i) -> p c t i", i=2),
-                in1=rw[:].unsqueeze(1).unsqueeze(3).to_broadcast([P, C // 2, 4, 2]),
+                in1=rw_walk[:],
                 op=MULT,
             )
 
@@ -233,7 +237,10 @@ def tile_prompt_map_edit_s13_kernel(tc, text, wv_bytes, wv_scale, reweight, attn
 
         def turn(n):
             for q in range(2):
-                ps = psum_y.tile([P, 4, C], F32, name="y_bank")
+                if q == 1 and n >= VALUES_DONE:
+                    ps = psum_v.tile([P, 4, C], F32, name="v_bank")
+                else:
+                    ps = psum_y.tile([P, 4, C], F32, name="y_bank")
                 y_ps[(n, q)] = ps
                 for j in range(4):
                     nc.tensor.transpose(ps[:, j, :], z_sb[n][:, 4 * q + j, :], ident[:])
@@ -262,8 +269,10 @@ def tile_prompt_map_edit_s13_kernel(tc, text, wv_bytes, wv_scale, reweight, attn
             else:
                 dst = out[h].rearrange("(k p s) c -> p k s c", k=2, s=RUN)[:, k]
             nc.sync.dma_start(out=dst[:, s0:s1, :], in_=y_sb[n][:, s0:s1, :])
-            if n + 1 < len(scale_groups):
-                load_scales(n + 1)
+            if n + 1 < len(scale_groups) - 1:
+                load_scales(n + 1, nc.sync)
+            if n == 5:
+                load_scales(len(scale_groups) - 1, nc.gpsimd)
             if n % 2 == 1 and WORDS_AHEAD + n // 2 < H:
                 load_words(WORDS_AHEAD + n // 2)
 

@@ -58,15 +58,14 @@ def tile_prompt_map_edit_s13_kernel(tc, text, wv_bytes, wv_scale, reweight, attn
                 wv_codes[(b, g)] = keep.tile([P, PAIR], U32, name="wv_codes%d%d" % (b, g), align_bytes=64)
                 wv_scales[(b, g)] = keep.tile([P, PAIR], U8, name="wv_scales%d%d" % (b, g), align_bytes=64)
         a_words = [keep.tile([P, 2 * PIX], U8, name="a_words%d" % h, align_bytes=64) for h in range(H)]
-        scale_groups = [range(SCALES_AHEAD)] + [range(h, h + 1) for h in range(SCALES_AHEAD, H - 2)] + [range(H - 2, H)]
-        scale_tiles = [keep.tile([P, len(r) * PIX], U8, name="a_scales%d" % r.start, align_bytes=64) for r in scale_groups[:-1]]
-        scale_tiles.append(a_words[2])
+        scale_groups = [range(SCALES_AHEAD)] + [range(h, h + 1) for h in range(SCALES_AHEAD, H)]
+        scale_tiles = [keep.tile([P, len(r) * PIX], U8, name="a_scales%d" % r.start, align_bytes=64) for r in scale_groups]
         a_scales = [scale_tiles[i][:, PIX * j : PIX * (j + 1)] for i, r in enumerate(scale_groups) for j in range(len(r))]
         u_codes = [keep.tile([P, C], U32, name="u_codes%d" % h, align_bytes=64) for h in range(H)]
         u_scales = [keep.tile([P, C], U8, name="u_scales%d" % h, align_bytes=64) for h in range(H)]
 
         nc.vector.memset(rn_rows[:].bitcast(I32), 0)
-        for tile in scale_tiles[:-1]:
+        for tile in scale_tiles:
             nc.vector.memset(tile[:].bitcast(I32), 0)
         make_identity(nc, ident[:])
 
@@ -78,12 +77,12 @@ def tile_prompt_map_edit_s13_kernel(tc, text, wv_bytes, wv_scale, reweight, attn
         def load_text(t):
             nc.sync.dma_start(out=text_sb[t][:], in_=text_rows[:, t, :])
 
-        def load_scales(i, queue):
+        def load_scales(i):
             heads = scale_groups[i]
             rows = attn_scales[heads.start : heads.stop].bitcast(I32).rearrange("h (q r) n -> r q h n", r=4)
             dst = scale_tiles[i][:].bitcast(I32).rearrange("p (h n) -> p h n", h=len(heads))
             for r in range(4):
-                queue.dma_start(out=dst[r:128:32], in_=rows[r])
+                nc.sync.dma_start(out=dst[r:128:32], in_=rows[r])
 
         def load_words(h):
             nc.sync.dma_start(out=a_words[h][:], in_=attn_words[h])
@@ -100,7 +99,7 @@ def tile_prompt_map_edit_s13_kernel(tc, text, wv_bytes, wv_scale, reweight, attn
         load_wv(2)
         load_wv(3)
         load_words(0)
-        load_scales(0, nc.sync)
+        load_scales(0)
         for h in range(1, WORDS_AHEAD):
             load_words(h)
 
@@ -269,10 +268,8 @@ def tile_prompt_map_edit_s13_kernel(tc, text, wv_bytes, wv_scale, reweight, attn
             else:
                 dst = out[h].rearrange("(k p s) c -> p k s c", k=2, s=RUN)[:, k]
             nc.sync.dma_start(out=dst[:, s0:s1, :], in_=y_sb[n][:, s0:s1, :])
-            if n + 1 < len(scale_groups) - 1:
-                load_scales(n + 1, nc.sync)
-            if n == 5:
-                load_scales(len(scale_groups) - 1, nc.gpsimd)
+            if n + 1 < len(scale_groups):
+                load_scales(n + 1)
             if n % 2 == 1 and WORDS_AHEAD + n // 2 < H:
                 load_words(WORDS_AHEAD + n // 2)
 

@@ -131,6 +131,11 @@ def tile_prompt_map_edit_s13_kernel(tc, text, wv_bytes, wv_scale, reweight, attn
                     in_=bank[:].rearrange("p (g u) m -> p g m u", u=2),
                 )
 
+        def turn_renorm(ps, turned, slots):
+            for s in slots:
+                cols = rn_rows[:, s:HALF:RUN] if turned else rn_rows[:, P * s : P * (s + 1)]
+                nc.tensor.matmul(ps[:, turned, s, :], lhsT=cols, rhs=pick[:], start=True, stop=True)
+
         def text_quant(t):
             nc.vector.quantize_mx(out=text_codes[t][:].bitcast(E4X4), scales=text_scales[t][:], in_=text_gr[t][:])
 
@@ -287,11 +292,6 @@ def tile_prompt_map_edit_s13_kernel(tc, text, wv_bytes, wv_scale, reweight, attn
         wv_quant(0, 0)
         widen(range(0, 2), 1, "vvvs")
         wv_quant(1, 0)
-        rn_ps = psum_v.tile([P, 2, RUN, STEPS], F32, name="v_bank")
-        for s in range(RUN):
-            nc.tensor.matmul(rn_ps[:, 0, s, :], lhsT=rn_rows[:, P * s : P * (s + 1)], rhs=pick[:], start=True, stop=True)
-            nc.tensor.matmul(rn_ps[:, 1, s, :], lhsT=rn_rows[:, s:HALF:RUN], rhs=pick[:], start=True, stop=True)
-        nc.scalar.copy(out=rn[:], in_=rn_ps[:].rearrange("p d s n -> p d n s"))
         text_quant(0)
         text_turn(1)
         interleave(0, 1)
@@ -299,6 +299,8 @@ def tile_prompt_map_edit_s13_kernel(tc, text, wv_bytes, wv_scale, reweight, attn
         text_quant(1)
         wv_quant(0, 1)
         text_turn(3)
+        rn_ps = psum_y.tile([P, 2, RUN, STEPS], F32, name="y_bank")
+        turn_renorm(rn_ps, 1, range(RUN // 2))
         widen(one(0), 2, "vvvv")
         text_quant(2)
         for h in range(2):
@@ -317,6 +319,9 @@ def tile_prompt_map_edit_s13_kernel(tc, text, wv_bytes, wv_scale, reweight, attn
         for h in range(2):
             values(h, range(3), range(3, 4))
             values(h, range(3, 4), range(4))
+        turn_renorm(rn_ps, 0, range(RUN))
+        turn_renorm(rn_ps, 1, range(RUN // 2, RUN))
+        nc.scalar.copy(out=rn[:], in_=rn_ps[:].rearrange("p d s n -> p d n s"))
         interleave(*later[0])
         u_evict(0)
         wv_quant(*later[0])

@@ -17,17 +17,22 @@ COPY = mybir.ActivationFunctionType.Copy
 MULT = mybir.AluOpType.mult
 
 P = 128
-T, E, H, C, PIX = 512, 2048, 8, 128, 2048
+E, H, C, PIX = 2048, 8, 128, 2048
 D = H * C
-G = E // 512
+PASS = 4 * P
+G = E // PASS
+BANK = 512
 HALF = PIX // 2
 RUN = HALF // P
 STEPS = 2 * H
+PAIRS = H // 2
 PAIR = 2 * C
-VALUES_DONE = 10
-WORDS_AHEAD = 8
-SCALES_AHEAD = 3
+
 DIRECT = range(6)
+SCALES_AHEAD = len(DIRECT) // 2
+WIDENED_AHEAD = 7
+UNITS_IN_STEP_0 = 2
+LAST_PAIR_FROM = 8
 
 
 def tile_prompt_map_edit_s13_kernel(tc, text, wv_bytes, wv_scale, reweight, attn_words, attn_scales, renorm, out):
@@ -53,7 +58,7 @@ def tile_prompt_map_edit_s13_kernel(tc, text, wv_bytes, wv_scale, reweight, attn
         text_scales = [keep.tile([P, E // 4], U8, name="text_scales%d" % t, align_bytes=64) for t in range(4)]
         wv_codes = {}
         wv_scales = {}
-        for b in range(H // 2):
+        for b in range(PAIRS):
             for g in range(G):
                 wv_codes[(b, g)] = keep.tile([P, PAIR], U32, name="wv_codes%d%d" % (b, g), align_bytes=64)
                 wv_scales[(b, g)] = keep.tile([P, PAIR], U8, name="wv_scales%d%d" % (b, g), align_bytes=64)
@@ -72,7 +77,7 @@ def tile_prompt_map_edit_s13_kernel(tc, text, wv_bytes, wv_scale, reweight, attn
         text_rows = text.rearrange("(m t) e -> m t e", t=4)
 
         def load_wv(g):
-            nc.sync.dma_start(out=wv_raw[g][:], in_=wv_bytes[512 * g : 512 * (g + 1), :].rearrange("(p t) n -> p (t n)", t=4))
+            nc.sync.dma_start(out=wv_raw[g][:], in_=wv_bytes[PASS * g : PASS * (g + 1), :].rearrange("(p t) n -> p (t n)", t=4))
 
         def load_text(t):
             nc.sync.dma_start(out=text_sb[t][:], in_=text_rows[:, t, :])
@@ -82,7 +87,7 @@ def tile_prompt_map_edit_s13_kernel(tc, text, wv_bytes, wv_scale, reweight, attn
             rows = attn_scales[heads.start : heads.stop].bitcast(I32).rearrange("h (q r) n -> r q h n", r=4)
             dst = scale_tiles[i][:].bitcast(I32).rearrange("p (h n) -> p h n", h=len(heads))
             for r in range(4):
-                nc.sync.dma_start(out=dst[r:128:32], in_=rows[r])
+                nc.sync.dma_start(out=dst[r:P:32], in_=rows[r])
 
         def load_words(h):
             nc.sync.dma_start(out=a_words[h][:], in_=attn_words[h])
@@ -100,13 +105,14 @@ def tile_prompt_map_edit_s13_kernel(tc, text, wv_bytes, wv_scale, reweight, attn
         load_wv(3)
         load_words(0)
         load_scales(0)
-        for h in range(1, WORDS_AHEAD):
+        for h in range(1, H):
             load_words(h)
 
         text_gr = {}
         wide = {}
         grouped = {}
         v_ps = {}
+        v_passes = {}
         u_gr = {}
         z_ps = {}
         z_sb = {}
@@ -125,9 +131,9 @@ def tile_prompt_map_edit_s13_kernel(tc, text, wv_bytes, wv_scale, reweight, attn
                 for gg in range(2):
                     g = 2 * gp + gg
                     for u in range(2):
-                        nc.tensor.transpose(bank[:, 2 * gg + u, :], words[:, 256 * g + u : 256 * (g + 1) : 2], ident[:])
+                        nc.tensor.transpose(bank[:, 2 * gg + u, :], words[:, 2 * P * g + u : 2 * P * (g + 1) : 2], ident[:])
                 nc.scalar.copy(
-                    out=gr[:, 1024 * gp : 1024 * (gp + 1)].bitcast(F32).rearrange("p (g m u) -> p g m u", g=2, u=2),
+                    out=gr[:, 2 * PASS * gp : 2 * PASS * (gp + 1)].bitcast(F32).rearrange("p (g m u) -> p g m u", g=2, u=2),
                     in_=bank[:].rearrange("p (g u) m -> p g m u", u=2),
                 )
 
@@ -139,12 +145,12 @@ def tile_prompt_map_edit_s13_kernel(tc, text, wv_bytes, wv_scale, reweight, attn
         def text_quant(t):
             nc.vector.quantize_mx(out=text_codes[t][:].bitcast(E4X4), scales=text_scales[t][:], in_=text_gr[t][:])
 
-        def widen(bs, g, engines):
-            w = work.tile([P, 4, PAIR * len(bs)], BF16, name="wide%d" % len(bs), bufs=8 if len(bs) == 1 else 2)
-            for b in bs:
-                wide[(b, g)] = w[:, :, PAIR * (b - bs.start) : PAIR * (b - bs.start + 1)]
+        def widen(pairs, g, engines):
+            w = work.tile([P, 4, PAIR * len(pairs)], BF16, name="wide%d" % len(pairs), bufs=8 if len(pairs) == 1 else 2)
+            for b in pairs:
+                wide[(b, g)] = w[:, :, PAIR * (b - pairs.start) : PAIR * (b - pairs.start + 1)]
             for t in range(4):
-                src = wv_raw[g][:, D * t + PAIR * bs.start : D * t + PAIR * bs.stop].bitcast(FP8)
+                src = wv_raw[g][:, D * t + PAIR * pairs.start : D * t + PAIR * pairs.stop].bitcast(FP8)
                 dst = w[:, t, :]
                 if engines[t] == "s":
                     nc.scalar.activation(out=dst, in_=src, func=COPY, scale=wscale[:, g, t : t + 1])
@@ -162,27 +168,25 @@ def tile_prompt_map_edit_s13_kernel(tc, text, wv_bytes, wv_scale, reweight, attn
         def wv_quant(b, g):
             nc.vector.quantize_mx(out=wv_codes[(b, g)][:].bitcast(E4X4), scales=wv_scales[(b, g)][:], in_=grouped[(b, g)][:])
 
-        done = {}
-
         def values(h, gs, ts):
             if h not in v_ps:
                 if h // 2 == 1:
                     v_ps[h] = psum_y.tile([P, 4, C], F32, name="y_bank")
                 else:
                     v_ps[h] = psum_v.tile([P, 4, C], F32, name="v_bank")
-                done[h] = 0
+                v_passes[h] = 0
             b, c0 = h // 2, C * (h % 2)
             for g in gs:
                 for t in ts:
-                    done[h] = done[h] + 1
+                    v_passes[h] = v_passes[h] + 1
                     nc.tensor.matmul_mx(
                         out=v_ps[h][:, t, :],
                         lhsT=text_codes[t][:, P * g : P * (g + 1)].bitcast(E4X4),
                         lhsT_scale=text_scales[t][:, P * g : P * (g + 1)],
                         rhs=wv_codes[(b, g)][:, c0 : c0 + C].bitcast(E4X4),
                         rhs_scale=wv_scales[(b, g)][:, c0 : c0 + C],
-                        start=(done[h] == 1),
-                        stop=(done[h] == 4 * G),
+                        start=(v_passes[h] == 1),
+                        stop=(v_passes[h] == 4 * G),
                     )
 
         def u_evict(h):
@@ -198,17 +202,17 @@ def tile_prompt_map_edit_s13_kernel(tc, text, wv_bytes, wv_scale, reweight, attn
         def u_quant(h):
             nc.vector.quantize_mx(out=u_codes[h][:].bitcast(E4X4), scales=u_scales[h][:], in_=u_gr[h][:])
 
-        def mix(n, i):
+        def mix_turned(n, q):
             h, k = divmod(n, 2)
-            ps = psum_z.tile([P, 512], F32, name="z_bank")
-            z_ps[(n, i)] = ps
-            n0 = HALF * k + 512 * i
+            ps = psum_z.tile([P, BANK], F32, name="z_bank")
+            z_ps[(n, q)] = ps
+            i0 = HALF * k + BANK * q
             nc.tensor.matmul_mx(
                 out=ps[:],
                 lhsT=u_codes[h][:].bitcast(E4X4),
                 lhsT_scale=u_scales[h][:],
-                rhs=a_words[h][:, 2 * n0 : 2 * (n0 + 512)].bitcast(F4X4),
-                rhs_scale=a_scales[h][:, n0 : n0 + 512],
+                rhs=a_words[h][:, 2 * i0 : 2 * (i0 + BANK)].bitcast(F4X4),
+                rhs_scale=a_scales[h][:, i0 : i0 + BANK],
                 start=True,
                 stop=True,
             )
@@ -218,30 +222,30 @@ def tile_prompt_map_edit_s13_kernel(tc, text, wv_bytes, wv_scale, reweight, attn
             ps = psum_z.tile([P, 4, C], F32, name="z_bank")
             y_ps[(n, q)] = ps
             for j in range(4):
-                n0 = HALF * k + P * (4 * q + j)
+                i0 = HALF * k + P * (4 * q + j)
                 nc.tensor.matmul_mx(
                     out=ps[:, j, :],
-                    lhsT=a_words[h][:, 2 * n0 : 2 * (n0 + P)].bitcast(F4X4),
-                    lhsT_scale=a_scales[h][:, n0 : n0 + P],
+                    lhsT=a_words[h][:, 2 * i0 : 2 * (i0 + P)].bitcast(F4X4),
+                    lhsT_scale=a_scales[h][:, i0 : i0 + P],
                     rhs=u_codes[h][:].bitcast(E4X4),
                     rhs_scale=u_scales[h][:],
                     start=True,
                     stop=True,
                 )
 
-        def regroup(n, i, on_scalar):
-            if i == 0:
+        def regroup(n, q, on_scalar):
+            if q == 0:
                 z_sb[n] = work.tile([P, RUN, P], F32, name="z_sb")
-            dst = z_sb[n][:, :, 64 * i : 64 * (i + 1)]
-            src = z_ps[(n, i)][:].rearrange("c (p s) -> c s p", s=RUN)
+            dst = z_sb[n][:, :, P // 2 * q : P // 2 * (q + 1)]
+            src = z_ps[(n, q)][:].rearrange("c (p s) -> c s p", s=RUN)
             if on_scalar:
                 nc.scalar.copy(out=dst, in_=src)
             else:
                 nc.vector.tensor_copy(out=dst, in_=src)
 
-        def turn(n):
+        def turn(n, values_done):
             for q in range(2):
-                if q == 1 and n >= VALUES_DONE:
+                if q == 1 and values_done:
                     ps = psum_v.tile([P, 4, C], F32, name="v_bank")
                 else:
                     ps = psum_y.tile([P, 4, C], F32, name="y_bank")
@@ -275,14 +279,11 @@ def tile_prompt_map_edit_s13_kernel(tc, text, wv_bytes, wv_scale, reweight, attn
             nc.sync.dma_start(out=dst[:, s0:s1, :], in_=y_sb[n][:, s0:s1, :])
             if n + 1 < len(scale_groups):
                 load_scales(n + 1)
-            if n % 2 == 1 and WORDS_AHEAD + n // 2 < H:
-                load_words(WORDS_AHEAD + n // 2)
 
         def one(b):
             return range(b, b + 1)
 
-        later = [(1, 1), (1, 2), (1, 3), (2, 0), (2, 1), (2, 2), (2, 3), (3, 0), (3, 1), (3, 2), (3, 3)]
-        ON_SCALAR = 7
+        later = [(b, g) for b in range(1, PAIRS) for g in range(G)][1:]
         nc.vector.tensor_copy(out=pick[:], in_=ident[:, 0:STEPS])
         widen(range(0, 2), 0, "vsvs")
         widen(one(2), 0, "vvvs")
@@ -310,7 +311,7 @@ def tile_prompt_map_edit_s13_kernel(tc, text, wv_bytes, wv_scale, reweight, attn
         wv_quant(0, 2)
         interleave(0, 3)
         text_quant(3)
-        for b, g in later[:ON_SCALAR]:
+        for b, g in later[:WIDENED_AHEAD]:
             if (b, g) not in wide:
                 widen(one(b), g, "ssss")
         for h in range(2):
@@ -327,28 +328,32 @@ def tile_prompt_map_edit_s13_kernel(tc, text, wv_bytes, wv_scale, reweight, attn
         wv_quant(*later[0])
         u_quant(0)
 
-        unit_step = [max(0, j - 2) for j in range(len(later))]
-        evict_step = [1, 3, 4, 6, 6, 10, 10]
-        passes = [(b, g) for b in range(1, 4) for g in range(G)]
-        mult_step = [min(unit_step[later.index(u)] + (2 if u[0] == 3 else 1), evict_step[2 * u[0] - 1] - 1) if u in later[1:] else 0 for u in passes]
+        unit_step = {unit: max(0, j - UNITS_IN_STEP_0) for j, unit in enumerate(later)}
+        mult_step = {(1, g): g // 2 for g in range(G)}
+        mult_step.update({(2, g): unit_step[(2, g)] + 1 for g in range(G)})
+        mult_step.update({(3, g): max(unit_step[(3, g)] + 1, LAST_PAIR_FROM) for g in range(G)})
+        evict_step = {h: 2 * h - 1 if h < 4 else mult_step[(h // 2, G - 1)] + 1 for h in range(1, H)}
+        last_unit_step = unit_step[later[-1]]
+        last_evict_step = evict_step[H - 1]
+
         pending = []
         for n in range(STEPS + 1):
-            units = [j for j in range(1, len(later)) if unit_step[j] == n]
-            ready = [h for h in range(1, H) if evict_step[h - 1] == n]
+            units = [j for j in range(1, len(later)) if unit_step[later[j]] == n]
+            ready = [h for h in range(1, H) if evict_step[h] == n]
             direct = n in DIRECT
+            turned = not direct and n < STEPS
             back = n >= 1 and n - 1 not in DIRECT
-            shared = n >= 11
             for q in range(2):
                 if direct:
                     mix_direct(n, q)
-                elif n < STEPS:
-                    mix(n, q)
-            if not direct and n < STEPS:
+                elif turned:
+                    mix_turned(n, q)
+            if turned:
                 regroup(n, 0, True)
             if back:
-                turn(n - 1)
-            if not direct and n < STEPS:
-                regroup(n, 1, not shared)
+                turn(n - 1, n > last_evict_step)
+            if turned:
+                regroup(n, 1, n <= last_evict_step)
             for h in ready:
                 u_evict(h)
             for j in units:
@@ -374,16 +379,16 @@ def tile_prompt_map_edit_s13_kernel(tc, text, wv_bytes, wv_scale, reweight, attn
             if back:
                 y_evict(n - 1, 0, True)
                 if n == STEPS:
-                    store(n - 1, 0, 4)
-                y_evict(n - 1, 1, n <= 8)
-                store(n - 1, 4 if n == STEPS else 0, RUN)
+                    store(n - 1, 0, RUN // 2)
+                y_evict(n - 1, 1, n <= last_unit_step)
+                store(n - 1, RUN // 2 if n == STEPS else 0, RUN)
             if direct:
                 y_evict(n, 0, True)
                 y_evict(n, 1, True)
                 store(n, 0, RUN)
             for h in ready:
                 u_quant(h)
-            for (b, g), m in zip(passes, mult_step):
+            for (b, g), m in mult_step.items():
                 if m == n:
                     values(2 * b, range(g, g + 1), range(4))
                     values(2 * b + 1, range(g, g + 1), range(4))

@@ -9,6 +9,7 @@ F32 = mybir.dt.float32
 BF16 = mybir.dt.bfloat16
 I32 = mybir.dt.int32
 U32 = mybir.dt.uint32
+U16 = mybir.dt.uint16
 U8 = mybir.dt.uint8
 FP8 = mybir.dt.float8_e4m3fn
 E4X4 = mybir.dt.float8_e4m3fn_x4
@@ -23,16 +24,16 @@ PASS = 4 * P
 G = E // PASS
 BANK = 512
 HALF = PIX // 2
-RUN = HALF // P
+RUN = BANK // P
 STEPS = 2 * H
+BANKS = 2 * STEPS
+ROWS = 16
 PAIRS = H // 2
 PAIR = 2 * C
 
-DIRECT = range(6)
-SCALES_AHEAD = len(DIRECT) // 2
-WIDENED_AHEAD = 7
-UNITS_IN_STEP_0 = 2
-LAST_PAIR_FROM = 8
+SORTED_BY_SCALAR = range(3, 10, 2)
+VECTOR_EVICTS_FROM = 10
+SPREAD_AHEAD = 8
 
 
 def tile_prompt_map_edit_s13_kernel(tc, text, wv_bytes, wv_scale, reweight, attn_words, attn_scales, renorm, out):
@@ -40,18 +41,17 @@ def tile_prompt_map_edit_s13_kernel(tc, text, wv_bytes, wv_scale, reweight, attn
     with ExitStack() as ctx:
         keep = ctx.enter_context(tc.tile_pool(name="keep", bufs=1))
         work = ctx.enter_context(tc.tile_pool(name="work", bufs=3))
-        psum_v = ctx.enter_context(tc.psum_pool(name="psum_v", bufs=2))
-        psum_z = ctx.enter_context(tc.psum_pool(name="psum_z", bufs=3))
-        psum_y = ctx.enter_context(tc.psum_pool(name="psum_y", bufs=3))
+        psum_v = ctx.enter_context(tc.psum_pool(name="psum_v", bufs=4))
+        psum_y = ctx.enter_context(tc.psum_pool(name="psum_y", bufs=4))
         ctx.enter_context(tc.manual_schedule())
 
         wscale = keep.tile([P, G, 8], F32, name="wscale")
         rw = keep.tile([P, 4], BF16, name="rw")
         rw_walk = keep.tile([P, C // 2, 4, 2], F32, name="rw_walk")
-        rn_rows = keep.tile([P, HALF], BF16, name="rn_rows")
-        rn = keep.tile([P, 2, STEPS, RUN], F32, name="rn")
+        rn_rows = keep.tile([P, BANK], BF16, name="rn_rows")
+        rn = keep.tile([P, BANKS, RUN], F32, name="rn")
         ident = keep.tile([P, P], F32, name="ident")
-        pick = keep.tile([P, STEPS], BF16, name="pick")
+        pick = keep.tile([P, BANKS], BF16, name="pick")
         wv_raw = [keep.tile([P, 4 * D], U8, name="wv_raw%d" % g) for g in range(G)]
         text_sb = [keep.tile([P, E], BF16, name="text_sb%d" % t) for t in range(4)]
         text_codes = [keep.tile([P, E // 4], U32, name="text_codes%d" % t, align_bytes=64) for t in range(4)]
@@ -62,15 +62,15 @@ def tile_prompt_map_edit_s13_kernel(tc, text, wv_bytes, wv_scale, reweight, attn
             for g in range(G):
                 wv_codes[(b, g)] = keep.tile([P, PAIR], U32, name="wv_codes%d%d" % (b, g), align_bytes=64)
                 wv_scales[(b, g)] = keep.tile([P, PAIR], U8, name="wv_scales%d%d" % (b, g), align_bytes=64)
-        a_words = [keep.tile([P, 2 * PIX], U8, name="a_words%d" % h, align_bytes=64) for h in range(H)]
-        scale_groups = [range(SCALES_AHEAD)] + [range(h, h + 1) for h in range(SCALES_AHEAD, H)]
-        scale_tiles = [keep.tile([P, len(r) * PIX], U8, name="a_scales%d" % r.start, align_bytes=64) for r in scale_groups]
-        a_scales = [scale_tiles[i][:, PIX * j : PIX * (j + 1)] for i, r in enumerate(scale_groups) for j in range(len(r))]
+        a_words = [keep.tile([P, 2 * PIX], U8, name="a_words%d" % h) for h in range(H)]
+        rows_raw = keep.tile([P, PIX], U8, name="rows_raw")
+        rows_sorted = keep.tile([P, PIX], U8, name="rows_sorted")
+        a_scales = [keep.tile([P, PIX], U8, name="a_scales%d" % h, align_bytes=64) for h in range(H)]
         u_codes = [keep.tile([P, C], U32, name="u_codes%d" % h, align_bytes=64) for h in range(H)]
         u_scales = [keep.tile([P, C], U8, name="u_scales%d" % h, align_bytes=64) for h in range(H)]
 
         nc.vector.memset(rn_rows[:].bitcast(I32), 0)
-        for tile in scale_tiles:
+        for tile in a_scales:
             nc.vector.memset(tile[:].bitcast(I32), 0)
         make_identity(nc, ident[:])
 
@@ -82,12 +82,12 @@ def tile_prompt_map_edit_s13_kernel(tc, text, wv_bytes, wv_scale, reweight, attn
         def load_text(t):
             nc.sync.dma_start(out=text_sb[t][:], in_=text_rows[:, t, :])
 
-        def load_scales(i):
-            heads = scale_groups[i]
-            rows = attn_scales[heads.start : heads.stop].bitcast(I32).rearrange("h (q r) n -> r q h n", r=4)
-            dst = scale_tiles[i][:].bitcast(I32).rearrange("p (h n) -> p h n", h=len(heads))
-            for r in range(4):
-                nc.sync.dma_start(out=dst[r:P:32], in_=rows[r])
+        def spread_scales(h, rs):
+            for r in rs:
+                nc.sync.dma_start(
+                    out=a_scales[h][:].bitcast(I32)[r:P:32, :],
+                    in_=rows_sorted[:].bitcast(I32)[ROWS * h + r : ROWS * (h + 1) : 4, :],
+                )
 
         def load_words(h):
             nc.sync.dma_start(out=a_words[h][:], in_=attn_words[h])
@@ -95,64 +95,69 @@ def tile_prompt_map_edit_s13_kernel(tc, text, wv_bytes, wv_scale, reweight, attn
         nc.scalar.dma_start(out=wscale[:, :, 0:4], in_=wv_scale.rearrange("(g p t) o -> p g (t o)", p=P, t=4))
         nc.scalar.dma_start(out=rw[:], in_=reweight.rearrange("(p t) -> p t", t=4))
         nc.scalar.copy(out=rw_walk[:], in_=rw[:].unsqueeze(1).unsqueeze(3).to_broadcast([P, C // 2, 4, 2]))
+        nc.sync.dma_start(out=rows_raw[:], in_=attn_scales.rearrange("h q n -> (h q) n"))
+        nc.vector.tensor_copy(
+            out=rows_sorted[:].rearrange("p (i s m) -> p i s m", s=RUN, m=P),
+            in_=rows_raw[:].rearrange("p (i m s) -> p i s m", s=RUN, m=P),
+        )
         load_wv(0)
         load_text(0)
+        nc.sync.dma_start(out=rn_rows[0:BANKS, :], in_=renorm.rearrange("h (i n) -> (h i) n", n=BANK))
         load_wv(1)
-        nc.sync.dma_start(out=rn_rows[0:STEPS, :], in_=renorm.rearrange("h (k n) -> (h k) n", k=2))
-        for t in range(1, 4):
-            load_text(t)
+        load_text(1)
         load_wv(2)
+        load_text(2)
+        load_text(3)
         load_wv(3)
-        load_words(0)
-        load_scales(0)
-        for h in range(1, H):
+        for h in range(H):
             load_words(h)
+            if h < SPREAD_AHEAD:
+                spread_scales(h, range(4))
 
         text_gr = {}
         wide = {}
+        wide_tiles = {}
         grouped = {}
         v_ps = {}
         v_passes = {}
         u_gr = {}
-        z_ps = {}
-        z_sb = {}
+        a_sorted = {}
         y_ps = {}
         y_sb = {}
 
-        def text_turn(t):
+        def text_turn(t, gp):
             words = text_sb[t][:].bitcast(F32)
-            gr = work.tile([P, E], BF16, name="text_gr", align_bytes=64, bufs=4)
-            text_gr[t] = gr
-            for gp in range(2):
-                if gp == 0:
-                    bank = psum_z.tile([P, 4, P], F32, name="z_bank")
-                else:
-                    bank = psum_y.tile([P, 4, P], F32, name="y_bank")
-                for gg in range(2):
-                    g = 2 * gp + gg
-                    for u in range(2):
-                        nc.tensor.transpose(bank[:, 2 * gg + u, :], words[:, 2 * P * g + u : 2 * P * (g + 1) : 2], ident[:])
-                nc.scalar.copy(
-                    out=gr[:, 2 * PASS * gp : 2 * PASS * (gp + 1)].bitcast(F32).rearrange("p (g m u) -> p g m u", g=2, u=2),
-                    in_=bank[:].rearrange("p (g u) m -> p g m u", u=2),
-                )
+            if gp == 0:
+                text_gr[t] = work.tile([P, E], BF16, name="text_gr", align_bytes=64, bufs=4)
+            bank = psum_y.tile([P, 4, P], F32, name="y_bank")
+            for gg in range(2):
+                g = 2 * gp + gg
+                for u in range(2):
+                    nc.tensor.transpose(bank[:, 2 * gg + u, :], words[:, 2 * P * g + u : 2 * P * (g + 1) : 2], ident[:])
+            nc.scalar.copy(
+                out=text_gr[t][:, 2 * PASS * gp : 2 * PASS * (gp + 1)].bitcast(F32).rearrange("p (g m u) -> p g m u", g=2, u=2),
+                in_=bank[:].rearrange("p (g u) m -> p g m u", u=2),
+            )
 
-        def turn_renorm(ps, turned, slots):
-            for s in slots:
-                cols = rn_rows[:, s:HALF:RUN] if turned else rn_rows[:, P * s : P * (s + 1)]
-                nc.tensor.matmul(ps[:, turned, s, :], lhsT=cols, rhs=pick[:], start=True, stop=True)
+        def turn_renorm():
+            ps = psum_y.tile([P, RUN, BANKS], F32, name="y_bank")
+            for s in range(RUN):
+                nc.tensor.matmul(ps[:, s, :], lhsT=rn_rows[:, s:BANK:RUN], rhs=pick[:], start=True, stop=True)
+            nc.scalar.copy(out=rn[:], in_=ps[:].rearrange("p s i -> p i s"))
 
         def text_quant(t):
             nc.vector.quantize_mx(out=text_codes[t][:].bitcast(E4X4), scales=text_scales[t][:], in_=text_gr[t][:])
 
-        def widen(pairs, g, engines):
-            w = work.tile([P, 4, PAIR * len(pairs)], BF16, name="wide%d" % len(pairs), bufs=8 if len(pairs) == 1 else 2)
-            for b in pairs:
-                wide[(b, g)] = w[:, :, PAIR * (b - pairs.start) : PAIR * (b - pairs.start + 1)]
-            for t in range(4):
+        def widen(pairs, g, ts, on_scalar):
+            if (pairs.start, g) not in wide_tiles:
+                w = work.tile([P, 4, PAIR * len(pairs)], BF16, name="wide%d" % len(pairs), bufs=G)
+                wide_tiles[(pairs.start, g)] = w
+                for b in pairs:
+                    wide[(b, g)] = w[:, :, PAIR * (b - pairs.start) : PAIR * (b - pairs.start + 1)]
+            for t in ts:
                 src = wv_raw[g][:, D * t + PAIR * pairs.start : D * t + PAIR * pairs.stop].bitcast(FP8)
-                dst = w[:, t, :]
-                if engines[t] == "s":
+                dst = wide_tiles[(pairs.start, g)][:, t, :]
+                if on_scalar:
                     nc.scalar.activation(out=dst, in_=src, func=COPY, scale=wscale[:, g, t : t + 1])
                 else:
                     nc.vector.tensor_scalar(out=dst, in0=src, scalar1=wscale[:, g, t : t + 1], scalar2=None, op0=MULT)
@@ -170,10 +175,7 @@ def tile_prompt_map_edit_s13_kernel(tc, text, wv_bytes, wv_scale, reweight, attn
 
         def values(h, gs, ts):
             if h not in v_ps:
-                if h // 2 == 1:
-                    v_ps[h] = psum_y.tile([P, 4, C], F32, name="y_bank")
-                else:
-                    v_ps[h] = psum_v.tile([P, 4, C], F32, name="v_bank")
+                v_ps[h] = psum_v.tile([P, 4, C], F32, name="v_bank")
                 v_passes[h] = 0
             b, c0 = h // 2, C * (h % 2)
             for g in gs:
@@ -202,193 +204,136 @@ def tile_prompt_map_edit_s13_kernel(tc, text, wv_bytes, wv_scale, reweight, attn
         def u_quant(h):
             nc.vector.quantize_mx(out=u_codes[h][:].bitcast(E4X4), scales=u_scales[h][:], in_=u_gr[h][:])
 
-        def mix_turned(n, q):
+        def sort_words(n):
             h, k = divmod(n, 2)
-            ps = psum_z.tile([P, BANK], F32, name="z_bank")
-            z_ps[(n, q)] = ps
-            i0 = HALF * k + BANK * q
-            nc.tensor.matmul_mx(
-                out=ps[:],
-                lhsT=u_codes[h][:].bitcast(E4X4),
-                lhsT_scale=u_scales[h][:],
-                rhs=a_words[h][:, 2 * i0 : 2 * (i0 + BANK)].bitcast(F4X4),
-                rhs_scale=a_scales[h][:, i0 : i0 + BANK],
-                start=True,
-                stop=True,
-            )
+            a_sorted[n] = work.tile([P, 2 * HALF], U8, name="a_sorted", align_bytes=64, bufs=5)
+            src = a_words[h][:, 2 * HALF * k : 2 * HALF * (k + 1)].bitcast(U16).rearrange("p (q m s) -> p q s m", q=2, s=RUN)
+            dst = a_sorted[n][:].bitcast(U16).rearrange("p (q s m) -> p q s m", q=2, s=RUN)
+            if n in SORTED_BY_SCALAR:
+                nc.scalar.copy(out=dst, in_=src)
+            else:
+                nc.vector.tensor_copy(out=dst, in_=src)
 
-        def mix_direct(n, q):
+        def mix(n, q):
             h, k = divmod(n, 2)
-            ps = psum_z.tile([P, 4, C], F32, name="z_bank")
+            ps = psum_y.tile([P, RUN, C], F32, name="y_bank")
             y_ps[(n, q)] = ps
-            for j in range(4):
-                i0 = HALF * k + P * (4 * q + j)
+            for s in range(RUN):
+                i0 = BANK * q + P * s
                 nc.tensor.matmul_mx(
-                    out=ps[:, j, :],
-                    lhsT=a_words[h][:, 2 * i0 : 2 * (i0 + P)].bitcast(F4X4),
-                    lhsT_scale=a_scales[h][:, i0 : i0 + P],
+                    out=ps[:, s, :],
+                    lhsT=a_sorted[n][:, 2 * i0 : 2 * (i0 + P)].bitcast(F4X4),
+                    lhsT_scale=a_scales[h][:, HALF * k + i0 : HALF * k + i0 + P],
                     rhs=u_codes[h][:].bitcast(E4X4),
                     rhs_scale=u_scales[h][:],
                     start=True,
                     stop=True,
                 )
 
-        def regroup(n, q, on_scalar):
-            if q == 0:
-                z_sb[n] = work.tile([P, RUN, P], F32, name="z_sb")
-            dst = z_sb[n][:, :, P // 2 * q : P // 2 * (q + 1)]
-            src = z_ps[(n, q)][:].rearrange("c (p s) -> c s p", s=RUN)
-            if on_scalar:
-                nc.scalar.copy(out=dst, in_=src)
-            else:
-                nc.vector.tensor_copy(out=dst, in_=src)
-
-        def turn(n, values_done):
-            for q in range(2):
-                if q == 1 and values_done:
-                    ps = psum_v.tile([P, 4, C], F32, name="v_bank")
-                else:
-                    ps = psum_y.tile([P, 4, C], F32, name="y_bank")
-                y_ps[(n, q)] = ps
-                for j in range(4):
-                    nc.tensor.transpose(ps[:, j, :], z_sb[n][:, 4 * q + j, :], ident[:])
-
         def y_evict(n, q, on_scalar):
             if n not in y_sb:
-                y_sb[n] = work.tile([P, RUN, C], F32, name="y_sb", bufs=10)
+                y_sb[n] = work.tile([P, 2, RUN, C], F32, name="y_sb", bufs=10)
             ps = y_ps[(n, q)]
-            fac = rn[:, 0 if n in DIRECT else 1, n, :]
+            fac = rn[:, 2 * n + q, :]
             if on_scalar:
-                for j in range(4):
-                    s = 4 * q + j
-                    nc.scalar.activation(out=y_sb[n][:, s, :], in_=ps[:, j, :], func=COPY, scale=fac[:, s : s + 1])
+                for s in range(RUN):
+                    nc.scalar.activation(out=y_sb[n][:, q, s, :], in_=ps[:, s, :], func=COPY, scale=fac[:, s : s + 1])
             else:
-                nc.vector.tensor_tensor(
-                    out=y_sb[n][:, 4 * q : 4 * q + 4, :],
-                    in0=ps[:],
-                    in1=fac[:, 4 * q : 4 * q + 4].unsqueeze(2).to_broadcast([P, 4, C]),
-                    op=MULT,
-                )
+                nc.vector.tensor_tensor(out=y_sb[n][:, q], in0=ps[:], in1=fac.unsqueeze(2).to_broadcast([P, RUN, C]), op=MULT)
 
-        def store(n, s0, s1):
+        def store(n, q0, q1):
             h, k = divmod(n, 2)
-            if n in DIRECT:
-                dst = out[h].rearrange("(k s p) c -> p k s c", k=2, s=RUN)[:, k]
-            else:
-                dst = out[h].rearrange("(k p s) c -> p k s c", k=2, s=RUN)[:, k]
-            nc.sync.dma_start(out=dst[:, s0:s1, :], in_=y_sb[n][:, s0:s1, :])
-            if n + 1 < len(scale_groups):
-                load_scales(n + 1)
+            dst = out[h].rearrange("(k q p s) c -> p k q (s c)", k=2, q=2, s=RUN)[:, k]
+            nc.sync.dma_start(out=dst[:, q0:q1, :], in_=y_sb[n][:].rearrange("p q s c -> p q (s c)")[:, q0:q1, :])
+            if h + SPREAD_AHEAD < H:
+                spread_scales(h + SPREAD_AHEAD, range(2 * k, 2 * k + 2))
 
         def one(b):
             return range(b, b + 1)
 
-        later = [(b, g) for b in range(1, PAIRS) for g in range(G)][1:]
-        nc.vector.tensor_copy(out=pick[:], in_=ident[:, 0:STEPS])
-        widen(range(0, 2), 0, "vsvs")
-        widen(one(2), 0, "vvvs")
+        nc.vector.tensor_copy(out=pick[:], in_=ident[:, 0:BANKS])
+        mid = range(1, 3)
+        widen(one(0), 0, range(4), False)
+        widen(mid, 0, range(4), True)
+        widen(one(3), 0, range(4), False)
         interleave(0, 0)
-        text_turn(0)
-        interleave(1, 0)
+        text_turn(0, 0)
+        widen(mid, 1, one(0), True)
+        text_turn(0, 1)
+        turn_renorm()
+        widen(mid, 1, one(1), True)
+        widen(one(0), 1, range(4), False)
         wv_quant(0, 0)
-        widen(range(0, 2), 1, "vvvs")
+        interleave(1, 0)
+        interleave(0, 1)
         wv_quant(1, 0)
         text_quant(0)
-        text_turn(1)
-        interleave(0, 1)
-        text_turn(2)
-        text_quant(1)
         wv_quant(0, 1)
-        text_turn(3)
-        rn_ps = psum_y.tile([P, 2, RUN, STEPS], F32, name="y_bank")
-        turn_renorm(rn_ps, 1, range(RUN // 2))
-        widen(one(0), 2, "vvvv")
-        text_quant(2)
-        for h in range(2):
-            values(h, range(2), range(3))
+        text_turn(1, 0)
+        widen(mid, 1, one(2), True)
+        text_turn(1, 1)
+        widen(mid, 1, one(3), True)
+        widen(one(0), 2, range(4), False)
+        interleave(2, 0)
         interleave(0, 2)
-        widen(one(0), 3, "vvss")
+        wv_quant(2, 0)
+        text_quant(1)
         wv_quant(0, 2)
+        text_turn(2, 0)
+        widen(mid, 2, one(0), True)
+        text_turn(2, 1)
+        text_turn(3, 0)
+        text_turn(3, 1)
+        for h in range(2):
+            values(h, range(3), range(2))
+        widen(mid, 2, range(1, 4), True)
+        widen(mid, 3, range(4), True)
+        widen(one(0), 3, range(4), False)
+        text_quant(2)
         interleave(0, 3)
-        text_quant(3)
-        for b, g in later[:WIDENED_AHEAD]:
-            if (b, g) not in wide:
-                widen(one(b), g, "ssss")
-        for h in range(2):
-            values(h, range(2, 3), range(3))
+        sort_words(0)
         wv_quant(0, 3)
+        text_quant(3)
         for h in range(2):
-            values(h, range(3), range(3, 4))
-            values(h, range(3, 4), range(4))
-        turn_renorm(rn_ps, 0, range(RUN))
-        turn_renorm(rn_ps, 1, range(RUN // 2, RUN))
-        nc.scalar.copy(out=rn[:], in_=rn_ps[:].rearrange("p d s n -> p d n s"))
-        interleave(*later[0])
+            values(h, one(3), range(2))
+            values(h, range(4), one(2))
+        for h in range(2):
+            values(h, range(4), one(3))
+        interleave(1, 1)
         u_evict(0)
-        wv_quant(*later[0])
+        wv_quant(1, 1)
         u_quant(0)
+        sort_words(1)
+        for h in range(2, 4):
+            values(h, one(0), range(4))
 
-        unit_step = {unit: max(0, j - UNITS_IN_STEP_0) for j, unit in enumerate(later)}
-        mult_step = {(1, g): g // 2 for g in range(G)}
-        mult_step.update({(2, g): unit_step[(2, g)] + 1 for g in range(G)})
-        mult_step.update({(3, g): max(unit_step[(3, g)] + 1, LAST_PAIR_FROM) for g in range(G)})
-        evict_step = {h: 2 * h - 1 if h < 4 else mult_step[(h // 2, G - 1)] + 1 for h in range(1, H)}
-        last_unit_step = unit_step[later[-1]]
-        last_evict_step = evict_step[H - 1]
-
-        pending = []
-        for n in range(STEPS + 1):
-            units = [j for j in range(1, len(later)) if unit_step[later[j]] == n]
-            ready = [h for h in range(1, H) if evict_step[h] == n]
-            direct = n in DIRECT
-            turned = not direct and n < STEPS
-            back = n >= 1 and n - 1 not in DIRECT
+        later = [(1, 2), (1, 3)] + [(b, g) for b in range(2, PAIRS) for g in range(G)][1:]
+        passes = [(1, 1), (1, 2), (1, 3), (2, 0)] + later[2:]
+        for n in range(STEPS):
+            unit = later[n] if n < len(later) else None
             for q in range(2):
-                if direct:
-                    mix_direct(n, q)
-                elif turned:
-                    mix_turned(n, q)
-            if turned:
-                regroup(n, 0, True)
-            if back:
-                turn(n - 1, n > last_evict_step)
-            if turned:
-                regroup(n, 1, n <= last_evict_step)
-            for h in ready:
-                u_evict(h)
-            for j in units:
-                interleave(*later[j])
-                spaced = bool(pending) or bool(ready)
-                for i in pending:
-                    wv_quant(*later[i])
-                pending.clear()
-                for h in ready:
-                    u_quant(h)
-                ready = []
-                if j + 1 < len(later) and later[j + 1] not in wide:
-                    widen(one(later[j + 1][0]), later[j + 1][1], "vvvv")
-                    spaced = True
-                if spaced:
-                    wv_quant(*later[j])
-                else:
-                    pending.append(j)
-            if not units:
-                for i in pending:
-                    wv_quant(*later[i])
-                pending.clear()
-            if back:
-                y_evict(n - 1, 0, True)
-                if n == STEPS:
-                    store(n - 1, 0, RUN // 2)
-                y_evict(n - 1, 1, n <= last_unit_step)
-                store(n - 1, RUN // 2 if n == STEPS else 0, RUN)
-            if direct:
-                y_evict(n, 0, True)
-                y_evict(n, 1, True)
-                store(n, 0, RUN)
-            for h in ready:
-                u_quant(h)
-            for (b, g), m in mult_step.items():
-                if m == n:
-                    values(2 * b, range(g, g + 1), range(4))
-                    values(2 * b + 1, range(g, g + 1), range(4))
+                mix(n, q)
+            for b, g in passes:
+                if (later.index((b, g)) + 1 if (b, g) in later else b - 1) == n:
+                    values(2 * b, one(g), range(4))
+                    values(2 * b + 1, one(g), range(4))
+            if unit:
+                interleave(*unit)
+            if n % 2 == 1 and n // 2 + 1 < H:
+                u_quant(n // 2 + 1)
+            if n + 2 < STEPS and n + 2 not in SORTED_BY_SCALAR:
+                sort_words(n + 2)
+            if n + 1 < len(later) and later[n + 1] not in wide:
+                widen(one(later[n + 1][0]), later[n + 1][1], range(4), False)
+            if unit:
+                wv_quant(*unit)
+            if n % 2 == 0 and n // 2 + 1 < H:
+                u_evict(n // 2 + 1)
+            last = n == STEPS - 1
+            y_evict(n, 0, True)
+            if last:
+                store(n, 0, 1)
+            y_evict(n, 1, n < VECTOR_EVICTS_FROM)
+            store(n, 1 if last else 0, 2)
+            if n + 3 < STEPS and n + 3 in SORTED_BY_SCALAR:
+                sort_words(n + 3)

@@ -33,7 +33,7 @@ PAIR = 2 * C
 
 SORTED_BY_SCALAR = range(3, 10, 2)
 VECTOR_EVICTS_FROM = 10
-SPREAD_AHEAD = 8
+SPREAD_AHEAD = 4
 
 
 def tile_prompt_map_edit_s13_kernel(tc, text, wv_bytes, wv_scale, reweight, attn_words, attn_scales, renorm, out):
@@ -97,8 +97,8 @@ def tile_prompt_map_edit_s13_kernel(tc, text, wv_bytes, wv_scale, reweight, attn
         nc.scalar.copy(out=rw_walk[:], in_=rw[:].unsqueeze(1).unsqueeze(3).to_broadcast([P, C // 2, 4, 2]))
         nc.sync.dma_start(out=rows_raw[:], in_=attn_scales.rearrange("h q n -> (h q) n"))
         nc.vector.tensor_copy(
-            out=rows_sorted[:].rearrange("p (i s m) -> p i s m", s=RUN, m=P),
-            in_=rows_raw[:].rearrange("p (i m s) -> p i s m", s=RUN, m=P),
+            out=rows_sorted[:].rearrange("p (i s c m) -> p i c s m", s=RUN, c=P // 16, m=16),
+            in_=rows_raw[:].rearrange("p (i c m s) -> p i c s m", s=RUN, c=P // 16, m=16),
         )
         load_wv(0)
         load_text(0)
@@ -110,9 +110,8 @@ def tile_prompt_map_edit_s13_kernel(tc, text, wv_bytes, wv_scale, reweight, attn
         load_text(3)
         load_wv(3)
         for h in range(H):
+            spread_scales(h // 2, range(2 * (h % 2), 2 * (h % 2) + 2))
             load_words(h)
-            if h < SPREAD_AHEAD:
-                spread_scales(h, range(4))
 
         text_gr = {}
         wide = {}
@@ -207,8 +206,8 @@ def tile_prompt_map_edit_s13_kernel(tc, text, wv_bytes, wv_scale, reweight, attn
         def sort_words(n):
             h, k = divmod(n, 2)
             a_sorted[n] = work.tile([P, 2 * HALF], U8, name="a_sorted", align_bytes=64, bufs=5)
-            src = a_words[h][:, 2 * HALF * k : 2 * HALF * (k + 1)].bitcast(U16).rearrange("p (q m s) -> p q s m", q=2, s=RUN)
-            dst = a_sorted[n][:].bitcast(U16).rearrange("p (q s m) -> p q s m", q=2, s=RUN)
+            src = a_words[h][:, 2 * HALF * k : 2 * HALF * (k + 1)].bitcast(U16).rearrange("p (q c m s) -> p q c s m", q=2, s=RUN, m=8)
+            dst = a_sorted[n][:].bitcast(U16).rearrange("p (q s c m) -> p q c s m", q=2, s=RUN, m=8)
             if n in SORTED_BY_SCALAR:
                 nc.scalar.copy(out=dst, in_=src)
             else:

@@ -24,15 +24,16 @@ PASS = 4 * P
 G = E // PASS
 BANK = 512
 HALF = PIX // 2
-RUN = BANK // P
+SLOTS = BANK // P
+RUN = HALF // P
 STEPS = 2 * H
-BANKS = 2 * STEPS
 ROWS = 16
-PAIRS = H // 2
-PAIR = 2 * C
+UNIT = 2 * C
+FIRST_UNITS = [(range(0, 2), range(g, g + 1)) for g in range(G)]
+LATER_UNITS = [(range(h, h + 1), range(g, g + 2)) for h in range(2, H) for g in range(0, G, 2)]
 
-SORTED_BY_SCALAR = range(3, 10, 2)
-VECTOR_EVICTS_FROM = 10
+SORTED_BY_SCALAR = range(3, STEPS, 4)
+VECTOR_EVICTS_FROM = 13
 SPREAD_AHEAD = 4
 
 
@@ -41,27 +42,35 @@ def tile_prompt_map_edit_s13_kernel(tc, text, wv_bytes, wv_scale, reweight, attn
     with ExitStack() as ctx:
         keep = ctx.enter_context(tc.tile_pool(name="keep", bufs=1))
         work = ctx.enter_context(tc.tile_pool(name="work", bufs=3))
-        psum_v = ctx.enter_context(tc.psum_pool(name="psum_v", bufs=4))
-        psum_y = ctx.enter_context(tc.psum_pool(name="psum_y", bufs=4))
+        psum_v = ctx.enter_context(tc.psum_pool(name="psum_v", bufs=3))
+        psum_y = ctx.enter_context(tc.psum_pool(name="psum_y", bufs=5))
         ctx.enter_context(tc.manual_schedule())
 
         wscale = keep.tile([P, G, 8], F32, name="wscale")
         rw = keep.tile([P, 4], BF16, name="rw")
         rw_walk = keep.tile([P, C // 2, 4, 2], F32, name="rw_walk")
-        rn_rows = keep.tile([P, BANK], BF16, name="rn_rows")
-        rn = keep.tile([P, BANKS, RUN], F32, name="rn")
+        rn_rows = keep.tile([P, HALF], BF16, name="rn_rows")
+        rn = keep.tile([P, STEPS, RUN], F32, name="rn")
         ident = keep.tile([P, P], F32, name="ident")
-        pick = keep.tile([P, BANKS], BF16, name="pick")
+        pick = keep.tile([P, STEPS], BF16, name="pick")
         wv_raw = [keep.tile([P, 4 * D], U8, name="wv_raw%d" % g) for g in range(G)]
         text_sb = [keep.tile([P, E], BF16, name="text_sb%d" % t) for t in range(4)]
         text_codes = [keep.tile([P, E // 4], U32, name="text_codes%d" % t, align_bytes=64) for t in range(4)]
         text_scales = [keep.tile([P, E // 4], U8, name="text_scales%d" % t, align_bytes=64) for t in range(4)]
         wv_codes = {}
         wv_scales = {}
-        for b in range(PAIRS):
-            for g in range(G):
-                wv_codes[(b, g)] = keep.tile([P, PAIR], U32, name="wv_codes%d%d" % (b, g), align_bytes=64)
-                wv_scales[(b, g)] = keep.tile([P, PAIR], U8, name="wv_scales%d%d" % (b, g), align_bytes=64)
+        wv_at = {}
+        for u in FIRST_UNITS + LATER_UNITS:
+            wv_codes[u] = keep.tile([P, UNIT], U32, name="wv_codes%d%d%d" % (u[0].start, u[1].start, len(u[0])), align_bytes=64)
+            wv_scales[u] = keep.tile([P, UNIT], U8, name="wv_scales%d%d%d" % (u[0].start, u[1].start, len(u[0])), align_bytes=64)
+            for i, (g, h) in enumerate((g, h) for g in u[1] for h in u[0]):
+                wv_at[(h, g)] = (u, C * i)
+        wide = {}
+        for heads, span in ((range(0, 2), 1), (range(2, 6), 2), (range(6, 8), 2)):
+            for g0 in range(0, G, span):
+                w = keep.tile([P, span, 4, C * len(heads)], BF16, name="wide%d%d" % (heads.start, g0))
+                for g in range(g0, g0 + span):
+                    wide[(heads.start, g)] = (w, g - g0)
         a_words = [keep.tile([P, 2 * PIX], U8, name="a_words%d" % h) for h in range(H)]
         rows_raw = keep.tile([P, PIX], U8, name="rows_raw")
         rows_sorted = keep.tile([P, PIX], U8, name="rows_sorted")
@@ -96,13 +105,14 @@ def tile_prompt_map_edit_s13_kernel(tc, text, wv_bytes, wv_scale, reweight, attn
         nc.scalar.dma_start(out=rw[:], in_=reweight.rearrange("(p t) -> p t", t=4))
         nc.scalar.copy(out=rw_walk[:], in_=rw[:].unsqueeze(1).unsqueeze(3).to_broadcast([P, C // 2, 4, 2]))
         nc.sync.dma_start(out=rows_raw[:], in_=attn_scales.rearrange("h q n -> (h q) n"))
+        nc.sync.dma_start(out=rn_rows[0:STEPS, :], in_=renorm.rearrange("h (k n) -> (h k) n", k=2))
+        nc.vector.tensor_copy(out=pick[:], in_=ident[:, 0:STEPS])
         nc.vector.tensor_copy(
-            out=rows_sorted[:].rearrange("p (i s c m) -> p i c s m", s=RUN, c=P // 16, m=16),
-            in_=rows_raw[:].rearrange("p (i c m s) -> p i c s m", s=RUN, c=P // 16, m=16),
+            out=rows_sorted[:].rearrange("p (k q s m) -> p k q m s", k=2, q=2, s=SLOTS),
+            in_=rows_raw[:].rearrange("p (k m q s) -> p k q m s", k=2, q=2, s=SLOTS),
         )
         load_wv(0)
         load_text(0)
-        nc.sync.dma_start(out=rn_rows[0:BANKS, :], in_=renorm.rearrange("h (i n) -> (h i) n", n=BANK))
         load_wv(1)
         load_text(1)
         load_wv(2)
@@ -114,8 +124,6 @@ def tile_prompt_map_edit_s13_kernel(tc, text, wv_bytes, wv_scale, reweight, attn
             load_words(h)
 
         text_gr = {}
-        wide = {}
-        wide_tiles = {}
         grouped = {}
         v_ps = {}
         v_passes = {}
@@ -139,53 +147,50 @@ def tile_prompt_map_edit_s13_kernel(tc, text, wv_bytes, wv_scale, reweight, attn
             )
 
         def turn_renorm():
-            ps = psum_y.tile([P, RUN, BANKS], F32, name="y_bank")
-            for s in range(RUN):
-                nc.tensor.matmul(ps[:, s, :], lhsT=rn_rows[:, s:BANK:RUN], rhs=pick[:], start=True, stop=True)
-            nc.scalar.copy(out=rn[:], in_=ps[:].rearrange("p s i -> p i s"))
+            ps = psum_v.tile([P, RUN, STEPS], F32, name="v_bank")
+            for j in range(RUN):
+                nc.tensor.matmul(ps[:, j, :], lhsT=rn_rows[:, j:HALF:RUN], rhs=pick[:], start=True, stop=True)
+            return ps
 
         def text_quant(t):
             nc.vector.quantize_mx(out=text_codes[t][:].bitcast(E4X4), scales=text_scales[t][:], in_=text_gr[t][:])
 
-        def widen(pairs, g, ts, on_scalar):
-            if (pairs.start, g) not in wide_tiles:
-                w = work.tile([P, 4, PAIR * len(pairs)], BF16, name="wide%d" % len(pairs), bufs=G)
-                wide_tiles[(pairs.start, g)] = w
-                for b in pairs:
-                    wide[(b, g)] = w[:, :, PAIR * (b - pairs.start) : PAIR * (b - pairs.start + 1)]
+        def widen(heads, g, ts, on_scalar):
+            w, gi = wide[(heads.start, g)]
             for t in ts:
-                src = wv_raw[g][:, D * t + PAIR * pairs.start : D * t + PAIR * pairs.stop].bitcast(FP8)
-                dst = wide_tiles[(pairs.start, g)][:, t, :]
+                src = wv_raw[g][:, D * t + C * heads.start : D * t + C * heads.stop].bitcast(FP8)
                 if on_scalar:
-                    nc.scalar.activation(out=dst, in_=src, func=COPY, scale=wscale[:, g, t : t + 1])
+                    nc.scalar.activation(out=w[:, gi, t, :], in_=src, func=COPY, scale=wscale[:, g, t : t + 1])
                 else:
-                    nc.vector.tensor_scalar(out=dst, in0=src, scalar1=wscale[:, g, t : t + 1], scalar2=None, op0=MULT)
+                    nc.vector.tensor_scalar(out=w[:, gi, t, :], in0=src, scalar1=wscale[:, g, t : t + 1], scalar2=None, op0=MULT)
 
-        def interleave(b, g):
-            gr = work.tile([P, 4 * PAIR], BF16, name="grouped", align_bytes=64)
-            grouped[(b, g)] = gr
+        def interleave(u):
+            heads, gs = u
+            first = max(h for h in (0, 2, 6) if h <= heads.start)
+            planes = wide[(first, gs.start)][0][:, :, :, C * (heads.start - first) : C * (heads.stop - first)]
+            grouped[u] = work.tile([P, 4 * UNIT], BF16, name="grouped", align_bytes=64)
             nc.vector.tensor_copy(
-                out=gr[:].rearrange("p (c i t) -> p c t i", i=4, t=4),
-                in_=wide[(b, g)].rearrange("p t (c i) -> p c t i", i=4),
+                out=grouped[u][:].rearrange("p (g c i t) -> p g c t i", g=len(gs), i=4, t=4),
+                in_=planes.rearrange("p g t (c i) -> p g c t i", i=4),
             )
 
-        def wv_quant(b, g):
-            nc.vector.quantize_mx(out=wv_codes[(b, g)][:].bitcast(E4X4), scales=wv_scales[(b, g)][:], in_=grouped[(b, g)][:])
+        def wv_quant(u):
+            nc.vector.quantize_mx(out=wv_codes[u][:].bitcast(E4X4), scales=wv_scales[u][:], in_=grouped[u][:])
 
         def values(h, gs, ts):
             if h not in v_ps:
                 v_ps[h] = psum_v.tile([P, 4, C], F32, name="v_bank")
                 v_passes[h] = 0
-            b, c0 = h // 2, C * (h % 2)
             for g in gs:
+                u, c0 = wv_at[(h, g)]
                 for t in ts:
                     v_passes[h] = v_passes[h] + 1
                     nc.tensor.matmul_mx(
                         out=v_ps[h][:, t, :],
                         lhsT=text_codes[t][:, P * g : P * (g + 1)].bitcast(E4X4),
                         lhsT_scale=text_scales[t][:, P * g : P * (g + 1)],
-                        rhs=wv_codes[(b, g)][:, c0 : c0 + C].bitcast(E4X4),
-                        rhs_scale=wv_scales[(b, g)][:, c0 : c0 + C],
+                        rhs=wv_codes[u][:, c0 : c0 + C].bitcast(E4X4),
+                        rhs_scale=wv_scales[u][:, c0 : c0 + C],
                         start=(v_passes[h] == 1),
                         stop=(v_passes[h] == 4 * G),
                     )
@@ -206,8 +211,8 @@ def tile_prompt_map_edit_s13_kernel(tc, text, wv_bytes, wv_scale, reweight, attn
         def sort_words(n):
             h, k = divmod(n, 2)
             a_sorted[n] = work.tile([P, 2 * HALF], U8, name="a_sorted", align_bytes=64, bufs=5)
-            src = a_words[h][:, 2 * HALF * k : 2 * HALF * (k + 1)].bitcast(U16).rearrange("p (q c m s) -> p q c s m", q=2, s=RUN, m=8)
-            dst = a_sorted[n][:].bitcast(U16).rearrange("p (q s c m) -> p q c s m", q=2, s=RUN, m=8)
+            src = a_words[h][:, 2 * HALF * k : 2 * HALF * (k + 1)].bitcast(U16).rearrange("p (m q s) -> p q m s", q=2, s=SLOTS)
+            dst = a_sorted[n][:].bitcast(U16).rearrange("p (q s m) -> p q m s", q=2, s=SLOTS)
             if n in SORTED_BY_SCALAR:
                 nc.scalar.copy(out=dst, in_=src)
             else:
@@ -215,9 +220,9 @@ def tile_prompt_map_edit_s13_kernel(tc, text, wv_bytes, wv_scale, reweight, attn
 
         def mix(n, q):
             h, k = divmod(n, 2)
-            ps = psum_y.tile([P, RUN, C], F32, name="y_bank")
+            ps = psum_y.tile([P, SLOTS, C], F32, name="y_bank")
             y_ps[(n, q)] = ps
-            for s in range(RUN):
+            for s in range(SLOTS):
                 i0 = BANK * q + P * s
                 nc.tensor.matmul_mx(
                     out=ps[:, s, :],
@@ -231,18 +236,18 @@ def tile_prompt_map_edit_s13_kernel(tc, text, wv_bytes, wv_scale, reweight, attn
 
         def y_evict(n, q, on_scalar):
             if n not in y_sb:
-                y_sb[n] = work.tile([P, 2, RUN, C], F32, name="y_sb", bufs=10)
+                y_sb[n] = work.tile([P, 2, SLOTS, C], F32, name="y_sb", bufs=10)
             ps = y_ps[(n, q)]
-            fac = rn[:, 2 * n + q, :]
+            fac = rn[:, n, SLOTS * q : SLOTS * (q + 1)]
             if on_scalar:
-                for s in range(RUN):
+                for s in range(SLOTS):
                     nc.scalar.activation(out=y_sb[n][:, q, s, :], in_=ps[:, s, :], func=COPY, scale=fac[:, s : s + 1])
             else:
-                nc.vector.tensor_tensor(out=y_sb[n][:, q], in0=ps[:], in1=fac.unsqueeze(2).to_broadcast([P, RUN, C]), op=MULT)
+                nc.vector.tensor_tensor(out=y_sb[n][:, q], in0=ps[:], in1=fac.unsqueeze(2).to_broadcast([P, SLOTS, C]), op=MULT)
 
         def store(n, q0, q1):
             h, k = divmod(n, 2)
-            dst = out[h].rearrange("(k q p s) c -> p k q (s c)", k=2, q=2, s=RUN)[:, k]
+            dst = out[h].rearrange("(k p q s) c -> p k q (s c)", k=2, q=2, s=SLOTS)[:, k]
             nc.sync.dma_start(out=dst[:, q0:q1, :], in_=y_sb[n][:].rearrange("p q s c -> p q (s c)")[:, q0:q1, :])
             if h + SPREAD_AHEAD < H:
                 spread_scales(h + SPREAD_AHEAD, range(2 * k, 2 * k + 2))
@@ -250,84 +255,75 @@ def tile_prompt_map_edit_s13_kernel(tc, text, wv_bytes, wv_scale, reweight, attn
         def one(b):
             return range(b, b + 1)
 
-        nc.vector.tensor_copy(out=pick[:], in_=ident[:, 0:BANKS])
-        mid = range(1, 3)
-        widen(one(0), 0, range(4), False)
+        low, mid, high = range(0, 2), range(2, 6), range(6, 8)
+        first = FIRST_UNITS
+        rn_ps = turn_renorm()
+        widen(low, 0, range(4), False)
         widen(mid, 0, range(4), True)
-        widen(one(3), 0, range(4), False)
-        interleave(0, 0)
+        nc.scalar.copy(out=rn[:], in_=rn_ps[:].rearrange("p j n -> p n j"))
+        widen(high, 0, range(4), False)
+        interleave(first[0])
         text_turn(0, 0)
         widen(mid, 1, one(0), True)
         text_turn(0, 1)
-        turn_renorm()
-        widen(mid, 1, one(1), True)
-        widen(one(0), 1, range(4), False)
-        wv_quant(0, 0)
-        interleave(1, 0)
-        interleave(0, 1)
-        wv_quant(1, 0)
+        widen(mid, 1, range(1, 3), True)
+        widen(low, 1, range(4), False)
+        wv_quant(first[0])
+        widen(high, 1, range(4), False)
+        interleave(first[1])
         text_quant(0)
-        wv_quant(0, 1)
+        wv_quant(first[1])
         text_turn(1, 0)
-        widen(mid, 1, one(2), True)
-        text_turn(1, 1)
         widen(mid, 1, one(3), True)
-        widen(one(0), 2, range(4), False)
-        interleave(2, 0)
-        interleave(0, 2)
-        wv_quant(2, 0)
-        text_quant(1)
-        wv_quant(0, 2)
-        text_turn(2, 0)
+        text_turn(1, 1)
         widen(mid, 2, one(0), True)
-        text_turn(2, 1)
-        text_turn(3, 0)
-        text_turn(3, 1)
-        for h in range(2):
+        widen(low, 2, range(4), False)
+        widen(high, 2, range(4), False)
+        interleave(first[2])
+        text_quant(1)
+        wv_quant(first[2])
+        for t in range(2, 4):
+            text_turn(t, 0)
+            text_turn(t, 1)
+        for h in low:
             values(h, range(3), range(2))
         widen(mid, 2, range(1, 4), True)
         widen(mid, 3, range(4), True)
-        widen(one(0), 3, range(4), False)
+        widen(low, 3, range(4), False)
         text_quant(2)
-        interleave(0, 3)
-        sort_words(0)
-        wv_quant(0, 3)
+        interleave(first[3])
         text_quant(3)
-        for h in range(2):
-            values(h, one(3), range(2))
-            values(h, range(4), one(2))
-        for h in range(2):
-            values(h, range(4), one(3))
-        interleave(1, 1)
+        wv_quant(first[3])
+        for t in range(2, 4):
+            for h in low:
+                values(h, range(3), one(t))
+        for h in low:
+            values(h, one(3), range(4))
+        sort_words(0)
         u_evict(0)
-        wv_quant(1, 1)
-        u_quant(0)
         sort_words(1)
-        for h in range(2, 4):
-            values(h, one(0), range(4))
+        u_quant(0)
 
-        later = [(1, 2), (1, 3)] + [(b, g) for b in range(2, PAIRS) for g in range(G)][1:]
-        passes = [(1, 1), (1, 2), (1, 3), (2, 0)] + later[2:]
         for n in range(STEPS):
-            unit = later[n] if n < len(later) else None
+            unit = LATER_UNITS[n] if n < len(LATER_UNITS) else None
+            ready = n // 2 + 1 if n % 2 == 0 and n // 2 + 1 < H else None
             for q in range(2):
                 mix(n, q)
-            for b, g in passes:
-                if (later.index((b, g)) + 1 if (b, g) in later else b - 1) == n:
-                    values(2 * b, one(g), range(4))
-                    values(2 * b + 1, one(g), range(4))
+            if 1 <= n <= len(LATER_UNITS):
+                heads, gs = LATER_UNITS[n - 1]
+                values(heads.start, gs, range(4))
             if unit:
-                interleave(*unit)
-            if n % 2 == 1 and n // 2 + 1 < H:
-                u_quant(n // 2 + 1)
+                interleave(unit)
             if n + 2 < STEPS and n + 2 not in SORTED_BY_SCALAR:
                 sort_words(n + 2)
-            if n + 1 < len(later) and later[n + 1] not in wide:
-                widen(one(later[n + 1][0]), later[n + 1][1], range(4), False)
+            if ready:
+                u_evict(ready)
+            if n in (1, 5):
+                widen(high, 3, range(n // 2, n // 2 + 2), False)
             if unit:
-                wv_quant(*unit)
-            if n % 2 == 0 and n // 2 + 1 < H:
-                u_evict(n // 2 + 1)
+                wv_quant(unit)
+            if ready:
+                u_quant(ready)
             last = n == STEPS - 1
             y_evict(n, 0, True)
             if last:

@@ -34,6 +34,8 @@ LATER_UNITS = [(range(h, h + 1), range(g, g + 2)) for h in range(2, H) for g in 
 
 SORTED_BY_SCALAR = range(3, STEPS, 4)
 VECTOR_EVICTS_FROM = 13
+GROUPED = 4
+DIRECT = range(2)
 SPREAD_AHEAD = 4
 
 
@@ -65,21 +67,17 @@ def tile_prompt_map_edit_s13_kernel(tc, text, wv_bytes, wv_scale, reweight, attn
             wv_scales[u] = keep.tile([P, UNIT], U8, name="wv_scales%d%d%d" % (u[0].start, u[1].start, len(u[0])), align_bytes=64)
             for i, (g, h) in enumerate((g, h) for g in u[1] for h in u[0]):
                 wv_at[(h, g)] = (u, C * i)
-        wide = {}
-        for heads, span in ((range(0, 2), 1), (range(2, 6), 2), (range(6, 8), 2)):
-            for g0 in range(0, G, span):
-                w = keep.tile([P, span, 4, C * len(heads)], BF16, name="wide%d%d" % (heads.start, g0))
-                for g in range(g0, g0 + span):
-                    wide[(heads.start, g)] = (w, g - g0)
-        a_words = [keep.tile([P, 2 * PIX], U8, name="a_words%d" % h) for h in range(H)]
-        rows_raw = keep.tile([P, PIX], U8, name="rows_raw")
+        wide = [[keep.tile([P, 2, 4, D // 2], BF16, name="wide%d%d" % (half, gp)) for gp in range(2)] for half in range(2)]
+        a_words = [keep.tile([P, 2 * PIX], U8, name="a_words%d" % h, align_bytes=64) for h in range(H)]
+        rows_raw = keep.tile([P, PIX], U8, name="rows_raw", align_bytes=64)
         rows_sorted = keep.tile([P, PIX], U8, name="rows_sorted")
-        a_scales = [keep.tile([P, PIX], U8, name="a_scales%d" % h, align_bytes=64) for h in range(H)]
+        zeroed = [keep.tile([P, PIX], U8, name="a_scales%d" % i, align_bytes=64) for i in range(SPREAD_AHEAD - 1)]
+        a_scales = [(zeroed + [rows_raw])[h % SPREAD_AHEAD] for h in range(H)]
         u_codes = [keep.tile([P, C], U32, name="u_codes%d" % h, align_bytes=64) for h in range(H)]
         u_scales = [keep.tile([P, C], U8, name="u_scales%d" % h, align_bytes=64) for h in range(H)]
 
         nc.vector.memset(rn_rows[:].bitcast(I32), 0)
-        for tile in a_scales:
+        for tile in zeroed:
             nc.vector.memset(tile[:].bitcast(I32), 0)
         make_identity(nc, ident[:])
 
@@ -92,11 +90,9 @@ def tile_prompt_map_edit_s13_kernel(tc, text, wv_bytes, wv_scale, reweight, attn
             nc.sync.dma_start(out=text_sb[t][:], in_=text_rows[:, t, :])
 
         def spread_scales(h, rs):
+            rows = attn_scales[h].bitcast(I32) if 2 * h in DIRECT else rows_sorted[:].bitcast(I32)[ROWS * h : ROWS * (h + 1), :]
             for r in rs:
-                nc.sync.dma_start(
-                    out=a_scales[h][:].bitcast(I32)[r:P:32, :],
-                    in_=rows_sorted[:].bitcast(I32)[ROWS * h + r : ROWS * (h + 1) : 4, :],
-                )
+                nc.sync.dma_start(out=a_scales[h][:].bitcast(I32)[r:P:32, :], in_=rows[r:ROWS:4, :])
 
         def load_words(h):
             nc.sync.dma_start(out=a_words[h][:], in_=attn_words[h])
@@ -132,6 +128,9 @@ def tile_prompt_map_edit_s13_kernel(tc, text, wv_bytes, wv_scale, reweight, attn
         y_ps = {}
         y_sb = {}
 
+        def one(i):
+            return range(i, i + 1)
+
         def text_turn(t, gp):
             words = text_sb[t][:].bitcast(F32)
             if gp == 0:
@@ -148,30 +147,35 @@ def tile_prompt_map_edit_s13_kernel(tc, text, wv_bytes, wv_scale, reweight, attn
 
         def turn_renorm():
             ps = psum_v.tile([P, RUN, STEPS], F32, name="v_bank")
+            d = len(DIRECT)
             for j in range(RUN):
-                nc.tensor.matmul(ps[:, j, :], lhsT=rn_rows[:, j:HALF:RUN], rhs=pick[:], start=True, stop=True)
+                nc.tensor.matmul(ps[:, j, d:], lhsT=rn_rows[:, j:HALF:RUN], rhs=pick[:, d:], start=True, stop=True)
+            for j in range(RUN):
+                nc.tensor.matmul(ps[:, j, 0:d], lhsT=rn_rows[:, P * j : P * (j + 1)], rhs=pick[:, 0:d], start=True, stop=True)
             return ps
 
         def text_quant(t):
             nc.vector.quantize_mx(out=text_codes[t][:].bitcast(E4X4), scales=text_scales[t][:], in_=text_gr[t][:])
 
+        def planes(heads, gs):
+            half, first = divmod(heads.start, H // 2)
+            g0 = gs.start % 2
+            return wide[half][gs.start // 2][:, g0 : g0 + len(gs), :, C * first : C * (first + len(heads))]
+
         def widen(heads, g, ts, on_scalar):
-            w, gi = wide[(heads.start, g)]
             for t in ts:
                 src = wv_raw[g][:, D * t + C * heads.start : D * t + C * heads.stop].bitcast(FP8)
+                dst = planes(heads, one(g))[:, 0, t, :]
                 if on_scalar:
-                    nc.scalar.activation(out=w[:, gi, t, :], in_=src, func=COPY, scale=wscale[:, g, t : t + 1])
+                    nc.scalar.activation(out=dst, in_=src, func=COPY, scale=wscale[:, g, t : t + 1])
                 else:
-                    nc.vector.tensor_scalar(out=w[:, gi, t, :], in0=src, scalar1=wscale[:, g, t : t + 1], scalar2=None, op0=MULT)
+                    nc.vector.tensor_scalar(out=dst, in0=src, scalar1=wscale[:, g, t : t + 1], scalar2=None, op0=MULT)
 
         def interleave(u):
-            heads, gs = u
-            first = max(h for h in (0, 2, 6) if h <= heads.start)
-            planes = wide[(first, gs.start)][0][:, :, :, C * (heads.start - first) : C * (heads.stop - first)]
-            grouped[u] = work.tile([P, 4 * UNIT], BF16, name="grouped", align_bytes=64)
+            grouped[u] = work.tile([P, 4 * UNIT], BF16, name="grouped", align_bytes=64, bufs=GROUPED)
             nc.vector.tensor_copy(
-                out=grouped[u][:].rearrange("p (g c i t) -> p g c t i", g=len(gs), i=4, t=4),
-                in_=planes.rearrange("p g t (c i) -> p g c t i", i=4),
+                out=grouped[u][:].rearrange("p (g c i t) -> p g c t i", g=len(u[1]), i=4, t=4),
+                in_=planes(*u).rearrange("p g t (c i) -> p g c t i", i=4),
             )
 
         def wv_quant(u):
@@ -222,11 +226,12 @@ def tile_prompt_map_edit_s13_kernel(tc, text, wv_bytes, wv_scale, reweight, attn
             h, k = divmod(n, 2)
             ps = psum_y.tile([P, SLOTS, C], F32, name="y_bank")
             y_ps[(n, q)] = ps
+            words = a_words[h][:, 2 * HALF * k : 2 * HALF * (k + 1)] if n in DIRECT else a_sorted[n][:]
             for s in range(SLOTS):
                 i0 = BANK * q + P * s
                 nc.tensor.matmul_mx(
                     out=ps[:, s, :],
-                    lhsT=a_sorted[n][:, 2 * i0 : 2 * (i0 + P)].bitcast(F4X4),
+                    lhsT=words[:, 2 * i0 : 2 * (i0 + P)].bitcast(F4X4),
                     lhsT_scale=a_scales[h][:, HALF * k + i0 : HALF * k + i0 + P],
                     rhs=u_codes[h][:].bitcast(E4X4),
                     rhs_scale=u_scales[h][:],
@@ -247,79 +252,76 @@ def tile_prompt_map_edit_s13_kernel(tc, text, wv_bytes, wv_scale, reweight, attn
 
         def store(n, q0, q1):
             h, k = divmod(n, 2)
-            dst = out[h].rearrange("(k p q s) c -> p k q (s c)", k=2, q=2, s=SLOTS)[:, k]
-            nc.sync.dma_start(out=dst[:, q0:q1, :], in_=y_sb[n][:].rearrange("p q s c -> p q (s c)")[:, q0:q1, :])
-            if h + SPREAD_AHEAD < H:
-                spread_scales(h + SPREAD_AHEAD, range(2 * k, 2 * k + 2))
+            pixels = "(k j p) c -> p k j c" if n in DIRECT else "(k p j) c -> p k j c"
+            dst = out[h].rearrange(pixels, k=2, j=RUN)[:, k, SLOTS * q0 : SLOTS * q1, :]
+            nc.sync.dma_start(out=dst, in_=y_sb[n][:].rearrange("p q s c -> p (q s) c")[:, SLOTS * q0 : SLOTS * q1, :])
+            done, part = divmod(n - 1, 2)
+            if 0 <= done < H - SPREAD_AHEAD:
+                spread_scales(done + SPREAD_AHEAD, range(2 * part, 2 * part + 2))
 
-        def one(b):
-            return range(b, b + 1)
-
-        low, mid, high = range(0, 2), range(2, 6), range(6, 8)
-        first = FIRST_UNITS
+        low, high = range(0, 4), range(4, 8)
+        first, later = FIRST_UNITS, LATER_UNITS
         rn_ps = turn_renorm()
-        widen(low, 0, range(4), False)
-        widen(mid, 0, range(4), True)
+        widen(range(0, 2), 0, range(4), False)
+        widen(high, 0, range(4), True)
         nc.scalar.copy(out=rn[:], in_=rn_ps[:].rearrange("p j n -> p n j"))
-        widen(high, 0, range(4), False)
+        widen(range(2, 4), 0, range(4), False)
         interleave(first[0])
         text_turn(0, 0)
-        widen(mid, 1, one(0), True)
+        widen(high, 1, one(0), True)
         text_turn(0, 1)
-        widen(mid, 1, range(1, 3), True)
+        widen(high, 1, range(1, 3), True)
         widen(low, 1, range(4), False)
         wv_quant(first[0])
-        widen(high, 1, range(4), False)
         interleave(first[1])
         text_quant(0)
-        wv_quant(first[1])
         text_turn(1, 0)
-        widen(mid, 1, one(3), True)
+        widen(high, 1, one(3), True)
         text_turn(1, 1)
-        widen(mid, 2, one(0), True)
+        widen(high, 2, one(0), True)
         widen(low, 2, range(4), False)
-        widen(high, 2, range(4), False)
+        wv_quant(first[1])
         interleave(first[2])
         text_quant(1)
         wv_quant(first[2])
         for t in range(2, 4):
             text_turn(t, 0)
             text_turn(t, 1)
-        for h in low:
+        for h in range(2):
             values(h, range(3), range(2))
-        widen(mid, 2, range(1, 4), True)
-        widen(mid, 3, range(4), True)
-        widen(low, 3, range(4), False)
+        widen(high, 2, range(1, 4), True)
+        widen(high, 3, range(4), True)
+        widen(range(0, 2), 3, range(4), False)
         text_quant(2)
         interleave(first[3])
         text_quant(3)
         wv_quant(first[3])
         for t in range(2, 4):
-            for h in low:
+            for h in range(2):
                 values(h, range(3), one(t))
-        for h in low:
+        for h in range(2):
             values(h, one(3), range(4))
-        sort_words(0)
+        interleave(later[0])
         u_evict(0)
-        sort_words(1)
+        wv_quant(later[0])
         u_quant(0)
 
         for n in range(STEPS):
-            unit = LATER_UNITS[n] if n < len(LATER_UNITS) else None
+            unit = later[n] if 1 <= n < len(later) else None
             ready = n // 2 + 1 if n % 2 == 0 and n // 2 + 1 < H else None
             for q in range(2):
                 mix(n, q)
-            if 1 <= n <= len(LATER_UNITS):
-                heads, gs = LATER_UNITS[n - 1]
+            if 1 <= n <= len(later):
+                heads, gs = later[n - 1]
                 values(heads.start, gs, range(4))
+            if n == 0:
+                widen(range(2, 4), 3, range(4), False)
             if unit:
                 interleave(unit)
             if n + 2 < STEPS and n + 2 not in SORTED_BY_SCALAR:
                 sort_words(n + 2)
             if ready:
                 u_evict(ready)
-            if n in (1, 5):
-                widen(high, 3, range(n // 2, n // 2 + 2), False)
             if unit:
                 wv_quant(unit)
             if ready:

@@ -104,8 +104,8 @@ def tile_prompt_map_edit_s13_kernel(tc, text, wv_bytes, wv_scale, reweight, attn
         nc.sync.dma_start(out=rn_rows[0:STEPS, :], in_=renorm.rearrange("h (k n) -> (h k) n", k=2))
         nc.vector.tensor_copy(out=pick[:], in_=ident[:, 0:STEPS])
         nc.vector.tensor_copy(
-            out=rows_sorted[:].rearrange("p (k q s m) -> p k q m s", k=2, q=2, s=SLOTS),
-            in_=rows_raw[:].rearrange("p (k m q s) -> p k q m s", k=2, q=2, s=SLOTS),
+            out=rows_sorted[:].rearrange("p (i s e m) -> p i s m e", s=2, e=2, m=P),
+            in_=rows_raw[:].rearrange("p (i m s e) -> p i s m e", s=2, e=2, m=P),
         )
         load_wv(0)
         load_text(0)
@@ -149,7 +149,7 @@ def tile_prompt_map_edit_s13_kernel(tc, text, wv_bytes, wv_scale, reweight, attn
             ps = psum_v.tile([P, RUN, STEPS], F32, name="v_bank")
             d = len(DIRECT)
             for j in range(RUN):
-                nc.tensor.matmul(ps[:, j, d:], lhsT=rn_rows[:, j:HALF:RUN], rhs=pick[:, d:], start=True, stop=True)
+                nc.tensor.matmul(ps[:, j, d:], lhsT=rn_rows[:, BANK * (j // SLOTS) + j % SLOTS : BANK * (j // SLOTS + 1) : SLOTS], rhs=pick[:, d:], start=True, stop=True)
             for j in range(RUN):
                 nc.tensor.matmul(ps[:, j, 0:d], lhsT=rn_rows[:, P * j : P * (j + 1)], rhs=pick[:, 0:d], start=True, stop=True)
             return ps
@@ -215,12 +215,18 @@ def tile_prompt_map_edit_s13_kernel(tc, text, wv_bytes, wv_scale, reweight, attn
         def sort_words(n):
             h, k = divmod(n, 2)
             a_sorted[n] = work.tile([P, 2 * HALF], U8, name="a_sorted", align_bytes=64, bufs=5)
-            src = a_words[h][:, 2 * HALF * k : 2 * HALF * (k + 1)].bitcast(U16).rearrange("p (m q s) -> p q m s", q=2, s=SLOTS)
-            dst = a_sorted[n][:].bitcast(U16).rearrange("p (q s m) -> p q m s", q=2, s=SLOTS)
+            src = a_words[h][:, 2 * HALF * k : 2 * HALF * (k + 1)].bitcast(U16)
+            dst = a_sorted[n][:].bitcast(U16)
             if n in SORTED_BY_SCALAR:
-                nc.scalar.copy(out=dst, in_=src)
+                nc.scalar.copy(
+                    out=dst.rearrange("p (q s m) -> p q m s", q=2, s=SLOTS),
+                    in_=src.rearrange("p (q m s) -> p q m s", q=2, s=SLOTS),
+                )
             else:
-                nc.vector.tensor_copy(out=dst, in_=src)
+                nc.vector.tensor_copy(
+                    out=dst.rearrange("p (q s e m) -> p q s m e", q=2, s=2, e=2),
+                    in_=src.rearrange("p (q m s e) -> p q s m e", q=2, s=2, e=2),
+                )
 
         def mix(n, q):
             h, k = divmod(n, 2)
@@ -252,9 +258,12 @@ def tile_prompt_map_edit_s13_kernel(tc, text, wv_bytes, wv_scale, reweight, attn
 
         def store(n, q0, q1):
             h, k = divmod(n, 2)
-            pixels = "(k j p) c -> p k j c" if n in DIRECT else "(k p j) c -> p k j c"
-            dst = out[h].rearrange(pixels, k=2, j=RUN)[:, k, SLOTS * q0 : SLOTS * q1, :]
-            nc.sync.dma_start(out=dst, in_=y_sb[n][:].rearrange("p q s c -> p (q s) c")[:, SLOTS * q0 : SLOTS * q1, :])
+            if n in DIRECT:
+                dst = out[h].rearrange("(k j p) c -> p k j c", k=2, j=RUN)[:, k, SLOTS * q0 : SLOTS * q1, :]
+                nc.sync.dma_start(out=dst, in_=y_sb[n][:].rearrange("p q s c -> p (q s) c")[:, SLOTS * q0 : SLOTS * q1, :])
+            else:
+                dst = out[h].rearrange("(k q p s) c -> p k q (s c)", k=2, q=2, s=SLOTS)[:, k, q0:q1, :]
+                nc.sync.dma_start(out=dst, in_=y_sb[n][:].rearrange("p q s c -> p q (s c)")[:, q0:q1, :])
             done, part = divmod(n - 1, 2)
             if 0 <= done < H - SPREAD_AHEAD:
                 spread_scales(done + SPREAD_AHEAD, range(2 * part, 2 * part + 2))

@@ -28,15 +28,13 @@ SLOTS = BANK // P
 RUN = HALF // P
 STEPS = 2 * H
 ROWS = 16
-UNIT = 2 * C
-FIRST_UNITS = [(range(0, 2), range(g, g + 1)) for g in range(G)]
-LATER_UNITS = [(range(h, h + 1), range(g, g + 2)) for h in range(2, H) for g in range(0, G, 2)]
+LOW = H // 2
 
-SORTED_BY_SCALAR = range(3, STEPS, 4)
+DIRECT_HEADS = 2
+DIRECT = range(2 * DIRECT_HEADS)
+SORTED_BY_SCALAR = range(2 * DIRECT_HEADS, 2 * DIRECT_HEADS + 2)
 VECTOR_EVICTS_FROM = 13
-GROUPED = 4
-DIRECT = range(2)
-SPREAD_AHEAD = 4
+SPREAD_AHEAD = 3
 
 
 def tile_prompt_map_edit_s13_kernel(tc, text, wv_bytes, wv_scale, reweight, attn_words, attn_scales, renorm, out):
@@ -49,6 +47,7 @@ def tile_prompt_map_edit_s13_kernel(tc, text, wv_bytes, wv_scale, reweight, attn
         ctx.enter_context(tc.manual_schedule())
 
         wscale = keep.tile([P, G, 8], F32, name="wscale")
+        scale_walk = [keep.tile([P, C, 4], F32, name="scale_walk%d" % g) for g in range(G)]
         rw = keep.tile([P, 4], BF16, name="rw")
         rw_walk = keep.tile([P, C // 2, 4, 2], F32, name="rw_walk")
         rn_rows = keep.tile([P, HALF], BF16, name="rn_rows")
@@ -59,26 +58,32 @@ def tile_prompt_map_edit_s13_kernel(tc, text, wv_bytes, wv_scale, reweight, attn
         text_sb = [keep.tile([P, E], BF16, name="text_sb%d" % t) for t in range(4)]
         text_codes = [keep.tile([P, E // 4], U32, name="text_codes%d" % t, align_bytes=64) for t in range(4)]
         text_scales = [keep.tile([P, E // 4], U8, name="text_scales%d" % t, align_bytes=64) for t in range(4)]
+        low_units = [(0, LOW, g, 1) for g in range(G - 1)] + [(0, 2, G - 1, 1), (2, 2, G - 1, 1)]
+        high_units = {h: (h, 1, 0, G) for h in range(LOW, H)}
         wv_codes = {}
         wv_scales = {}
         wv_at = {}
-        for u in FIRST_UNITS + LATER_UNITS:
-            wv_codes[u] = keep.tile([P, UNIT], U32, name="wv_codes%d%d%d" % (u[0].start, u[1].start, len(u[0])), align_bytes=64)
-            wv_scales[u] = keep.tile([P, UNIT], U8, name="wv_scales%d%d%d" % (u[0].start, u[1].start, len(u[0])), align_bytes=64)
-            for i, (g, h) in enumerate((g, h) for g in u[1] for h in u[0]):
-                wv_at[(h, g)] = (u, C * i)
-        wide = [[keep.tile([P, 2, 4, D // 2], BF16, name="wide%d%d" % (half, gp)) for gp in range(2)] for half in range(2)]
+        for u in low_units + list(high_units.values()):
+            h0, nh, g0, ng = u
+            wv_codes[u] = keep.tile([P, C * nh * ng], U32, name="wv_codes%d%d" % (h0, g0), align_bytes=64)
+            wv_scales[u] = keep.tile([P, C * nh * ng], U8, name="wv_scales%d%d" % (h0, g0), align_bytes=64)
+            for g in range(ng):
+                for h in range(nh):
+                    wv_at[(h0 + h, g0 + g)] = (u, C * (nh * g + h))
+        wide = keep.tile([P, G, 4, D // 2], BF16, name="wide")
         a_words = [keep.tile([P, 2 * PIX], U8, name="a_words%d" % h, align_bytes=64) for h in range(H)]
         rows_raw = keep.tile([P, PIX], U8, name="rows_raw", align_bytes=64)
         rows_sorted = keep.tile([P, PIX], U8, name="rows_sorted")
-        zeroed = [keep.tile([P, PIX], U8, name="a_scales%d" % i, align_bytes=64) for i in range(SPREAD_AHEAD - 1)]
-        a_scales = [(zeroed + [rows_raw])[h % SPREAD_AHEAD] for h in range(H)]
+        direct_planes = keep.tile([P, DIRECT_HEADS * PIX], U8, name="direct_planes", align_bytes=64)
+        spare_plane = keep.tile([P, PIX], U8, name="spare_plane", align_bytes=64)
+        a_scales = [direct_planes[:, PIX * h : PIX * (h + 1)] for h in range(DIRECT_HEADS)] + [rows_raw[:], spare_plane[:]]
+        a_scales = a_scales + [a_words[h - 4][:, 0:PIX] for h in range(4, H)]
         u_codes = [keep.tile([P, C], U32, name="u_codes%d" % h, align_bytes=64) for h in range(H)]
         u_scales = [keep.tile([P, C], U8, name="u_scales%d" % h, align_bytes=64) for h in range(H)]
 
         nc.vector.memset(rn_rows[:].bitcast(I32), 0)
-        for tile in zeroed:
-            nc.vector.memset(tile[:].bitcast(I32), 0)
+        nc.vector.memset(direct_planes[:].bitcast(I32), 0)
+        nc.vector.memset(spare_plane[:].bitcast(I32), 0)
         make_identity(nc, ident[:])
 
         text_rows = text.rearrange("(m t) e -> m t e", t=4)
@@ -89,23 +94,32 @@ def tile_prompt_map_edit_s13_kernel(tc, text, wv_bytes, wv_scale, reweight, attn
         def load_text(t):
             nc.sync.dma_start(out=text_sb[t][:], in_=text_rows[:, t, :])
 
-        def spread_scales(h, rs):
-            rows = attn_scales[h].bitcast(I32) if 2 * h in DIRECT else rows_sorted[:].bitcast(I32)[ROWS * h : ROWS * (h + 1), :]
-            for r in rs:
-                nc.sync.dma_start(out=a_scales[h][:].bitcast(I32)[r:P:32, :], in_=rows[r:ROWS:4, :])
+        def load_direct_scales(r):
+            rows = attn_scales[0:DIRECT_HEADS].bitcast(I32).rearrange("h q n -> q h n")
+            nc.sync.dma_start(out=direct_planes[:].bitcast(I32).rearrange("p (h n) -> p h n", h=DIRECT_HEADS)[r:P:32], in_=rows[r:ROWS:4])
+
+        def spread_scales(h, r):
+            rows = rows_sorted[:].bitcast(I32)[ROWS * h : ROWS * (h + 1), :]
+            nc.sync.dma_start(out=a_scales[h].bitcast(I32)[r:P:32, :], in_=rows[r:ROWS:4, :])
 
         def load_words(h):
             nc.sync.dma_start(out=a_words[h][:], in_=attn_words[h])
 
         nc.scalar.dma_start(out=wscale[:, :, 0:4], in_=wv_scale.rearrange("(g p t) o -> p g (t o)", p=P, t=4))
         nc.scalar.dma_start(out=rw[:], in_=reweight.rearrange("(p t) -> p t", t=4))
+        for g in range(G):
+            spread = wscale[:, g, 0:4].unsqueeze(1).to_broadcast([P, C, 4])
+            if g < 2:
+                nc.vector.tensor_copy(out=scale_walk[g][:], in_=spread)
+            else:
+                nc.scalar.copy(out=scale_walk[g][:], in_=spread)
         nc.scalar.copy(out=rw_walk[:], in_=rw[:].unsqueeze(1).unsqueeze(3).to_broadcast([P, C // 2, 4, 2]))
         nc.sync.dma_start(out=rows_raw[:], in_=attn_scales.rearrange("h q n -> (h q) n"))
         nc.sync.dma_start(out=rn_rows[0:STEPS, :], in_=renorm.rearrange("h (k n) -> (h k) n", k=2))
         nc.vector.tensor_copy(out=pick[:], in_=ident[:, 0:STEPS])
         nc.vector.tensor_copy(
-            out=rows_sorted[:].rearrange("p (i s e m) -> p i s m e", s=2, e=2, m=P),
-            in_=rows_raw[:].rearrange("p (i m s e) -> p i s m e", s=2, e=2, m=P),
+            out=rows_sorted[:].rearrange("p (k s e m) -> p k s m e", k=2, e=2, m=P),
+            in_=rows_raw[:].rearrange("p (k m s e) -> p k s m e", k=2, e=2, m=P),
         )
         load_wv(0)
         load_text(0)
@@ -116,7 +130,10 @@ def tile_prompt_map_edit_s13_kernel(tc, text, wv_bytes, wv_scale, reweight, attn
         load_text(3)
         load_wv(3)
         for h in range(H):
-            spread_scales(h // 2, range(2 * (h % 2), 2 * (h % 2) + 2))
+            if h < 4:
+                load_direct_scales(h)
+            else:
+                spread_scales(DIRECT_HEADS, h - 4)
             load_words(h)
 
         text_gr = {}
@@ -149,7 +166,7 @@ def tile_prompt_map_edit_s13_kernel(tc, text, wv_bytes, wv_scale, reweight, attn
             ps = psum_v.tile([P, RUN, STEPS], F32, name="v_bank")
             d = len(DIRECT)
             for j in range(RUN):
-                nc.tensor.matmul(ps[:, j, d:], lhsT=rn_rows[:, BANK * (j // SLOTS) + j % SLOTS : BANK * (j // SLOTS + 1) : SLOTS], rhs=pick[:, d:], start=True, stop=True)
+                nc.tensor.matmul(ps[:, j, d:], lhsT=rn_rows[:, j:HALF:RUN], rhs=pick[:, d:], start=True, stop=True)
             for j in range(RUN):
                 nc.tensor.matmul(ps[:, j, 0:d], lhsT=rn_rows[:, P * j : P * (j + 1)], rhs=pick[:, 0:d], start=True, stop=True)
             return ps
@@ -157,25 +174,32 @@ def tile_prompt_map_edit_s13_kernel(tc, text, wv_bytes, wv_scale, reweight, attn
         def text_quant(t):
             nc.vector.quantize_mx(out=text_codes[t][:].bitcast(E4X4), scales=text_scales[t][:], in_=text_gr[t][:])
 
-        def planes(heads, gs):
-            half, first = divmod(heads.start, H // 2)
-            g0 = gs.start % 2
-            return wide[half][gs.start // 2][:, g0 : g0 + len(gs), :, C * first : C * (first + len(heads))]
+        def group_tile(u):
+            if u not in grouped:
+                grouped[u] = work.tile([P, 4 * C * u[1] * u[3]], BF16, name="grouped", align_bytes=64, bufs=3)
+            return grouped[u]
 
-        def widen(heads, g, ts, on_scalar):
+        def fuse(u, heads):
+            h0, nh, g, ng = u
+            planes = wv_raw[g][:].bitcast(FP8).rearrange("p (t n) -> p n t", t=4)
+            for h in heads:
+                nc.vector.tensor_tensor(
+                    out=group_tile(u)[:, 4 * C * (h - h0) : 4 * C * (h - h0 + 1)].rearrange("p (n t) -> p n t", t=4),
+                    in0=planes[:, C * h : C * (h + 1), :],
+                    in1=scale_walk[g][:],
+                    op=MULT,
+                )
+
+        def widen(g, ts):
             for t in ts:
-                src = wv_raw[g][:, D * t + C * heads.start : D * t + C * heads.stop].bitcast(FP8)
-                dst = planes(heads, one(g))[:, 0, t, :]
-                if on_scalar:
-                    nc.scalar.activation(out=dst, in_=src, func=COPY, scale=wscale[:, g, t : t + 1])
-                else:
-                    nc.vector.tensor_scalar(out=dst, in0=src, scalar1=wscale[:, g, t : t + 1], scalar2=None, op0=MULT)
+                src = wv_raw[g][:, D * t + D // 2 : D * (t + 1)].bitcast(FP8)
+                nc.scalar.activation(out=wide[:, g, t, :], in_=src, func=COPY, scale=wscale[:, g, t : t + 1])
 
-        def interleave(u):
-            grouped[u] = work.tile([P, 4 * UNIT], BF16, name="grouped", align_bytes=64, bufs=GROUPED)
+        def interleave(h):
+            c0 = C * (h - LOW)
             nc.vector.tensor_copy(
-                out=grouped[u][:].rearrange("p (g c i t) -> p g c t i", g=len(u[1]), i=4, t=4),
-                in_=planes(*u).rearrange("p g t (c i) -> p g c t i", i=4),
+                out=group_tile(high_units[h])[:].rearrange("p (g c i t) -> p g c t i", g=G, i=4, t=4),
+                in_=wide[:, :, :, c0 : c0 + C].rearrange("p g t (c i) -> p g c t i", i=4),
             )
 
         def wv_quant(u):
@@ -214,19 +238,13 @@ def tile_prompt_map_edit_s13_kernel(tc, text, wv_bytes, wv_scale, reweight, attn
 
         def sort_words(n):
             h, k = divmod(n, 2)
-            a_sorted[n] = work.tile([P, 2 * HALF], U8, name="a_sorted", align_bytes=64, bufs=5)
-            src = a_words[h][:, 2 * HALF * k : 2 * HALF * (k + 1)].bitcast(U16)
-            dst = a_sorted[n][:].bitcast(U16)
+            a_sorted[n] = work.tile([P, 2 * HALF], U8, name="a_sorted", align_bytes=64, bufs=6)
+            src = a_words[h][:, 2 * HALF * k : 2 * HALF * (k + 1)].bitcast(U16).rearrange("p (a m s e) -> p a s m e", a=2, s=4, e=2)
+            dst = a_sorted[n][:].bitcast(U16).rearrange("p (s e a m) -> p a s m e", a=2, s=4, e=2)
             if n in SORTED_BY_SCALAR:
-                nc.scalar.copy(
-                    out=dst.rearrange("p (q s m) -> p q m s", q=2, s=SLOTS),
-                    in_=src.rearrange("p (q m s) -> p q m s", q=2, s=SLOTS),
-                )
+                nc.scalar.copy(out=dst, in_=src)
             else:
-                nc.vector.tensor_copy(
-                    out=dst.rearrange("p (q s e m) -> p q s m e", q=2, s=2, e=2),
-                    in_=src.rearrange("p (q m s e) -> p q s m e", q=2, s=2, e=2),
-                )
+                nc.vector.tensor_copy(out=dst, in_=src)
 
         def mix(n, q):
             h, k = divmod(n, 2)
@@ -262,84 +280,87 @@ def tile_prompt_map_edit_s13_kernel(tc, text, wv_bytes, wv_scale, reweight, attn
                 dst = out[h].rearrange("(k j p) c -> p k j c", k=2, j=RUN)[:, k, SLOTS * q0 : SLOTS * q1, :]
                 nc.sync.dma_start(out=dst, in_=y_sb[n][:].rearrange("p q s c -> p (q s) c")[:, SLOTS * q0 : SLOTS * q1, :])
             else:
-                dst = out[h].rearrange("(k q p s) c -> p k q (s c)", k=2, q=2, s=SLOTS)[:, k, q0:q1, :]
-                nc.sync.dma_start(out=dst, in_=y_sb[n][:].rearrange("p q s c -> p q (s c)")[:, q0:q1, :])
-            done, part = divmod(n - 1, 2)
-            if 0 <= done < H - SPREAD_AHEAD:
-                spread_scales(done + SPREAD_AHEAD, range(2 * part, 2 * part + 2))
+                dst = out[h].rearrange("(k p j) c -> p k (j c)", k=2, j=RUN)[:, k, BANK * q0 : BANK * q1]
+                nc.sync.dma_start(out=dst, in_=y_sb[n][:].rearrange("p q s c -> p (q s c)")[:, BANK * q0 : BANK * q1])
+            if h + SPREAD_AHEAD < H:
+                for r in range(2 * k, 2 * k + 2):
+                    spread_scales(h + SPREAD_AHEAD, r)
 
-        low, high = range(0, 4), range(4, 8)
-        first, later = FIRST_UNITS, LATER_UNITS
+        low = range(LOW)
+        first_pair, second_pair = low_units[G - 1], low_units[G]
         rn_ps = turn_renorm()
-        widen(range(0, 2), 0, range(4), False)
-        widen(high, 0, range(4), True)
+        fuse(low_units[0], low)
+        widen(0, range(4))
         nc.scalar.copy(out=rn[:], in_=rn_ps[:].rearrange("p j n -> p n j"))
-        widen(range(2, 4), 0, range(4), False)
-        interleave(first[0])
         text_turn(0, 0)
-        widen(high, 1, one(0), True)
+        widen(1, one(0))
         text_turn(0, 1)
-        widen(high, 1, range(1, 3), True)
-        widen(low, 1, range(4), False)
-        wv_quant(first[0])
-        interleave(first[1])
+        widen(1, range(1, 3))
+        fuse(low_units[1], low)
+        wv_quant(low_units[0])
         text_quant(0)
+        wv_quant(low_units[1])
         text_turn(1, 0)
-        widen(high, 1, one(3), True)
+        widen(1, one(3))
         text_turn(1, 1)
-        widen(high, 2, one(0), True)
-        widen(low, 2, range(4), False)
-        wv_quant(first[1])
-        interleave(first[2])
+        widen(2, one(0))
+        fuse(low_units[2], low)
         text_quant(1)
-        wv_quant(first[2])
         for t in range(2, 4):
             text_turn(t, 0)
             text_turn(t, 1)
         for h in range(2):
-            values(h, range(3), range(2))
-        widen(high, 2, range(1, 4), True)
-        widen(high, 3, range(4), True)
-        widen(range(0, 2), 3, range(4), False)
-        text_quant(2)
-        interleave(first[3])
-        text_quant(3)
-        wv_quant(first[3])
-        for t in range(2, 4):
-            for h in range(2):
-                values(h, range(3), one(t))
+            values(h, range(2), range(2))
+        widen(2, range(1, 4))
+        widen(3, range(4))
+        fuse(first_pair, range(2))
+        wv_quant(low_units[2])
         for h in range(2):
-            values(h, one(3), range(4))
-        interleave(later[0])
+            values(h, one(2), range(2))
+        text_quant(2)
+        for h in range(2):
+            values(h, range(3), one(2))
+        wv_quant(first_pair)
+        for h in range(2):
+            values(h, one(3), range(3))
+        text_quant(3)
+        for h in range(2):
+            values(h, range(4), one(3))
+        values(2, range(3), range(4))
+        fuse(second_pair, one(2))
         u_evict(0)
-        wv_quant(later[0])
+        fuse(second_pair, one(3))
         u_quant(0)
+        sort_words(SORTED_BY_SCALAR[0])
 
+        to_sort = [n for n in range(STEPS) if n not in DIRECT and n not in SORTED_BY_SCALAR]
         for n in range(STEPS):
-            unit = later[n] if 1 <= n < len(later) else None
             ready = n // 2 + 1 if n % 2 == 0 and n // 2 + 1 < H else None
             for q in range(2):
                 mix(n, q)
-            if 1 <= n <= len(later):
-                heads, gs = later[n - 1]
-                values(heads.start, gs, range(4))
-            if n == 0:
-                widen(range(2, 4), 3, range(4), False)
-            if unit:
-                interleave(unit)
-            if n + 2 < STEPS and n + 2 not in SORTED_BY_SCALAR:
-                sort_words(n + 2)
+            if 2 <= n < 2 * H - 4:
+                values(n // 2 + 2, range(2 * (n % 2), 2 * (n % 2) + 2), range(4))
             if ready:
                 u_evict(ready)
-            if unit:
-                wv_quant(unit)
-            if ready:
+                if n == 0:
+                    wv_quant(second_pair)
+                    values(2, one(3), range(4))
+                elif ready + 2 < H:
+                    wv_quant(high_units[ready + 2])
+                else:
+                    sort_words(to_sort.pop(0))
                 u_quant(ready)
+                if ready + 3 < H:
+                    interleave(ready + 3)
+                elif ready + 2 < H:
+                    sort_words(to_sort.pop(0))
+            elif to_sort:
+                sort_words(to_sort.pop(0))
             last = n == STEPS - 1
             y_evict(n, 0, True)
             if last:
                 store(n, 0, 1)
             y_evict(n, 1, n < VECTOR_EVICTS_FROM)
             store(n, 1 if last else 0, 2)
-            if n + 3 < STEPS and n + 3 in SORTED_BY_SCALAR:
-                sort_words(n + 3)
+            if n == 1:
+                sort_words(SORTED_BY_SCALAR[1])

@@ -32,8 +32,9 @@ LOW = H // 2
 
 DIRECT_HEADS = 2
 DIRECT = range(2 * DIRECT_HEADS)
+SORTED = range(2 * DIRECT_HEADS, STEPS)
 SORTED_BY_SCALAR = range(2 * DIRECT_HEADS, 2 * DIRECT_HEADS + 2)
-VECTOR_EVICTS_FROM = 13
+VECTOR_EVICTS_FROM = 12
 SPREAD_AHEAD = 3
 
 
@@ -118,8 +119,8 @@ def tile_prompt_map_edit_s13_kernel(tc, text, wv_bytes, wv_scale, reweight, attn
         nc.sync.dma_start(out=rn_rows[0:STEPS, :], in_=renorm.rearrange("h (k n) -> (h k) n", k=2))
         nc.vector.tensor_copy(out=pick[:], in_=ident[:, 0:STEPS])
         nc.vector.tensor_copy(
-            out=rows_sorted[:].rearrange("p (k s e m) -> p k s m e", k=2, e=2, m=P),
-            in_=rows_raw[:].rearrange("p (k m s e) -> p k s m e", k=2, e=2, m=P),
+            out=rows_sorted[:].rearrange("p (k s e m) -> p k s m e", k=2, e=4, m=P),
+            in_=rows_raw[:].rearrange("p (k m s e) -> p k s m e", k=2, e=4, m=P),
         )
         load_wv(0)
         load_text(0)
@@ -162,14 +163,16 @@ def tile_prompt_map_edit_s13_kernel(tc, text, wv_bytes, wv_scale, reweight, attn
                 in_=bank[:].rearrange("p (g u) m -> p g m u", u=2),
             )
 
-        def turn_renorm():
-            ps = psum_v.tile([P, RUN, STEPS], F32, name="v_bank")
-            d = len(DIRECT)
-            for j in range(RUN):
-                nc.tensor.matmul(ps[:, j, d:], lhsT=rn_rows[:, j:HALF:RUN], rhs=pick[:, d:], start=True, stop=True)
-            for j in range(RUN):
-                nc.tensor.matmul(ps[:, j, 0:d], lhsT=rn_rows[:, P * j : P * (j + 1)], rhs=pick[:, 0:d], start=True, stop=True)
-            return ps
+        def turn_renorm(steps, slots, ps):
+            for j in slots:
+                pixels = rn_rows[:, P * j : P * (j + 1)] if steps == DIRECT else rn_rows[:, j:HALF:RUN]
+                nc.tensor.matmul(ps[:, j, steps.start : steps.stop], lhsT=pixels, rhs=pick[:, steps.start : steps.stop], start=True, stop=True)
+
+        def copy_renorm(steps, slots, ps):
+            nc.scalar.copy(
+                out=rn[:, steps.start : steps.stop, slots.start : slots.stop],
+                in_=ps[:, slots.start : slots.stop, steps.start : steps.stop].rearrange("p j n -> p n j"),
+            )
 
         def text_quant(t):
             nc.vector.quantize_mx(out=text_codes[t][:].bitcast(E4X4), scales=text_scales[t][:], in_=text_gr[t][:])
@@ -239,8 +242,8 @@ def tile_prompt_map_edit_s13_kernel(tc, text, wv_bytes, wv_scale, reweight, attn
         def sort_words(n):
             h, k = divmod(n, 2)
             a_sorted[n] = work.tile([P, 2 * HALF], U8, name="a_sorted", align_bytes=64, bufs=6)
-            src = a_words[h][:, 2 * HALF * k : 2 * HALF * (k + 1)].bitcast(U16).rearrange("p (a m s e) -> p a s m e", a=2, s=4, e=2)
-            dst = a_sorted[n][:].bitcast(U16).rearrange("p (s e a m) -> p a s m e", a=2, s=4, e=2)
+            src = a_words[h][:, 2 * HALF * k : 2 * HALF * (k + 1)].bitcast(U16).rearrange("p (a m s e) -> p a s m e", a=2, s=2, e=4)
+            dst = a_sorted[n][:].bitcast(U16).rearrange("p (s e a m) -> p a s m e", a=2, s=2, e=4)
             if n in SORTED_BY_SCALAR:
                 nc.scalar.copy(out=dst, in_=src)
             else:
@@ -288,10 +291,13 @@ def tile_prompt_map_edit_s13_kernel(tc, text, wv_bytes, wv_scale, reweight, attn
 
         low = range(LOW)
         first_pair, second_pair = low_units[G - 1], low_units[G]
-        rn_ps = turn_renorm()
+        rn_ps = psum_v.tile([P, RUN, STEPS], F32, name="v_bank")
+        turn_renorm(DIRECT, range(RUN), rn_ps)
+        turn_renorm(SORTED, range(SLOTS), rn_ps)
         fuse(low_units[0], low)
         widen(0, range(4))
-        nc.scalar.copy(out=rn[:], in_=rn_ps[:].rearrange("p j n -> p n j"))
+        copy_renorm(range(STEPS), range(SLOTS), rn_ps)
+        copy_renorm(DIRECT, range(SLOTS, RUN), rn_ps)
         text_turn(0, 0)
         widen(1, one(0))
         text_turn(0, 1)
@@ -306,12 +312,15 @@ def tile_prompt_map_edit_s13_kernel(tc, text, wv_bytes, wv_scale, reweight, attn
         widen(2, one(0))
         fuse(low_units[2], low)
         text_quant(1)
-        for t in range(2, 4):
-            text_turn(t, 0)
-            text_turn(t, 1)
+        text_turn(2, 0)
+        widen(2, one(1))
+        text_turn(2, 1)
+        widen(2, one(2))
+        text_turn(3, 0)
+        widen(2, one(3))
+        text_turn(3, 1)
         for h in range(2):
             values(h, range(2), range(2))
-        widen(2, range(1, 4))
         widen(3, range(4))
         fuse(first_pair, range(2))
         wv_quant(low_units[2])
@@ -340,6 +349,9 @@ def tile_prompt_map_edit_s13_kernel(tc, text, wv_bytes, wv_scale, reweight, attn
                 mix(n, q)
             if 2 <= n < 2 * H - 4:
                 values(n // 2 + 2, range(2 * (n % 2), 2 * (n % 2) + 2), range(4))
+            if n == 1:
+                rn_ps = psum_v.tile([P, RUN, STEPS], F32, name="v_bank")
+                turn_renorm(SORTED, range(SLOTS, RUN), rn_ps)
             if ready:
                 u_evict(ready)
                 if n == 0:
@@ -352,7 +364,7 @@ def tile_prompt_map_edit_s13_kernel(tc, text, wv_bytes, wv_scale, reweight, attn
                 u_quant(ready)
                 if ready + 3 < H:
                     interleave(ready + 3)
-                elif ready + 2 < H:
+                elif to_sort:
                     sort_words(to_sort.pop(0))
             elif to_sort:
                 sort_words(to_sort.pop(0))
@@ -363,4 +375,5 @@ def tile_prompt_map_edit_s13_kernel(tc, text, wv_bytes, wv_scale, reweight, attn
             y_evict(n, 1, n < VECTOR_EVICTS_FROM)
             store(n, 1 if last else 0, 2)
             if n == 1:
+                copy_renorm(SORTED, range(SLOTS, RUN), rn_ps)
                 sort_words(SORTED_BY_SCALAR[1])

@@ -33,9 +33,10 @@ LOW = H // 2
 DIRECT_HEADS = 2
 DIRECT = range(2 * DIRECT_HEADS)
 SORTED = range(2 * DIRECT_HEADS, STEPS)
-SORTED_BY_SCALAR = range(2 * DIRECT_HEADS, 2 * DIRECT_HEADS + 2)
-VECTOR_EVICTS_FROM = 12
+SORTED_BY_SCALAR = {7: 3, 10: 7}
+VECTOR_EVICTS = (13, 14, 15)
 SPREAD_AHEAD = 3
+VECTOR_SORTS = (2, 1, 0, 0, 0, 1, 0, 1, 0, 1, 2, 1, 1, 0, 0, 0)
 
 
 def tile_prompt_map_edit_s13_kernel(tc, text, wv_bytes, wv_scale, reweight, attn_words, attn_scales, renorm, out):
@@ -50,16 +51,15 @@ def tile_prompt_map_edit_s13_kernel(tc, text, wv_bytes, wv_scale, reweight, attn
         wscale = keep.tile([P, G, 8], F32, name="wscale")
         scale_walk = [keep.tile([P, C, 4], F32, name="scale_walk%d" % g) for g in range(G)]
         rw = keep.tile([P, 4], BF16, name="rw")
-        rw_walk = keep.tile([P, C // 2, 4, 2], F32, name="rw_walk")
         rn_rows = keep.tile([P, HALF], BF16, name="rn_rows")
         rn = keep.tile([P, STEPS, RUN], F32, name="rn")
         ident = keep.tile([P, P], F32, name="ident")
-        pick = keep.tile([P, STEPS], BF16, name="pick")
+        pick = keep.tile([P, len(DIRECT)], BF16, name="pick")
         wv_raw = [keep.tile([P, 4 * D], U8, name="wv_raw%d" % g) for g in range(G)]
         text_sb = [keep.tile([P, E], BF16, name="text_sb%d" % t) for t in range(4)]
         text_codes = [keep.tile([P, E // 4], U32, name="text_codes%d" % t, align_bytes=64) for t in range(4)]
         text_scales = [keep.tile([P, E // 4], U8, name="text_scales%d" % t, align_bytes=64) for t in range(4)]
-        low_units = [(0, LOW, g, 1) for g in range(G - 1)] + [(0, 2, G - 1, 1), (2, 2, G - 1, 1)]
+        low_units = [(0, LOW, 0, 1), (0, 2, 1, 1), (0, 2, 2, 1), (0, 2, 3, 1), (2, 2, 1, 1), (2, 2, 2, 2)]
         high_units = {h: (h, 1, 0, G) for h in range(LOW, H)}
         wv_codes = {}
         wv_scales = {}
@@ -71,7 +71,7 @@ def tile_prompt_map_edit_s13_kernel(tc, text, wv_bytes, wv_scale, reweight, attn
             for g in range(ng):
                 for h in range(nh):
                     wv_at[(h0 + h, g0 + g)] = (u, C * (nh * g + h))
-        wide = keep.tile([P, G, 4, D // 2], BF16, name="wide")
+        wide = keep.tile([P, G, 4, D - 2 * C], BF16, name="wide")
         a_words = [keep.tile([P, 2 * PIX], U8, name="a_words%d" % h, align_bytes=64) for h in range(H)]
         rows_raw = keep.tile([P, PIX], U8, name="rows_raw", align_bytes=64)
         rows_sorted = keep.tile([P, PIX], U8, name="rows_sorted")
@@ -114,15 +114,9 @@ def tile_prompt_map_edit_s13_kernel(tc, text, wv_bytes, wv_scale, reweight, attn
                 nc.vector.tensor_copy(out=scale_walk[g][:], in_=spread)
             else:
                 nc.scalar.copy(out=scale_walk[g][:], in_=spread)
-        nc.scalar.copy(out=rw_walk[:], in_=rw[:].unsqueeze(1).unsqueeze(3).to_broadcast([P, C // 2, 4, 2]))
-        nc.sync.dma_start(out=rows_raw[:], in_=attn_scales.rearrange("h q n -> (h q) n"))
-        nc.sync.dma_start(out=rn_rows[0:STEPS, :], in_=renorm.rearrange("h (k n) -> (h k) n", k=2))
-        nc.vector.tensor_copy(out=pick[:], in_=ident[:, 0:STEPS])
-        nc.vector.tensor_copy(
-            out=rows_sorted[:].rearrange("p (k s e m) -> p k s m e", k=2, e=4, m=P),
-            in_=rows_raw[:].rearrange("p (k m s e) -> p k s m e", k=2, e=4, m=P),
-        )
         load_wv(0)
+        nc.sync.dma_start(out=rn_rows[0:STEPS, :], in_=renorm.rearrange("h (k n) -> (h k) n", k=2))
+        nc.vector.tensor_copy(out=pick[:], in_=ident[:, 0 : len(DIRECT)])
         load_text(0)
         load_wv(1)
         load_text(1)
@@ -130,11 +124,10 @@ def tile_prompt_map_edit_s13_kernel(tc, text, wv_bytes, wv_scale, reweight, attn
         load_text(2)
         load_text(3)
         load_wv(3)
+        nc.sync.dma_start(out=rows_raw[:], in_=attn_scales.rearrange("h q n -> (h q) n"))
         for h in range(H):
             if h < 4:
                 load_direct_scales(h)
-            else:
-                spread_scales(DIRECT_HEADS, h - 4)
             load_words(h)
 
         text_gr = {}
@@ -163,46 +156,49 @@ def tile_prompt_map_edit_s13_kernel(tc, text, wv_bytes, wv_scale, reweight, attn
                 in_=bank[:].rearrange("p (g u) m -> p g m u", u=2),
             )
 
-        def turn_renorm(steps, slots, ps):
-            for j in slots:
-                pixels = rn_rows[:, P * j : P * (j + 1)] if steps == DIRECT else rn_rows[:, j:HALF:RUN]
-                nc.tensor.matmul(ps[:, j, steps.start : steps.stop], lhsT=pixels, rhs=pick[:, steps.start : steps.stop], start=True, stop=True)
+        def turn_direct_renorm():
+            ps = psum_v.tile([P, RUN, len(DIRECT)], F32, name="v_bank")
+            for j in range(RUN):
+                nc.tensor.matmul(ps[:, j, :], lhsT=rn_rows[:, P * j : P * (j + 1)], rhs=pick[:], start=True, stop=True)
+            return ps
 
-        def copy_renorm(steps, slots, ps):
-            nc.scalar.copy(
-                out=rn[:, steps.start : steps.stop, slots.start : slots.stop],
-                in_=ps[:, slots.start : slots.stop, steps.start : steps.stop].rearrange("p j n -> p n j"),
-            )
+        def turn_sorted_renorm():
+            ps = psum_v.tile([P, RUN // 2, P], F32, name="v_bank")
+            words = rn_rows[:].bitcast(F32)
+            for i in range(RUN // 2):
+                nc.tensor.transpose(ps[:, i, :], words[:, i : HALF // 2 : RUN // 2], ident[:])
+            return ps
 
         def text_quant(t):
             nc.vector.quantize_mx(out=text_codes[t][:].bitcast(E4X4), scales=text_scales[t][:], in_=text_gr[t][:])
 
         def group_tile(u):
             if u not in grouped:
-                grouped[u] = work.tile([P, 4 * C * u[1] * u[3]], BF16, name="grouped", align_bytes=64, bufs=3)
+                grouped[u] = work.tile([P, 4 * C * u[1] * u[3]], BF16, name="grouped", align_bytes=64, bufs=4)
             return grouped[u]
 
-        def fuse(u, heads):
-            h0, nh, g, ng = u
+        def fuse(g, heads):
             planes = wv_raw[g][:].bitcast(FP8).rearrange("p (t n) -> p n t", t=4)
             for h in heads:
+                u, c0 = wv_at[(h, g)]
                 nc.vector.tensor_tensor(
-                    out=group_tile(u)[:, 4 * C * (h - h0) : 4 * C * (h - h0 + 1)].rearrange("p (n t) -> p n t", t=4),
+                    out=group_tile(u)[:, 4 * c0 : 4 * (c0 + C)].rearrange("p (n t) -> p n t", t=4),
                     in0=planes[:, C * h : C * (h + 1), :],
                     in1=scale_walk[g][:],
                     op=MULT,
                 )
 
         def widen(g, ts):
+            first = LOW if g < 2 else 2
             for t in ts:
-                src = wv_raw[g][:, D * t + D // 2 : D * (t + 1)].bitcast(FP8)
-                nc.scalar.activation(out=wide[:, g, t, :], in_=src, func=COPY, scale=wscale[:, g, t : t + 1])
+                src = wv_raw[g][:, D * t + C * first : D * (t + 1)].bitcast(FP8)
+                nc.scalar.activation(out=wide[:, g, t, C * (first - 2) :], in_=src, func=COPY, scale=wscale[:, g, t : t + 1])
 
-        def interleave(h):
-            c0 = C * (h - LOW)
+        def interleave(u):
+            h0, nh, g0, ng = u
             nc.vector.tensor_copy(
-                out=group_tile(high_units[h])[:].rearrange("p (g c i t) -> p g c t i", g=G, i=4, t=4),
-                in_=wide[:, :, :, c0 : c0 + C].rearrange("p g t (c i) -> p g c t i", i=4),
+                out=group_tile(u)[:].rearrange("p (g c i t) -> p g c t i", g=ng, i=4, t=4),
+                in_=wide[:, g0 : g0 + ng, :, C * (h0 - 2) : C * (h0 - 2 + nh)].rearrange("p g t (c i) -> p g c t i", i=4),
             )
 
         def wv_quant(u):
@@ -232,7 +228,7 @@ def tile_prompt_map_edit_s13_kernel(tc, text, wv_bytes, wv_scale, reweight, attn
             nc.vector.tensor_tensor(
                 out=ug[:].rearrange("p (c i t) -> p c t i", i=2, t=4),
                 in0=v_ps[h][:].rearrange("p t (c i) -> p c t i", i=2),
-                in1=rw_walk[:],
+                in1=rw[:].unsqueeze(1).unsqueeze(3).to_broadcast([P, C // 2, 4, 2]),
                 op=MULT,
             )
 
@@ -241,13 +237,19 @@ def tile_prompt_map_edit_s13_kernel(tc, text, wv_bytes, wv_scale, reweight, attn
 
         def sort_words(n):
             h, k = divmod(n, 2)
-            a_sorted[n] = work.tile([P, 2 * HALF], U8, name="a_sorted", align_bytes=64, bufs=6)
+            a_sorted[n] = work.tile([P, 2 * HALF], U8, name="a_sorted", align_bytes=64, bufs=7)
             src = a_words[h][:, 2 * HALF * k : 2 * HALF * (k + 1)].bitcast(U16).rearrange("p (a m s e) -> p a s m e", a=2, s=2, e=4)
             dst = a_sorted[n][:].bitcast(U16).rearrange("p (s e a m) -> p a s m e", a=2, s=2, e=4)
             if n in SORTED_BY_SCALAR:
                 nc.scalar.copy(out=dst, in_=src)
             else:
                 nc.vector.tensor_copy(out=dst, in_=src)
+
+        def sort_scales(k):
+            nc.vector.tensor_copy(
+                out=rows_sorted[:, HALF * k : HALF * (k + 1)].rearrange("p (s e m) -> p s m e", e=4, m=P),
+                in_=rows_raw[:, HALF * k : HALF * (k + 1)].rearrange("p (m s e) -> p s m e", e=4, m=P),
+            )
 
         def mix(n, q):
             h, k = divmod(n, 2)
@@ -279,30 +281,26 @@ def tile_prompt_map_edit_s13_kernel(tc, text, wv_bytes, wv_scale, reweight, attn
 
         def store(n, q0, q1):
             h, k = divmod(n, 2)
+            if h + SPREAD_AHEAD < H:
+                for r in range(2 * k, 2 * k + 2):
+                    spread_scales(h + SPREAD_AHEAD, r)
             if n in DIRECT:
                 dst = out[h].rearrange("(k j p) c -> p k j c", k=2, j=RUN)[:, k, SLOTS * q0 : SLOTS * q1, :]
                 nc.sync.dma_start(out=dst, in_=y_sb[n][:].rearrange("p q s c -> p (q s) c")[:, SLOTS * q0 : SLOTS * q1, :])
             else:
                 dst = out[h].rearrange("(k p j) c -> p k (j c)", k=2, j=RUN)[:, k, BANK * q0 : BANK * q1]
                 nc.sync.dma_start(out=dst, in_=y_sb[n][:].rearrange("p q s c -> p (q s c)")[:, BANK * q0 : BANK * q1])
-            if h + SPREAD_AHEAD < H:
-                for r in range(2 * k, 2 * k + 2):
-                    spread_scales(h + SPREAD_AHEAD, r)
 
-        low = range(LOW)
-        first_pair, second_pair = low_units[G - 1], low_units[G]
-        rn_ps = psum_v.tile([P, RUN, STEPS], F32, name="v_bank")
-        turn_renorm(DIRECT, range(RUN), rn_ps)
-        turn_renorm(SORTED, range(SLOTS), rn_ps)
-        fuse(low_units[0], low)
+        pair = range(2)
+        rn_ps = turn_direct_renorm()
+        fuse(0, range(LOW))
         widen(0, range(4))
-        copy_renorm(range(STEPS), range(SLOTS), rn_ps)
-        copy_renorm(DIRECT, range(SLOTS, RUN), rn_ps)
+        nc.scalar.copy(out=rn[:, 0 : len(DIRECT), :], in_=rn_ps[:].rearrange("p j n -> p n j"))
         text_turn(0, 0)
         widen(1, one(0))
         text_turn(0, 1)
         widen(1, range(1, 3))
-        fuse(low_units[1], low)
+        fuse(1, range(3))
         wv_quant(low_units[0])
         text_quant(0)
         wv_quant(low_units[1])
@@ -310,70 +308,82 @@ def tile_prompt_map_edit_s13_kernel(tc, text, wv_bytes, wv_scale, reweight, attn
         widen(1, one(3))
         text_turn(1, 1)
         widen(2, one(0))
-        fuse(low_units[2], low)
+        fuse(2, pair)
+        fuse(1, one(3))
         text_quant(1)
-        text_turn(2, 0)
-        widen(2, one(1))
-        text_turn(2, 1)
-        widen(2, one(2))
-        text_turn(3, 0)
-        widen(2, one(3))
-        text_turn(3, 1)
-        for h in range(2):
-            values(h, range(2), range(2))
-        widen(3, range(4))
-        fuse(first_pair, range(2))
         wv_quant(low_units[2])
-        for h in range(2):
-            values(h, one(2), range(2))
+        for t in range(2, 4):
+            text_turn(t, 0)
+            text_turn(t, 1)
+        for h in pair:
+            values(h, range(3), range(2))
+        widen(2, range(1, 4))
+        widen(3, range(4))
+        fuse(3, pair)
         text_quant(2)
-        for h in range(2):
-            values(h, range(3), one(2))
-        wv_quant(first_pair)
-        for h in range(2):
-            values(h, one(3), range(3))
+        values(0, range(3), one(2))
+        wv_quant(low_units[3])
+        values(0, one(3), range(3))
         text_quant(3)
-        for h in range(2):
-            values(h, range(4), one(3))
-        values(2, range(3), range(4))
-        fuse(second_pair, one(2))
+        values(0, range(4), one(3))
+        values(1, range(3), one(2))
+        values(1, one(3), range(3))
+        values(1, range(4), one(3))
+        wv_quant(low_units[4])
+        values(2, range(2), range(4))
+        sort_scales(0)
         u_evict(0)
-        fuse(second_pair, one(3))
+        sort_scales(1)
+        for r in range(4):
+            spread_scales(DIRECT_HEADS, r)
         u_quant(0)
-        sort_words(SORTED_BY_SCALAR[0])
 
-        to_sort = [n for n in range(STEPS) if n not in DIRECT and n not in SORTED_BY_SCALAR]
-        for n in range(STEPS):
+        to_sort = [n for n in SORTED if n not in SORTED_BY_SCALAR]
+
+        def vector_work(n):
             ready = n // 2 + 1 if n % 2 == 0 and n // 2 + 1 < H else None
-            for q in range(2):
-                mix(n, q)
-            if 2 <= n < 2 * H - 4:
-                values(n // 2 + 2, range(2 * (n % 2), 2 * (n % 2) + 2), range(4))
+            sorts = [to_sort.pop(0) for i in range(VECTOR_SORTS[n])]
             if n == 1:
-                rn_ps = psum_v.tile([P, RUN, STEPS], F32, name="v_bank")
-                turn_renorm(SORTED, range(SLOTS, RUN), rn_ps)
+                interleave(low_units[5])
+                sort_words(sorts.pop(0))
+                wv_quant(low_units[5])
+                interleave(high_units[LOW])
             if ready:
                 u_evict(ready)
-                if n == 0:
-                    wv_quant(second_pair)
-                    values(2, one(3), range(4))
-                elif ready + 2 < H:
+                if n > 0 and ready + 2 < H:
                     wv_quant(high_units[ready + 2])
                 else:
-                    sort_words(to_sort.pop(0))
+                    sort_words(sorts.pop(0))
                 u_quant(ready)
-                if ready + 3 < H:
-                    interleave(ready + 3)
-                elif to_sort:
-                    sort_words(to_sort.pop(0))
-            elif to_sort:
-                sort_words(to_sort.pop(0))
+            for later in sorts:
+                sort_words(later)
+            if ready and n > 0 and ready + 3 < H:
+                interleave(high_units[ready + 3])
+
+        for n in range(STEPS):
+            for q in range(2):
+                mix(n, q)
+            if n == 0:
+                rn_ps = turn_sorted_renorm()
+            if n == 3:
+                values(2, range(2, 4), range(4))
+                values(3, range(4), range(4))
+                vector_work(2)
+            if 4 <= n < 2 * H - 4:
+                values(n // 2 + 2, range(2 * (n % 2), 2 * (n % 2) + 2), range(4))
+            if n != 2:
+                vector_work(n)
             last = n == STEPS - 1
             y_evict(n, 0, True)
             if last:
                 store(n, 0, 1)
-            y_evict(n, 1, n < VECTOR_EVICTS_FROM)
+            y_evict(n, 1, n not in VECTOR_EVICTS)
             store(n, 1 if last else 0, 2)
-            if n == 1:
-                copy_renorm(SORTED, range(SLOTS, RUN), rn_ps)
-                sort_words(SORTED_BY_SCALAR[1])
+            if n == 0:
+                nc.scalar.copy(
+                    out=rn[:, len(DIRECT) :, :].rearrange("p n (i e) -> p n i e", e=2),
+                    in_=rn_ps[:].bitcast(BF16).rearrange("p i (n e) -> p n i e", e=2)[:, len(DIRECT) : STEPS],
+                )
+            for later in SORTED_BY_SCALAR:
+                if SORTED_BY_SCALAR[later] == n:
+                    sort_words(later)

@@ -30,13 +30,13 @@ STEPS = 2 * H
 ROWS = 16
 LOW = H // 2
 
-DIRECT_HEADS = 2
+DIRECT_HEADS = 3
 DIRECT = range(2 * DIRECT_HEADS)
 SORTED = range(2 * DIRECT_HEADS, STEPS)
-SORTED_BY_SCALAR = {7: 3, 10: 7}
+SORTED_BY_SCALAR = {9: 3}
 VECTOR_EVICTS = (13, 14, 15)
 SPREAD_AHEAD = 3
-VECTOR_SORTS = (2, 1, 0, 0, 0, 1, 0, 1, 0, 1, 2, 1, 1, 0, 0, 0)
+VECTOR_SORTS = (2, 1, 0, 0, 0, 0, 0, 1, 0, 1, 2, 1, 1, 0, 0, 0)
 
 
 def tile_prompt_map_edit_s13_kernel(tc, text, wv_bytes, wv_scale, reweight, attn_words, attn_scales, renorm, out):
@@ -76,15 +76,13 @@ def tile_prompt_map_edit_s13_kernel(tc, text, wv_bytes, wv_scale, reweight, attn
         rows_raw = keep.tile([P, PIX], U8, name="rows_raw", align_bytes=64)
         rows_sorted = keep.tile([P, PIX], U8, name="rows_sorted")
         direct_planes = keep.tile([P, DIRECT_HEADS * PIX], U8, name="direct_planes", align_bytes=64)
-        spare_plane = keep.tile([P, PIX], U8, name="spare_plane", align_bytes=64)
-        a_scales = [direct_planes[:, PIX * h : PIX * (h + 1)] for h in range(DIRECT_HEADS)] + [rows_raw[:], spare_plane[:]]
+        a_scales = [direct_planes[:, PIX * h : PIX * (h + 1)] for h in range(DIRECT_HEADS)] + [rows_raw[:]]
         a_scales = a_scales + [a_words[h - 4][:, 0:PIX] for h in range(4, H)]
         u_codes = [keep.tile([P, C], U32, name="u_codes%d" % h, align_bytes=64) for h in range(H)]
         u_scales = [keep.tile([P, C], U8, name="u_scales%d" % h, align_bytes=64) for h in range(H)]
 
         nc.vector.memset(rn_rows[:].bitcast(I32), 0)
         nc.vector.memset(direct_planes[:].bitcast(I32), 0)
-        nc.vector.memset(spare_plane[:].bitcast(I32), 0)
         make_identity(nc, ident[:])
 
         text_rows = text.rearrange("(m t) e -> m t e", t=4)
@@ -334,8 +332,6 @@ def tile_prompt_map_edit_s13_kernel(tc, text, wv_bytes, wv_scale, reweight, attn
         sort_scales(0)
         u_evict(0)
         sort_scales(1)
-        for r in range(4):
-            spread_scales(DIRECT_HEADS, r)
         u_quant(0)
 
         to_sort = [n for n in SORTED if n not in SORTED_BY_SCALAR]

from contextlib import ExitStack

import concourse.mybir as mybir
from concourse.masks import make_identity

FLOPS = 2 * 512 * 2048 * 1024 + 2 * 8 * 2048 * 512 * 128

F32 = mybir.dt.float32
BF16 = mybir.dt.bfloat16
I32 = mybir.dt.int32
U32 = mybir.dt.uint32
U16 = mybir.dt.uint16
U8 = mybir.dt.uint8
FP8 = mybir.dt.float8_e4m3fn
E4X4 = mybir.dt.float8_e4m3fn_x4
F4X4 = mybir.dt.float4_e2m1fn_x4
COPY = mybir.ActivationFunctionType.Copy
MULT = mybir.AluOpType.mult

P = 128
E, H, C, PIX = 2048, 8, 128, 2048
D = H * C
PASS = 4 * P
G = E // PASS
BANK = 512
HALF = PIX // 2
SLOTS = BANK // P
RUN = HALF // P
STEPS = 2 * H
ROWS = 16
LOW = H // 2

DIRECT_HEADS = 3
DIRECT = range(2 * DIRECT_HEADS)
SORTED = range(2 * DIRECT_HEADS, STEPS)
SORTED_BY_SCALAR = {9: 3}
VECTOR_EVICTS = (13, 14, 15)
SPREAD_AHEAD = 3
VECTOR_SORTS = (2, 1, 0, 0, 0, 0, 0, 1, 0, 1, 2, 1, 1, 0, 0, 0)


def tile_prompt_map_edit_s13_kernel(tc, text, wv_bytes, wv_scale, reweight, attn_words, attn_scales, renorm, out):
    nc = tc.nc
    with ExitStack() as ctx:
        keep = ctx.enter_context(tc.tile_pool(name="keep", bufs=1))
        work = ctx.enter_context(tc.tile_pool(name="work", bufs=3))
        psum_v = ctx.enter_context(tc.psum_pool(name="psum_v", bufs=3))
        psum_y = ctx.enter_context(tc.psum_pool(name="psum_y", bufs=5))
        ctx.enter_context(tc.manual_schedule())

        wscale = keep.tile([P, G, 8], F32, name="wscale")
        scale_walk = [keep.tile([P, C, 4], F32, name="scale_walk%d" % g) for g in range(G)]
        rw = keep.tile([P, 4], BF16, name="rw")
        rn_rows = keep.tile([P, HALF], BF16, name="rn_rows")
        rn = keep.tile([P, STEPS, RUN], F32, name="rn")
        ident = keep.tile([P, P], F32, name="ident")
        pick = keep.tile([P, len(DIRECT)], BF16, name="pick")
        wv_raw = [keep.tile([P, 4 * D], U8, name="wv_raw%d" % g) for g in range(G)]
        text_sb = [keep.tile([P, E], BF16, name="text_sb%d" % t) for t in range(4)]
        text_codes = [keep.tile([P, E // 4], U32, name="text_codes%d" % t, align_bytes=64) for t in range(4)]
        text_scales = [keep.tile([P, E // 4], U8, name="text_scales%d" % t, align_bytes=64) for t in range(4)]
        low_units = [(0, LOW, 0, 1), (0, 2, 1, 1), (0, 2, 2, 1), (0, 2, 3, 1), (2, 2, 1, 1), (2, 2, 2, 2)]
        high_units = {h: (h, 1, 0, G) for h in range(LOW, H)}
        wv_codes = {}
        wv_scales = {}
        wv_at = {}
        for u in low_units + list(high_units.values()):
            h0, nh, g0, ng = u
            wv_codes[u] = keep.tile([P, C * nh * ng], U32, name="wv_codes%d%d" % (h0, g0), align_bytes=64)
            wv_scales[u] = keep.tile([P, C * nh * ng], U8, name="wv_scales%d%d" % (h0, g0), align_bytes=64)
            for g in range(ng):
                for h in range(nh):
                    wv_at[(h0 + h, g0 + g)] = (u, C * (nh * g + h))
        wide = keep.tile([P, G, 4, D - 2 * C], BF16, name="wide")
        a_words = [keep.tile([P, 2 * PIX], U8, name="a_words%d" % h, align_bytes=64) for h in range(H)]
        rows_raw = keep.tile([P, PIX], U8, name="rows_raw", align_bytes=64)
        rows_sorted = keep.tile([P, PIX], U8, name="rows_sorted")
        direct_planes = keep.tile([P, DIRECT_HEADS * PIX], U8, name="direct_planes", align_bytes=64)
        a_scales = [direct_planes[:, PIX * h : PIX * (h + 1)] for h in range(DIRECT_HEADS)] + [rows_raw[:]]
        a_scales = a_scales + [a_words[h - 4][:, 0:PIX] for h in range(4, H)]
        u_codes = [keep.tile([P, C], U32, name="u_codes%d" % h, align_bytes=64) for h in range(H)]
        u_scales = [keep.tile([P, C], U8, name="u_scales%d" % h, align_bytes=64) for h in range(H)]

        nc.vector.memset(rn_rows[:].bitcast(I32), 0)
        nc.vector.memset(direct_planes[:].bitcast(I32), 0)
        make_identity(nc, ident[:])

        text_rows = text.rearrange("(m t) e -> m t e", t=4)

        def load_wv(g):
            nc.sync.dma_start(out=wv_raw[g][:], in_=wv_bytes[PASS * g : PASS * (g + 1), :].rearrange("(p t) n -> p (t n)", t=4))

        def load_text(t):
            nc.sync.dma_start(out=text_sb[t][:], in_=text_rows[:, t, :])

        def load_direct_scales(r):
            rows = attn_scales[0:DIRECT_HEADS].bitcast(I32).rearrange("h q n -> q h n")
            nc.sync.dma_start(out=direct_planes[:].bitcast(I32).rearrange("p (h n) -> p h n", h=DIRECT_HEADS)[r:P:32], in_=rows[r:ROWS:4])

        def spread_scales(h, r):
            rows = rows_sorted[:].bitcast(I32)[ROWS * h : ROWS * (h + 1), :]
            nc.sync.dma_start(out=a_scales[h].bitcast(I32)[r:P:32, :], in_=rows[r:ROWS:4, :])

        def load_words(h):
            nc.sync.dma_start(out=a_words[h][:], in_=attn_words[h])

        nc.scalar.dma_start(out=wscale[:, :, 0:4], in_=wv_scale.rearrange("(g p t) o -> p g (t o)", p=P, t=4))
        nc.scalar.dma_start(out=rw[:], in_=reweight.rearrange("(p t) -> p t", t=4))
        for g in range(G):
            spread = wscale[:, g, 0:4].unsqueeze(1).to_broadcast([P, C, 4])
            if g < 2:
                nc.vector.tensor_copy(out=scale_walk[g][:], in_=spread)
            else:
                nc.scalar.copy(out=scale_walk[g][:], in_=spread)
        load_wv(0)
        nc.sync.dma_start(out=rn_rows[0:STEPS, :], in_=renorm.rearrange("h (k n) -> (h k) n", k=2))
        nc.vector.tensor_copy(out=pick[:], in_=ident[:, 0 : len(DIRECT)])
        load_text(0)
        load_wv(1)
        load_text(1)
        load_wv(2)
        load_text(2)
        load_text(3)
        load_wv(3)
        nc.sync.dma_start(out=rows_raw[:], in_=attn_scales.rearrange("h q n -> (h q) n"))
        for h in range(H):
            if h < 4:
                load_direct_scales(h)
            load_words(h)

        text_gr = {}
        grouped = {}
        v_ps = {}
        v_passes = {}
        u_gr = {}
        a_sorted = {}
        y_ps = {}
        y_sb = {}

        def one(i):
            return range(i, i + 1)

        def text_turn(t, gp):
            words = text_sb[t][:].bitcast(F32)
            if gp == 0:
                text_gr[t] = work.tile([P, E], BF16, name="text_gr", align_bytes=64, bufs=4)
            bank = psum_y.tile([P, 4, P], F32, name="y_bank")
            for gg in range(2):
                g = 2 * gp + gg
                for u in range(2):
                    nc.tensor.transpose(bank[:, 2 * gg + u, :], words[:, 2 * P * g + u : 2 * P * (g + 1) : 2], ident[:])
            nc.scalar.copy(
                out=text_gr[t][:, 2 * PASS * gp : 2 * PASS * (gp + 1)].bitcast(F32).rearrange("p (g m u) -> p g m u", g=2, u=2),
                in_=bank[:].rearrange("p (g u) m -> p g m u", u=2),
            )

        def turn_direct_renorm():
            ps = psum_v.tile([P, RUN, len(DIRECT)], F32, name="v_bank")
            for j in range(RUN):
                nc.tensor.matmul(ps[:, j, :], lhsT=rn_rows[:, P * j : P * (j + 1)], rhs=pick[:], start=True, stop=True)
            return ps

        def turn_sorted_renorm():
            ps = psum_v.tile([P, RUN // 2, P], F32, name="v_bank")
            words = rn_rows[:].bitcast(F32)
            for i in range(RUN // 2):
                nc.tensor.transpose(ps[:, i, :], words[:, i : HALF // 2 : RUN // 2], ident[:])
            return ps

        def text_quant(t):
            nc.vector.quantize_mx(out=text_codes[t][:].bitcast(E4X4), scales=text_scales[t][:], in_=text_gr[t][:])

        def group_tile(u):
            if u not in grouped:
                grouped[u] = work.tile([P, 4 * C * u[1] * u[3]], BF16, name="grouped", align_bytes=64, bufs=4)
            return grouped[u]

        def fuse(g, heads):
            planes = wv_raw[g][:].bitcast(FP8).rearrange("p (t n) -> p n t", t=4)
            for h in heads:
                u, c0 = wv_at[(h, g)]
                nc.vector.tensor_tensor(
                    out=group_tile(u)[:, 4 * c0 : 4 * (c0 + C)].rearrange("p (n t) -> p n t", t=4),
                    in0=planes[:, C * h : C * (h + 1), :],
                    in1=scale_walk[g][:],
                    op=MULT,
                )

        def widen(g, ts):
            first = LOW if g < 2 else 2
            for t in ts:
                src = wv_raw[g][:, D * t + C * first : D * (t + 1)].bitcast(FP8)
                nc.scalar.activation(out=wide[:, g, t, C * (first - 2) :], in_=src, func=COPY, scale=wscale[:, g, t : t + 1])

        def interleave(u):
            h0, nh, g0, ng = u
            nc.vector.tensor_copy(
                out=group_tile(u)[:].rearrange("p (g c i t) -> p g c t i", g=ng, i=4, t=4),
                in_=wide[:, g0 : g0 + ng, :, C * (h0 - 2) : C * (h0 - 2 + nh)].rearrange("p g t (c i) -> p g c t i", i=4),
            )

        def wv_quant(u):
            nc.vector.quantize_mx(out=wv_codes[u][:].bitcast(E4X4), scales=wv_scales[u][:], in_=grouped[u][:])

        def values(h, gs, ts):
            if h not in v_ps:
                v_ps[h] = psum_v.tile([P, 4, C], F32, name="v_bank")
                v_passes[h] = 0
            for g in gs:
                u, c0 = wv_at[(h, g)]
                for t in ts:
                    v_passes[h] = v_passes[h] + 1
                    nc.tensor.matmul_mx(
                        out=v_ps[h][:, t, :],
                        lhsT=text_codes[t][:, P * g : P * (g + 1)].bitcast(E4X4),
                        lhsT_scale=text_scales[t][:, P * g : P * (g + 1)],
                        rhs=wv_codes[u][:, c0 : c0 + C].bitcast(E4X4),
                        rhs_scale=wv_scales[u][:, c0 : c0 + C],
                        start=(v_passes[h] == 1),
                        stop=(v_passes[h] == 4 * G),
                    )

        def u_evict(h):
            ug = work.tile([P, 4 * C], BF16, name="u_gr", align_bytes=64, bufs=2)
            u_gr[h] = ug
            nc.vector.tensor_tensor(
                out=ug[:].rearrange("p (c i t) -> p c t i", i=2, t=4),
                in0=v_ps[h][:].rearrange("p t (c i) -> p c t i", i=2),
                in1=rw[:].unsqueeze(1).unsqueeze(3).to_broadcast([P, C // 2, 4, 2]),
                op=MULT,
            )

        def u_quant(h):
            nc.vector.quantize_mx(out=u_codes[h][:].bitcast(E4X4), scales=u_scales[h][:], in_=u_gr[h][:])

        def sort_words(n):
            h, k = divmod(n, 2)
            a_sorted[n] = work.tile([P, 2 * HALF], U8, name="a_sorted", align_bytes=64, bufs=7)
            src = a_words[h][:, 2 * HALF * k : 2 * HALF * (k + 1)].bitcast(U16).rearrange("p (a m s e) -> p a s m e", a=2, s=2, e=4)
            dst = a_sorted[n][:].bitcast(U16).rearrange("p (s e a m) -> p a s m e", a=2, s=2, e=4)
            if n in SORTED_BY_SCALAR:
                nc.scalar.copy(out=dst, in_=src)
            else:
                nc.vector.tensor_copy(out=dst, in_=src)

        def sort_scales(k):
            nc.vector.tensor_copy(
                out=rows_sorted[:, HALF * k : HALF * (k + 1)].rearrange("p (s e m) -> p s m e", e=4, m=P),
                in_=rows_raw[:, HALF * k : HALF * (k + 1)].rearrange("p (m s e) -> p s m e", e=4, m=P),
            )

        def mix(n, q):
            h, k = divmod(n, 2)
            ps = psum_y.tile([P, SLOTS, C], F32, name="y_bank")
            y_ps[(n, q)] = ps
            words = a_words[h][:, 2 * HALF * k : 2 * HALF * (k + 1)] if n in DIRECT else a_sorted[n][:]
            for s in range(SLOTS):
                i0 = BANK * q + P * s
                nc.tensor.matmul_mx(
                    out=ps[:, s, :],
                    lhsT=words[:, 2 * i0 : 2 * (i0 + P)].bitcast(F4X4),
                    lhsT_scale=a_scales[h][:, HALF * k + i0 : HALF * k + i0 + P],
                    rhs=u_codes[h][:].bitcast(E4X4),
                    rhs_scale=u_scales[h][:],
                    start=True,
                    stop=True,
                )

        def y_evict(n, q, on_scalar):
            if n not in y_sb:
                y_sb[n] = work.tile([P, 2, SLOTS, C], F32, name="y_sb", bufs=10)
            ps = y_ps[(n, q)]
            fac = rn[:, n, SLOTS * q : SLOTS * (q + 1)]
            if on_scalar:
                for s in range(SLOTS):
                    nc.scalar.activation(out=y_sb[n][:, q, s, :], in_=ps[:, s, :], func=COPY, scale=fac[:, s : s + 1])
            else:
                nc.vector.tensor_tensor(out=y_sb[n][:, q], in0=ps[:], in1=fac.unsqueeze(2).to_broadcast([P, SLOTS, C]), op=MULT)

        def store(n, q0, q1):
            h, k = divmod(n, 2)
            if h + SPREAD_AHEAD < H:
                for r in range(2 * k, 2 * k + 2):
                    spread_scales(h + SPREAD_AHEAD, r)
            if n in DIRECT:
                dst = out[h].rearrange("(k j p) c -> p k j c", k=2, j=RUN)[:, k, SLOTS * q0 : SLOTS * q1, :]
                nc.sync.dma_start(out=dst, in_=y_sb[n][:].rearrange("p q s c -> p (q s) c")[:, SLOTS * q0 : SLOTS * q1, :])
            else:
                dst = out[h].rearrange("(k p j) c -> p k (j c)", k=2, j=RUN)[:, k, BANK * q0 : BANK * q1]
                nc.sync.dma_start(out=dst, in_=y_sb[n][:].rearrange("p q s c -> p (q s c)")[:, BANK * q0 : BANK * q1])

        pair = range(2)
        rn_ps = turn_direct_renorm()
        fuse(0, range(LOW))
        widen(0, range(4))
        nc.scalar.copy(out=rn[:, 0 : len(DIRECT), :], in_=rn_ps[:].rearrange("p j n -> p n j"))
        text_turn(0, 0)
        widen(1, one(0))
        text_turn(0, 1)
        widen(1, range(1, 3))
        fuse(1, range(3))
        wv_quant(low_units[0])
        text_quant(0)
        wv_quant(low_units[1])
        text_turn(1, 0)
        widen(1, one(3))
        text_turn(1, 1)
        widen(2, one(0))
        fuse(2, pair)
        fuse(1, one(3))
        text_quant(1)
        wv_quant(low_units[2])
        for t in range(2, 4):
            text_turn(t, 0)
            text_turn(t, 1)
        for h in pair:
            values(h, range(3), range(2))
        widen(2, range(1, 4))
        widen(3, range(4))
        fuse(3, pair)
        text_quant(2)
        values(0, range(3), one(2))
        wv_quant(low_units[3])
        values(0, one(3), range(3))
        text_quant(3)
        values(0, range(4), one(3))
        values(1, range(3), one(2))
        values(1, one(3), range(3))
        values(1, range(4), one(3))
        wv_quant(low_units[4])
        values(2, range(2), range(4))
        sort_scales(0)
        u_evict(0)
        sort_scales(1)
        u_quant(0)

        to_sort = [n for n in SORTED if n not in SORTED_BY_SCALAR]

        def vector_work(n):
            ready = n // 2 + 1 if n % 2 == 0 and n // 2 + 1 < H else None
            sorts = [to_sort.pop(0) for i in range(VECTOR_SORTS[n])]
            if n == 1:
                interleave(low_units[5])
                sort_words(sorts.pop(0))
                wv_quant(low_units[5])
                interleave(high_units[LOW])
            if ready:
                u_evict(ready)
                if n > 0 and ready + 2 < H:
                    wv_quant(high_units[ready + 2])
                else:
                    sort_words(sorts.pop(0))
                u_quant(ready)
            for later in sorts:
                sort_words(later)
            if ready and n > 0 and ready + 3 < H:
                interleave(high_units[ready + 3])

        for n in range(STEPS):
            for q in range(2):
                mix(n, q)
            if n == 0:
                rn_ps = turn_sorted_renorm()
            if n == 3:
                values(2, range(2, 4), range(4))
                values(3, range(4), range(4))
                vector_work(2)
            if 4 <= n < 2 * H - 4:
                values(n // 2 + 2, range(2 * (n % 2), 2 * (n % 2) + 2), range(4))
            if n != 2:
                vector_work(n)
            last = n == STEPS - 1
            y_evict(n, 0, True)
            if last:
                store(n, 0, 1)
            y_evict(n, 1, n not in VECTOR_EVICTS)
            store(n, 1 if last else 0, 2)
            if n == 0:
                nc.scalar.copy(
                    out=rn[:, len(DIRECT) :, :].rearrange("p n (i e) -> p n i e", e=2),
                    in_=rn_ps[:].bitcast(BF16).rearrange("p i (n e) -> p n i e", e=2)[:, len(DIRECT) : STEPS],
                )
            for later in SORTED_BY_SCALAR:
                if SORTED_BY_SCALAR[later] == n:
                    sort_words(later)
